import numpy as np, ml_dtypes
CORES = [23,119,17,113]
N = 4
BF = ml_dtypes.bfloat16
def gentries(a):
    return np.ascontiguousarray(a.reshape(8, 16, -1).transpose(0, 2, 1)).reshape(8, -1)
def gtable(e):
    e = np.asarray(e); return np.ascontiguousarray(e.reshape(8, -1, 16).transpose(0, 2, 1)).reshape(128, -1).astype(np.int32)
P, M, B, R, VI, HO, NEED = 4096, 4096, 256, 16, 3, 1, 12
F, C, TM = B // 2, M // (B // 2), R // 2
HALF = (16 - NEED) // 2
def stock(rng):
    mem = np.stack([rng.permutation(M) for g in range(8)]); fo = np.zeros((8, M), np.int64)
    np.put_along_axis(fo, mem, np.tile(np.repeat(np.arange(F), C), (8, 1)), 1)
    ml = rng.choice(np.array([1, 1, 2, 2, 3, 3, 4, 5, 6, TM]), (8, F))
    st = rng.integers(1, F, (8, F, TM)); st[:, :, 0] = np.arange(F)
    return mem.reshape(8, F, C), fo, ml, np.add.accumulate(st, axis=2) % F
def runs(rng, st, fam, same):
    mem, fo, ml, mot = st; sh = fam.shape + (R,); gi = np.arange(8)[:, None]; gj = np.arange(8)[:, None, None]; s = np.arange(R)
    n = ml[gi, fam]; ln = np.minimum(n + rng.integers(0, n + 2), R)
    key = rng.random(sh); key[..., 0] = -1.0; key = np.where(s < ln[..., None], key, 2.0)
    k = np.add.accumulate((np.argsort(np.argsort(key, axis=-1), axis=-1) < n[..., None]).astype(np.int64), axis=-1) - 1
    k = np.minimum(k, TM - 1); fs = mot[gi, fam]; nm = mem[gj, fs, rng.integers(0, C, fs.shape)]
    t = np.take_along_axis(nm, k, -1); alike = mem[gj, np.take_along_axis(fs, k, -1), rng.integers(0, C, sh)]
    hit = (s == ln[..., None] - 1) | (rng.random(sh) < 0.06)
    return ln, np.where(hit, np.where(rng.random(sh) < same, t, alike), rng.integers(0, M, sh)), t
def voices(rng, st, base, alts, mode):
    x = base[:, np.arange(8)[:, None], st[1]]; pool = np.argsort(rng.random((256, 16)), axis=-1)
    m = pool[rng.integers(0, 256, (N, 8, M))] < rng.choice(np.array(alts), (N, 8, M))[..., None]
    if mode == "flip": y = -x
    elif mode == "near": y = np.where(x == 15, 14, x + 1)
    else: y = (x + 15 + rng.integers(1, 31, x.shape)) % 31 - 15
    return np.where(m, y, x)
def parts(rng, same=0.3, lo=F, mode="any", alts=(0, 1, HALF, HALF, HALF + 1), base=None, skew=1):
    st = stock(rng); fo = st[1]; gi = np.arange(8)[:, None]; s = np.arange(R)
    if base is None: base = rng.integers(-15, 16, (N, 8, F, 16))
    d = {"fo": fo, "x": voices(rng, st, base, alts, mode)}
    cf = np.argsort(rng.random((N, 8, B)), axis=-1) // 2; own = np.argsort(cf, axis=-1, kind="stable").reshape(N, 8, F, 2)
    ln, u, t = runs(rng, st, cf, same); d["cf"] = cf
    d["bl"] = np.where(rng.random(ln.shape) < 0.15, np.maximum(ln - 1, 1), ln); d["bu"] = u; d["bt"] = t
    bk = own[np.arange(N)[:, None, None], gi, fo[None], rng.integers(0, 2, (N, 8, M))]; v = rng.random(bk.shape)
    d["bk"] = np.where(v < 0.1, -1, np.where(v < 0.16, rng.integers(0, B, bk.shape), bk))
    ln, u, t = runs(rng, st, (lo * rng.random((N, 8, P // 2)) ** skew).astype(np.int64), same); m = s < ln[..., None]
    d["pu"] = np.stack([np.stack([np.resize(u[q, g][m[q, g]], P) for g in range(8)]) for q in range(N)])
    d["pt"] = np.stack([np.stack([np.resize(t[q, g][m[q, g]], P) for g in range(8)]) for q in range(N)])
    d["pn"] = np.where(rng.random((N, 8)) < 0.3, P, rng.integers(3 * P // 4, P + 1, (N, 8)))
    d["th"] = rng.integers(550, 850, (N, 8))
    return d
def pack(d):
    i = lambda a, *sh: np.ascontiguousarray(np.reshape(a, (N, 8) + sh)).astype(np.int32)
    return {"tones": np.ascontiguousarray(d["x"].transpose(0, 1, 3, 2)).reshape(N, 128, M).astype(np.float32).astype(BF),
            "pu": np.stack([gtable(a) for a in d["pu"]]), "pt": np.stack([gtable(a) for a in d["pt"]]), "pn": i(d["pn"], 1),
            "bu": i(d["bu"], B * R), "bt": i(d["bt"], B * R), "bl": i(d["bl"], B), "bk": i(d["bk"], M), "th": i(d["th"], 1)}
def signs(rng, *sh):
    return 15 * (2 * rng.integers(0, 2, sh) - 1)
def setup_inputs(rng):
    return pack(parts(rng))
def setup_inputs_spread(rng):
    b = rng.integers(-15, 16, (N, 8, F, 16)); b = np.sign(b) * (np.abs(b) >> rng.choice(np.array([0, 0, 0, 1, 2, 3]), (N, 8, F, 1)))
    d = parts(rng, same=0.5, base=b, skew=3)
    w = (2 * rng.integers(0, 2, (N, 8)) - 1) * np.minimum(np.exp2(12 * rng.random((N, 8))).astype(np.int64), 3600)
    d["th"] = np.where(rng.random((N, 8)) < 0.4, w, rng.integers(150, 900, (N, 8)))
    d["pn"] = np.where(rng.random((N, 8)) < 0.3, np.minimum(np.exp2(12 * rng.random((N, 8))).astype(np.int64), P), rng.integers(1, P + 1, (N, 8)))
    d["bk"] = np.where(rng.random((N, 8, M)) < 0.25, rng.integers(-1, B, (N, 8, M)), d["bk"])
    return pack(d)
def poles(rng, sh):
    mt = rng.integers(0, 3, sh + (1,)); mu = rng.integers(0, 3, sh + (1,)); a = rng.integers(0, 2, sh + (R,))
    t = np.where(mt == 0, a, np.where(mt == 1, a[..., :1], np.arange(R) % 2)); u = np.where(mu == 0, rng.integers(0, 2, sh + (R,)), np.where(mu == 1, t, 1 - t))
    return u * (M - 1), t * (M - 1)
def setup_inputs_ends(rng):
    lo = F // 4; d = parts(rng, same=0.8, lo=lo, mode="flip", base=signs(rng, N, 8, F, 16)); x = d["x"]
    v = signs(rng, N, 8, 16); x[:, :, 0] = v; x[:, :, M - 1] = -v
    m = rng.random((N, 8, P // R, 1)) < 0.75; u, t = poles(rng, (N, 8, P // R))
    d["pu"] = np.where(m, u, d["pu"].reshape(u.shape)).reshape(N, 8, P); d["pt"] = np.where(m, t, d["pt"].reshape(u.shape)).reshape(N, 8, P)
    dead = d["cf"] >= lo; u, t = poles(rng, (N, 8, B)); one = np.where(rng.random((N, 8, B)) < 0.5, 1, R)
    dead[..., 0] = True; dead[..., B - 1] = True
    d["bl"] = np.where(dead, one, d["bl"]); d["bu"] = np.where(dead[..., None], u, d["bu"]); d["bt"] = np.where(dead[..., None], t, d["bt"])
    d["bk"] = np.where(d["fo"][None] < lo, d["bk"], np.where(rng.random((N, 8, M)) < 0.5, -1, B - 1)); d["bk"][..., 0] = 0; d["bk"][..., M - 1] = B - 1
    d["bt"][:, :, 0] = 0; d["bt"][:, :, B - 1] = M - 1; turn = np.where(np.arange(R) % 2 == 0, M - 1, 0)
    for q in range(N):
        d["th"][q, rng.permutation(7)] = np.array([3600, 3600, -3600, -3600, -3600, 3151, 3150]); d["th"][q, 7] = 3600
        d["pn"][q, rng.permutation(7)] = np.array([1, 1, P, P, P, P - 1 - int(rng.integers(0, R)), P // 2 + int(rng.integers(0, R))]); d["pn"][q, 7] = P
        d["pt"][q, 7, P - R:] = turn; d["pu"][q, 7, P - R:] = M - 1 - turn; d["pu"][q, 7, P - 1] = turn[R - 1]
        for g in range(8):
            if d["th"][q, g] == 3600: d["bt"][q, g, B - 1] = turn; d["bl"][q, g, B - 1] = R
    return pack(d)
def setup_inputs_corners(rng):
    d = parts(rng); x = d["x"]; sh = int(rng.integers(0, 8)); s = np.arange(R)
    for g in range(8):
        kind = (g + sh) % 8; nm = rng.permutation(M); e, z, rest = nm[:12], nm[12], nm[13:]; lx = rng.integers(2, R + 1, 12); grow = int(np.sum(lx - 1))
        if kind == 7:
            d["bk"][::2, g] = -1; d["pn"][:, g] = P; continue
        for q in range(N):
            x[q, g, nm[:13]] = signs(rng, 13, 16); d["th"][q, g] = 3600; cs = rng.permutation(B)[:12]
            d["bk"][q, g] = -1; d["bk"][q, g, e] = cs; ln = lx
            a = rest[rng.integers(0, len(rest), P)]; b = rest[rng.integers(0, len(rest), P)]; at = R * (1 + rng.permutation(P // (2 * R) - 1)[:12])
            if kind == 4: at[0] = P - R
            ix = at[:, None] + s
            n = P; bt = np.repeat(e[:, None], R, axis=1)
            if kind == 0:
                n = 1; a[0] = e[0]; b[0] = e[0]; ln = np.full(12, 1 + q % 3)
            elif kind <= 4:
                a[at] = e; b[at] = e; a[at - 1] = z; b[at - 1] = z
                if kind == 4: ln = np.full(12, R)
                else: n = P - grow + (0, 0, -1, 1)[kind]
            elif kind == 5:
                a[ix] = e[:, None]; b[ix] = e[:, None]; ln = rng.choice(np.array([1, 2, 3]), 12)
            else:
                bt = np.where(s % 2 == 0, e[:, None], z); a[ix] = bt; ln = R - np.arange(12) % 2
            d["pt"][q, g] = a; d["pu"][q, g] = b; d["pn"][q, g] = n
            d["bl"][q, g, cs] = ln; d["bt"][q, g, cs] = bt; d["bu"][q, g, cs] = rest[rng.integers(0, len(rest), (12, R))]; d["bu"][q, g, cs, ln - 1] = e
    return pack(d)
def setup_inputs_crowd(rng):
    d = parts(rng); x = d["x"]; sh = int(rng.integers(0, 8)); nb = P // R
    full = min(nb, B); at = R * (np.arange(full) * (nb - 1) // (full - 1)); ix = at[:, None] + np.arange(R)
    for g in range(8):
        kind = (g + sh) % 8
        if kind == 3: continue
        if kind >= 4:
            nm = rng.permutation(M); e, rest = nm[:full], nm[full:]
            lo = 1 if kind == 6 or P - full * R + 3 * full // 2 > 280 else 3
            for q in range(N):
                x[q, g, e] = signs(rng, full, 16); d["th"][q, g] = 3600
                cs = rng.permutation(np.append(1 + rng.permutation(B - 2)[:full - 2], [0, B - 1]))
                d["bk"][q, g] = -1; d["bk"][q, g, e] = cs
                a = rest[rng.integers(0, len(rest), P)]; b = rest[rng.integers(0, len(rest), P)]
                if kind <= 5:
                    a[at] = e; b[at] = e; ln = np.full(full, R)
                else:
                    a[ix] = e[:, None]; b[ix] = e[:, None]; ln = lo + np.arange(full) % 2
                d["pt"][q, g] = a; d["pu"][q, g] = b; d["pn"][q, g] = P
                d["bl"][q, g, cs] = ln; d["bt"][q, g, cs] = e[:, None]; d["bu"][q, g, cs] = rest[rng.integers(0, len(rest), (full, R))]; d["bu"][q, g, cs, ln - 1] = e
            continue
        nm = rng.permutation(M)[:4]
        for q in range(N):
            x[q, g, nm] = signs(rng, 4, 16); cs = rng.permutation(B)[:3]; ln = rng.choice(np.array([2, 3, R - 1, R]), 3)
            d["bk"][q, g, nm] = np.append(cs, -1); d["bl"][q, g, cs] = ln; d["bt"][q, g, cs] = nm[:3, None]; d["bu"][q, g, cs, ln - 1] = nm[:3]
            w = np.zeros(nb, np.int64)
            if kind == 1: w[int(rng.choice(np.array([0, nb - 1, int(rng.integers(0, nb))])))] = 1
            if kind == 2: w = rng.integers(0, 3, nb)
            t = np.where(np.arange(P) % 2 == 0, nm[np.repeat(w, R)], nm[3])
            d["pt"][q, g] = t; d["pu"][q, g] = t; d["pn"][q, g] = P
    return pack(d)
def filler(rng, d, q, g, th, rest):
    d["th"][q, g] = th; d["pn"][q, g] = P; d["bk"][q, g] = -1
    d["pu"][q, g] = rest[rng.integers(0, len(rest), P)]; d["pt"][q, g] = rest[np.add.accumulate(rng.integers(1, len(rest), P)) % len(rest)]
def near(rng, a, n):
    i = rng.permutation(16)[:n]; y = np.array(a); y[i] = np.where(a[i] == 15, 14, a[i] + 1)
    return y
def lay(rng, n):
    s = np.arange(R); n = n[:, None]
    return np.sort(np.where(s < n, s, rng.integers(0, R, (len(n), R)) % n), axis=1)
def clones(rng, d, g):
    nm = rng.permutation(M); a = nm[:12 * R].reshape(12, R); b = nm[12 * R:24 * R].reshape(12, R); rest = nm[24 * R:]
    h = [int(v) for v in rng.integers(9, R + 1, 4)]; late = int(rng.integers(8, h[3]))
    na = np.array([3, 3, 2, h[0], h[1], R, h[2], R, h[3], 2, 1, 3]); nb = np.array([3, 2, 3, h[0], h[1], R, h[2], R, h[3], 1, 2, 3])
    for q in range(N):
        filler(rng, d, q, g, 3600, rest)
        x = rng.integers(-15, 16, (12, R, 16)); x[:3, 1] = x[:3, 0]; x[3, h[0] - 1] = x[3, h[0] - 2]; x[11, 1:3] = 0; y = np.array(x)
        y[1, 1] = x[1, 2]; x[2, 1] = y[2, 2]; x[9, 1] = 0; y[10, 1] = 0
        y[6, h[2] - 1] = near(rng, x[6, h[2] - 1], 17 - NEED); y[7, R - 1] = near(rng, x[7, R - 1], 16 - NEED); y[8, late] = near(rng, x[8, late], 17 - NEED)
        d["x"][q, g, a] = x; d["x"][q, g, b] = y; cs = rng.permutation(B)[:12]
        d["bk"][q, g, a[:, 0]] = cs; d["bk"][q, g, b[:, 0]] = cs
        ix = R * rng.permutation(P // R)[:12][:, None] + np.arange(R)
        d["pt"][q, g, ix] = np.take_along_axis(a, lay(rng, na), 1)
        d["bt"][q, g, cs] = np.take_along_axis(b, lay(rng, nb), 1); d["bu"][q, g, cs] = rest[rng.integers(0, len(rest), (12, R))]; d["bl"][q, g, cs] = R
def bound(rng, d, g, sg, ths):
    nm = rng.permutation(M); e, z, w, l, rest = nm[:16], nm[16:32], nm[32:96], nm[96:160], nm[160:]
    i = np.arange(16); pc = i & 1; bc = (i >> 1) & 1; s = np.arange(R); o = int(rng.integers(0, 4))
    for q in range(N):
        th = ths[(q + o) % 4]; filler(rng, d, q, g, th, rest)
        k = int(rng.integers(0, 16)); v = signs(rng, 16); v[k] = 1; up = sg * v; up[k] = th - sg * 3375; lo = np.array(up); lo[k] = up[k] - 1
        d["x"][q, g, e] = v; d["x"][q, g, w] = up; d["x"][q, g, l] = lo
        cs = rng.permutation(B)[:16]; d["bk"][q, g, e] = cs; at = R * rng.permutation(P // R)[:16]; t = np.where(s == 0, e[:, None], z[:, None])
        d["pt"][q, g, at[:, None] + s] = t; d["pu"][q, g, at] = np.where(pc == 1, l[rng.integers(0, 64, 16)], w[rng.integers(0, 64, 16)])
        d["bt"][q, g, cs] = t; d["bl"][q, g, cs] = np.where(bc == 1, R, 1)
        u = rest[rng.integers(0, len(rest), (16, R))]; u[:, 0] = np.where(bc == 1, l[rng.integers(0, 64, 16)], w[rng.integers(0, 64, 16)]); d["bu"][q, g, cs] = u
def singles(rng, d, g):
    pr = rng.permutation(M // 2); side = rng.integers(0, 2, 12); e = 2 * pr[:12] + side; y = 2 * pr[:12] + 1 - side
    rest = (2 * pr[12:, None] + np.arange(2)).reshape(-1)
    for q in range(N):
        filler(rng, d, q, g, -3600, rest)
        at = R * np.append(P // R - 1, rng.permutation(P // R - 1)[:11]) + R - 1; cs = rng.permutation(B)[:12]
        d["pt"][q, g, at] = e; d["pt"][q, g, at - 1] = y; d["pu"][q, g, at - 1] = y
        d["bk"][q, g, e] = cs; d["bl"][q, g, cs] = 1; d["bt"][q, g, cs, 0] = e; d["bu"][q, g, cs, 0] = rest[rng.integers(0, len(rest), 12)]
def setup_inputs_edge(rng):
    d = parts(rng, mode="near", alts=(HALF, HALF, HALF, HALF + 1)); x = d["x"]; sh = int(rng.integers(0, 8))
    m = rng.random((N, 8, P)) < 0.04; m[..., 0] = False; d["pt"] = np.where(m, np.roll(d["pt"], 1, axis=-1), d["pt"])
    for q in range(N):
        for g in range(8):
            if (g + sh) % 8 >= 4: continue
            u, t = d["pu"][q, g], d["pt"][q, g]; v = np.add.reduce(x[q, g][u] * x[q, g][t], axis=1)[:-1]
            v = np.unique(v[t[1:] != t[:-1]]); v = v[(v > 1026) & (v < 1300)]; w = v[np.isin(v - 1, v)]
            if len(w): d["th"][q, g] = rng.choice(w)
            elif len(v): d["th"][q, g] = rng.choice(v)
    for g in range(8):
        kind = (g + sh) % 8
        if kind == 4: clones(rng, d, g)
        elif kind == 5: bound(rng, d, g, -1, (-3375, -3371, -3372, -3378))
        elif kind == 6: bound(rng, d, g, 1, (3376, 3372, 3373, 3377))
        elif kind == 7: singles(rng, d, g)
    return pack(d)
def check_inputs(d):
    bad = []
    for k, lo, hi in (("tones", -15, 15), ("pu", 0, M - 1), ("pt", 0, M - 1), ("pn", 1, P), ("bu", 0, M - 1), ("bt", 0, M - 1), ("bl", 1, R), ("bk", -1, B - 1), ("th", -3600, 3600)):
        a = np.asarray(d[k]).astype(np.float32)
        if not np.all((a >= lo) & (a <= hi)): bad.append("range of " + k)
        elif k == "tones" and np.any(a != np.rint(a)): bad.append("whole numbers in tones")
        elif k == "tones" and np.any((a == 0) & np.signbit(a)): bad.append("-0.0 in tones")
    return bad
def tone_numbers(t, head):
    new = np.array(head); new[1:] |= t[1:] != t[:-1]; cnt = np.add.accumulate(new.astype(np.int64))
    return cnt - cnt[np.maximum.accumulate(np.where(head, np.arange(len(t)), 0))]
def visit(x, u, t, bu, bt, bl, bk, th):
    n = len(t); j = np.arange(n); s = np.arange(R)
    score = np.add.reduce(x[u] * x[t], axis=1)
    end = (j % R == R - 1) | (j == n - 1); end[:-1] |= (t[1:] != t[:-1]) & (score[:-1] >= th)
    head = np.ones(n, bool); head[1:] = end[:-1]
    first = np.flatnonzero(head); last = np.flatnonzero(end); size = last - first + 1
    k = tone_numbers(t, head)
    bh = np.zeros((B, R), bool); bh[:, 0] = True; kb = tone_numbers(bt.reshape(-1), bh.reshape(-1)).reshape(B, R)
    ci, si = np.nonzero(s < bl[:, None]); key = np.zeros((B, R), np.int64); key[ci, kb[ci, si]] = bt[ci, si]
    tones_of = kb[np.arange(B), bl - 1] + 1
    c = bk[t[first]]; c0 = np.maximum(c, 0)
    agree = np.add.reduce((x[t] == x[key[np.repeat(c0, size), k]]).astype(np.int64), axis=1) >= NEED
    match = (c >= 0) & (k[last] + 1 == tones_of[c0]) & (np.minimum.reduceat(agree.astype(np.int64), first) == 1)
    o = np.flatnonzero(match); o = o[np.unique(first[o] // R, return_index=True)[1]]
    o = o[np.unique(c[o], return_index=True)[1]]
    begin = np.array(first); length = np.array(size); begin[o] = n + c[o] * R; length[o] = bl[c[o]]
    before = np.add.accumulate(length) - length; src = (np.repeat(begin - before, length) + np.arange(np.sum(length)))[:P]
    nu = np.concatenate([u, bu.reshape(-1)])[src]; nt = np.concatenate([t, bt.reshape(-1)])[src]
    ix = np.minimum(first[o][:, None] + s, n - 1); bu, bt, bl = np.array(bu), np.array(bt), np.array(bl)
    bu[c[o]] = u[ix]; bt[c[o]] = t[ix]; bl[c[o]] = size[o]
    return nu, nt, bu, bt, bl
def reference(tones, pu, pt, pn, bu, bt, bl, bk, th):
    x = np.ascontiguousarray(tones.astype(np.float32).reshape(N, 8, 16, M).transpose(0, 1, 3, 2)).astype(np.int64)
    lu = np.stack([gentries(a) for a in pu]).astype(np.int64); lt = np.stack([gentries(a) for a in pt]).astype(np.int64)
    piece = {(r, g): (lu[r, g, :pn[r, g, 0]], lt[r, g, :pn[r, g, 0]]) for r in range(N) for g in range(8)}
    u = bu.astype(np.int64).reshape(N, 8, B, R); t = bt.astype(np.int64).reshape(N, 8, B, R); ln = bl.astype(np.int64); pt_ = bk.astype(np.int64)
    for v in range(VI):
        for q in range(N):
            r = (q - HO * v) % N
            for g in range(8):
                a, b, u[q, g], t[q, g], ln[q, g] = visit(x[q, g], piece[r, g][0], piece[r, g][1], u[q, g], t[q, g], ln[q, g], pt_[q, g], int(th[q, g, 0]))
                piece[r, g] = (a, b)
    fu = np.full((N, 8, P), -1, np.int64); ft = np.full((N, 8, P), -1, np.int64)
    for q in range(N):
        for g in range(8):
            a, b = piece[(q - HO * (VI - 1)) % N, g]; fu[q, g, :len(a)] = a; ft[q, g, :len(b)] = b
    live = np.arange(R) < ln[..., None]
    return {"yu": np.stack([gtable(a) for a in fu]).astype(np.float32), "yt": np.stack([gtable(a) for a in ft]).astype(np.float32),
            "zu": np.where(live, u, -1).reshape(N, 8, B * R).astype(np.float32), "zt": np.where(live, t, -1).reshape(N, 8, B * R).astype(np.float32)}

@@ -1,0 +1,847 @@
+from concourse.mybir import AluOpType as OP, ActivationFunctionType as AF
+
+F32, BF, F16, I32, U16 = "float32", "bfloat16", "float16", "int32", "uint16"
+SZ = {F32: 4, BF: 2, F16: 2, I32: 4, U16: 2}
+AW = 4128
+XT0, A0, BB, A1, XT1 = 0, 4096, 4096 + AW, 4096 + 2 * AW, 4096 + 3 * AW
+BIG, HUGE = float(2 ** 17), float(2 ** 22)
+
+
+def _s(shape, dt):
+    return ("sbuf", [128] + list(shape), dt)
+
+
+SCRATCH = {
+    "TN": _s([4112], BF), "XA": _s([XT1 + 4112], BF), "T1": _s([4096], BF), "T2": _s([4096], BF),
+    "LA": _s([8208], BF), "LB": _s([8208], BF), "RL": _s([8208], BF),
+    "WE": _s([24576], BF),
+    "S0": _s([1536], BF), "S1": _s([1536], BF), "R0": _s([1536], BF), "R1": _s([1536], BF),
+    "R2": _s([1280], BF), "R3": _s([1280], BF), "B1": _s([256], BF), "B2": _s([256], BF), "i5": _s([256], I32),
+    "SR0": _s([256], U16), "SR1": _s([256], U16), "SL0": _s([256], U16), "SL1": _s([256], U16),
+    "i0": _s([256], I32), "i1": _s([256], I32), "i2": _s([256], I32), "i3": _s([256], I32), "i4": _s([256], I32),
+    "f0": _s([256], F32), "f1": _s([256], F32), "f2": _s([256], F32), "f3": _s([256], F32),
+    "ism": _s([64], I32), "col": _s([48], F32), "XM": _s([16], F32), "sm": _s([208], F32), "smb": _s([96], BF),
+    "ONE": _s([256], BF), "ZB": _s([16], BF), "K1": _s([256], BF), "K2": _s([256], BF), "KZ": _s([256], BF), "IO": _s([256], F32), "JW": _s([256], F32), "J16": _s([256], F32), "CW": _s([256], F32),
+    "IB": _s([128], BF), "IF": _s([128], F32), "IH": _s([128], F16), "IN": _s([128], BF), "I8": _s([128], BF),
+    "IA": _s([128], BF), "IAN": _s([128], BF), "IG": _s([128], BF), "UT": _s([128], F32),
+    "BLK": _s([128], BF), "TI": _s([128], BF), "TS": _s([128], BF), "TC": _s([128], BF), "BVW": _s([128], BF),
+    "sel": _s([72], BF), "PH": _s([8], F32), "SX": _s([144], BF), "SX5": _s([144], BF), "SXU": _s([144], BF),
+    "SXT": _s([144], BF), "WM": _s([144], BF),
+    "MK": _s([256], F32), "RST": _s([256], F32), "KP": _s([256], BF), "XS": _s([256], F32), "OF": _s([128], F32), "S8": _s([256], BF), "B16": _s([256], BF),
+    "IOC": _s([256], BF), "CB": _s([256], BF), "THT": _s([256], F32), "G8": _s([256], F32), "TM": _s([256], F32),
+    "NL": _s([528], F16), "LT_": _s([256], U16), "LU": _s([256], U16), "LI": _s([256], U16), "LK": _s([256], U16),
+    "LBK": _s([256], U16), "LS": _s([80], U16), "NQ": _s([272], BF), "NV": _s([256], BF), "NE": _s([272], BF),
+    "C16": _s([272], BF), "THR": _s([256], F32), "Z": _s([256], F32), "NW": _s([256], BF),
+    "SS": _s([264], F32), "VI": _s([256], BF),
+    "LTB": _s([256], BF), "LTT": _s([272], BF), "LG": _s([256], BF), "VAL": _s([256], BF), "M2": _s([256], BF),
+    "WK": _s([520], F32), "WB": _s([520], F32), "YO": _s([512], F32), "ZO": _s([512], F32),
+}
+for _k in range(8):
+    SCRATCH["P%d" % _k] = ("psum", [128, 512], F32)
+SEMAPHORES = ["qv", "qa", "qt", "qp"] + ["d%d" % _k for _k in range(40)] + ["ar%d" % _k for _k in range(8)] + ["lo%d" % _k for _k in range(8)]
+ALLP = (1 << 128) - 1
+CY, PE, CHUNK, SLACK, ROUNDS = 1.04e-3, 0.53e-3, 512, 0.01, 40
+JITTER = 0.0
+
+
+def build(T):
+    ops = []
+
+    def R(name, a=0, b=None, st=1, p=None):
+        name = "T1" if name == "OH" else name
+        shp, dt = SCRATCH[name][1], SCRATCH[name][2]
+        if b is None:
+            b = shp[1]
+        pm = ALLP
+        ps = slice(0, 128)
+        if p is not None:
+            ps = slice(p[0], p[1], p[2])
+            pm = sum(1 << q for q in range(p[0], p[1], p[2]))
+        ap = T[name][ps, a:b:st] if st != 1 else T[name][ps, a:b]
+        return {"ap": ap, "acc": [(name, a * SZ[dt], b * SZ[dt], pm)], "off": [], "n": len(range(a, b, st)), "w": SZ[dt],
+                "ps": SCRATCH[name][0] == "psum", "rows": bin(pm).count("1")}
+
+    def X(name):
+        return {"ap": T[name][:], "acc": [], "off": [], "n": 0, "w": 4, "ps": False, "rows": 0}
+
+    def IND(win, off):
+        return {"ap": win["ap"].indirect(off["ap"]), "acc": win["acc"], "off": off["acc"], "n": 16 * off["n"], "w": win["w"], "ps": False}
+
+    def add(q, fn, outs, ins, grp=None, both=False):
+        rd, wr = [], []
+        views = [i for i in ins if isinstance(i, dict)]
+        for o in outs:
+            wr += o["acc"]
+            rd += o["off"]
+        for i in views:
+            rd += i["acc"] + i["off"]
+        o = outs[0]
+        n = o["n"]
+        if grp is not None:
+            c = max(x["n"] * x["w"] * x["rows"] for x in [o] + views) / 200e3
+        elif q == "t":
+            c = max(64, views[1]["n"]) * PE * (4 if views[0]["w"] == 4 else 1)
+        elif q == "p":
+            c = 0.15 + 2 * n * CY
+        elif o["off"]:
+            c = 0.05 + 3.5 * n * CY
+        elif views and views[0]["off"]:
+            c = 0.06 + 1.56 * n * CY
+        elif q == "a":
+            c = 0.1 + max(64, n) * CY
+        else:
+            f = 0.5 if all(x["w"] == 2 for x in [o] + views) else 1.0
+            if both and not (views[0]["ps"] or views[1]["ps"]):
+                f *= 2
+            c = 0.03 + max(64, n * f) * CY
+        ops.append({"q": q, "fn": fn, "rd": rd, "wr": wr, "grp": grp, "c": c})
+
+    def u(x):
+        return x["ap"] if isinstance(x, dict) else x
+
+    def ts(o, i, s1, op0, s2=None, op1=None):
+        if op1 is None:
+            add("v", lambda g: g.vector.tensor_scalar(u(o), u(i), u(s1), None, op0), [o], [i, s1])
+        else:
+            add("v", lambda g: g.vector.tensor_scalar(u(o), u(i), u(s1), u(s2), op0, op1), [o], [i, s1, s2])
+
+    def tt(o, a, b, op):
+        add("v", lambda g: g.vector.tensor_tensor(u(o), u(a), u(b), op), [o], [a, b], both=True)
+
+    def cp(o, i):
+        add("v", lambda g: g.vector.tensor_copy(u(o), u(i)), [o], [i])
+
+    def ms(o, c):
+        add("v", lambda g: g.vector.memset(u(o), c), [o], [])
+
+    def scan(o, d0, d1, init, op0, op1):
+        add("v", lambda g: g.vector.tensor_tensor_scan(u(o), u(d0), u(d1), init, op0, op1), [o], [d0, d1])
+
+    def act(o, i, scale=1.0, bias=0.0, fn=None):
+        f = fn if fn is not None else (AF.Copy if (not isinstance(bias, dict) and bias == 0.0) else AF.Identity)
+        add("a", lambda g: g.scalar.activation(u(o), u(i), f, u(bias), u(scale)), [o], [i, scale, bias])
+
+    def mm(o, l, r, st=True, sp=True):
+        add("t", lambda g: g.tensor.matmul(u(o), u(l), u(r), st, sp), [o], [l, r])
+
+    def iota(o, pat, base=0, cm=0, integer=False):
+        if integer:
+            add("p", lambda g: g.iota(u(o), pat, base, cm), [o], [])
+        else:
+            add("p", lambda g: g.iota(u(o), pat, base, cm, allow_small_or_imprecise_dtypes=True), [o], [])
+
+    def asel(o, i, pat, op, fill, base, cm):
+        add("p", lambda g: g.affine_select(u(o), u(i), pat, op, fill, base, cm), [o], [i])
+
+    ng = [0]
+
+    def dma(q, pairs):
+        k = ng[0]
+        ng[0] += 1
+        for o, i in pairs:
+            if q == "s":
+                add("s", lambda g, o=o, i=i: g.sync.dma_start(u(o), u(i)), [o], [i], "d%d" % k)
+            else:
+                add("a", lambda g, o=o, i=i: g.scalar.dma_start(u(o), u(i)), [o], [i], "d%d" % k)
+
+    def send(k, land, src, step=1):
+        ops.append({"q": "p", "send": (k, u(land), u(src)), "step": step, "rd": src["acc"], "wr": [], "grp": "lo%d" % k,
+                    "c": src["n"] * src["w"] * 128 / 60e3})
+
+    def arrive(k, land, step=1):
+        ops.append({"q": "x", "step": -step, "rd": [], "wr": land["acc"], "grp": "ar%d" % k, "c": 0.0, "after": "lo%d" % k})
+
+    def C(k):
+        return R("col", k, k + 1)
+
+    def XMc(k):
+        return R("XM", k, k + 1)
+
+    def rows(name, r, a, b):
+        return R(name, a, b, 1, (r, 128, 16))
+
+    P8 = (0, 8, 1)
+    P1 = (0, 1, 1)
+    cX, cG, cU, cT, cE1, cE2, cBV, cM, cO, cINV, cPW, cN, cTH, cA, cB_, cS4, cS16, cC = range(18)
+    sSC, sNE, sC, sN, sE1, sE2 = 0, 8, 16, 24, 48, 56
+
+    dma("s", [(R("i4"), X("bk"))])
+    dma("s", [(R("i2"), X("bt"))])
+    dma("a", [(R("ism", 0, 1, 1, P8), X("pn")), (R("ism", 4, 5, 1, P8), X("th")), (R("i5", 0, 256, 1, P8), X("bl"))])
+    dma("s", [(R("i0"), X("pt")), (R("i1"), X("pu"))])
+    dma("s", [(R("TN", 16, 4112), X("tones"))])
+    dma("s", [(R("i3"), X("bu"))])
+    for k in (1, 3, 4, 5):
+        for op in ops:
+            if op["grp"] == "d%d" % k:
+                op["behind"] = "d%d" % {1: 0, 3: 1, 4: 3, 5: 4}[k]
+    iota(R("ism", 8, 9), [[0, 1]], 0, 1, True)
+    iota(R("IO"), [[1, 256]])
+    ms(R("ONE"), 1.0)
+    ms(R("LB", 0, 4112), 0.0)
+    asel(R("IB"), R("ONE", 0, 128), [[-1, 128]], OP.is_equal, 0.0, 0, 1)
+    iota(R("G8", 0, 256, 1, P8), [[0, 2], [1, 8], [0, 16]], 0, -1)
+    ts(R("ism", 9, 10), R("ism", 8, 9), 15, OP.bitwise_and)
+    ts(R("ism", 10, 11), R("ism", 8, 9), 4, OP.arith_shift_right)
+    cp(R("col", cX, cX + 2), R("ism", 9, 11))
+    ts(R("XM"), R("IO", 0, 16), C(cX), OP.is_equal)
+    ts(R("PH"), R("IO", 0, 8), C(cG), OP.is_equal)
+    ts(R("G8", 0, 256, 1, P8), R("G8", 0, 256, 1, P8), 0.0, OP.is_equal)
+    act(R("IF"), R("IB"))
+    act(R("JW"), R("IO"), 16.0, C(cX))
+    act(C(cU), XMc(0), 1.0, XMc(1))
+    act(C(cT), XMc(2), 1.0, XMc(3))
+    act(R("sel", sN, sN + 8), R("PH"), C(cU))
+    act(R("sel", sN + 8, sN + 16), R("PH"), C(cT))
+    act(R("sel", sN + 16, sN + 24), R("PH"), C(cU))
+    cp(R("IH"), R("IB"))
+
+    def dig(dst, k, s, first):
+        first(R(dst, 512 * k, 512 * k + 256), s)
+        tt(R(dst, 512 * k + 256, 512 * k + 512), s, R(dst, 512 * k, 512 * k + 256), OP.subtract)
+
+    def stage(dst, src, off, which):
+        dma("s", [(R(dst, 256 * k, 256 * k + 256), rows(src, r, off, off + 4096)) for k, r in which])
+
+    def unstage(dst, off, src, which, q="s"):
+        dma(q, [(rows(dst, r, off, off + 4096), R(src, 256 * k, 256 * k + 256)) for k, r in which])
+
+    FOUR = [(r, r) for r in range(4)]
+    ts(R("LG"), R("i4"), 1.0, OP.add)
+    send(6, R("B1"), R("LG"), -1)
+    send(7, R("B2"), R("LG"), -2)
+    dig("S0", 1, R("i2"), cp)
+    unstage("LB", 0, "S0", FOUR[2:], "a")
+    dig("S0", 0, R("i3"), cp)
+    ms(R("TN", 0, 16), 0.0)
+    cp(R("sm", 0, 8, 4, P8), R("ism", 0, 8, 4, P8))
+    mm(R("P6", 400, 402), R("G8", 0, 128, 1, P8), R("sm", 0, 8, 4, P8))
+    ts(R("f2"), R("JW"), R("P6", 400, 401), OP.is_lt)
+    ts(R("f0"), R("i0"), 1.0, OP.add)
+    tt(R("f0"), R("f0"), R("f2"), OP.mult)
+    ts(R("LT_"), R("f0"), 15.0, OP.add)
+    ts(R("f1"), R("i1"), 1.0, OP.add)
+    tt(R("f1"), R("f1"), R("f2"), OP.mult)
+    ts(R("LU"), R("f1"), 15.0, OP.add)
+    act(R("sel", sSC, sSC + 8), R("PH"))
+    act(C(cC), XMc(4), 16.0)
+    act(R("sel", sC, sC + 8), R("PH"), C(cC))
+    act(R("IN"), R("IB"), -1.0)
+    act(R("I8"), R("IB"), -8192.0)
+    act(R("col", cTH, cTH + 1, 1, P8), R("sm", 4, 5, 1, P8), 1.0, 8192.0)
+    act(R("TM", 0, 256, 1, P8), R("G8", 0, 256, 1, P8), R("col", cTH, cTH + 1, 1, P8))
+    asel(R("TM", 0, 256, 1, P8), R("TM", 0, 256, 1, P8), [[0, 16], [1, 16]], OP.not_equal, -4096.0, -15, 0)
+    iota(R("f3", 0, 128), [[1, 8], [0, 16]])
+    ts(R("BLK"), R("f3", 0, 128), C(cG), OP.is_equal)
+    asel(R("TI"), R("BLK"), [[1, 128]], OP.is_ge, 0.0, 0, -1)
+    iota(R("B16"), [[16, 256]])
+    act(C(cA), C(cG), 16.0, 15.0)
+    ts(R("SX"), R("IO", 0, 144), C(cA), OP.is_equal)
+    ms(R("NQ", 0, 1), 1.0)
+    ms(R("NE", 0, 1), 0.0)
+    ms(R("C16", 0, 1), 0.0)
+    ms(R("OF"), 1.0)
+
+    def spread(dst, src):
+        cp(R("XS", 0, 256, 16), R(src, 15, 256, 16))
+        scan(dst, R("KP"), R("XS"), 0.0, OP.mult, OP.add)
+
+    def lin2bars(ps, src, base, sel, es=(0, 1)):
+        for e in es:
+            for s in range(16):
+                mm(R(ps[0], ps[1] + 128 * e + s, ps[1] + 128 * e + 128, 16), R(src, base + 2048 * e + s, base + 2048 * e + 2048, 16), sel)
+
+    def names2bars(src, base):
+        for e in (0, 1):
+            for s in range(16):
+                mm(R("P0", 256 * e + s, 256 * e + 256, 16), R(src, base + 2048 * e + s, base + 2048 * e + 2048, 16), R("sel", sN + 8 * e, sN + 8 * e + 16))
+
+    def t_list(dst):
+        ts(R("NL", 128, 384), R("P0", 128, 384), -2047.0, OP.add)
+        for e in (0, 1):
+            mm(R("P1", 128 * e, 128 * e + 128), R("NL", 128 + 128 * e, 256 + 128 * e), R("IH"))
+        ts(dst, R("P1", 0, 256), 2063.0, OP.add)
+
+    def u_bars():
+        ts(R("NL", 0, 128), R("P0", 0, 128), -2047.0, OP.add)
+        ts(R("NL", 384, 512), R("P0", 384, 512), -2047.0, OP.add)
+
+    def new_flags():
+        tt(R("NQ", 1, 256), R("NL", 128, 383), R("NL", 129, 384), OP.not_equal)
+        ms(R("NQ", 16, 257, 16), 1.0)
+
+    def new_w():
+        for e in (0, 1):
+            mm(R("P5", 256 + 128 * e, 384 + 128 * e), R("NQ", 128 * e, 128 * e + 128), R("IB"))
+        act(R("NW"), R("P5", 256, 512))
+
+    def steps(k0, k1):
+        for k in range(k0, k1):
+            act(R("OH", 256 * k, 256 * k + 256), R("P5", 0, 256), -1.0, k + 0.5, AF.Sign)
+
+    def pos_mm(k0, k1):
+        if k0 == 0:
+            mm(R("P0", 0, 256), R("ONE", 0, 128, 1, P1), R("B16", 0, 256, 1, P1), True, False)
+            mm(R("P0", 0, 256), R("ONE", 0, 128, 1, P1), R("B16", 0, 256, 1, P1), False, False)
+        for k in range(k0, k1):
+            mm(R("P0", 0, 256), R("SX", 15 - k, 143 - k), R("OH", 256 * k, 256 * k + 256), False, k == 15)
+
+    def gat(q, dst, a, b, win, lst):
+        for a0 in range(a, b, CHUNK):
+            b0 = min(b, a0 + CHUNK)
+            o, i = R(dst[0], dst[1] + a0, dst[1] + b0), IND(win, R(lst, a0 // 16, b0 // 16))
+            if q == "a":
+                act(o, i)
+            else:
+                cp(o, i)
+                if q == "f":
+                    act(o, i)
+                    other = ops.pop()
+                    ops[-1]["alt"] = {"v": ops[-1]["fn"], "a": other["fn"]}
+
+    def fill(name, a, b, c):
+        for a0 in range(a, b, 1024):
+            iota(R(name, a0, min(b, a0 + 1024)), [[0, min(b, a0 + 1024) - a0]], c, 0)
+
+    def last_tones(aoff):
+        act(R("M2"), IND(R("XA", aoff, aoff + AW), R("LS", 64, 80)))
+        cp(IND(R("XA", BB, BB + AW), R("LS", 64, 80)), R("M2"))
+
+    names2bars("LB", 0)
+    arrive(6, R("B1"), -1)
+    arrive(7, R("B2"), -2)
+    dma("s", [(rows("LB", 4 + k, 16, 4112), R(n)) for k, n in enumerate(("LG", "B1", "B2"))])
+    t_list(R("SL1"))
+    gat("f", ("XA", XT1), 0, 4096, R("TN"), "SL1")
+    new_flags()
+    new_w()
+    mm(R("P5", 0, 256), R("TI"), R("NW"))
+    cp(R("THR", 0, 256, 1, P8), R("i5", 0, 256, 1, P8))
+    mm(R("P7", 0, 256), R("G8", 0, 128, 1, P8), R("THR", 0, 256, 1, P8))
+    act(R("LTB"), R("P7", 0, 256), 1.0, -1.0)
+    act(R("M2"), R("P5", 0, 256))
+    for k in range(16):
+        ts(R("OH", 256 * k, 256 * k + 256), R("M2"), k + 0.5, OP.is_lt, 2.0, OP.mult)
+    pos_mm(0, 16)
+    ts(R("LK"), R("P0", 0, 256), 0.5, OP.mult)
+    ts(R("VI"), R("LTB"), C(cX), OP.is_ge)
+    tt(R("VI"), R("VI"), R("NW"), OP.mult)
+    for x in range(16):
+        mm(R("P6", 416, 432), R("SX", 15 - x, 143 - x), R("VI", x, 256, 16), x == 0, x == 15)
+    act(C(cB_), C(cX), 16.0, 15.0)
+    act(R("sm", 16, 32), R("IO", 0, 16), 256.0, C(cB_))
+    tt(R("sm", 16, 32), R("sm", 16, 32), R("P6", 416, 432), OP.add)
+    cp(R("LS", 64, 80), R("sm", 16, 32))
+    fill("XA", BB - 16, BB + AW + 16, 99)
+    iota(R("XA", A0, A0 + 16), [[0, 16]], 99, 0)
+    iota(R("XA", XT1 - 16, XT1), [[0, 16]], 99, 0)
+    iota(R("XA", XT1 + 4096, XT1 + 4112), [[0, 16]], 99, 0)
+    for e in (0, 1):
+        mm(R("P1", 128 * e, 128 * e + 128), R("f0", 128 * e, 128 * e + 128), R("IF"))
+    ts(R("NL", 128, 384), R("P1", 0, 256), -2048.0, OP.add)
+    ms(R("NL", 384, 400), 0.0)
+
+    def late_constants_a():
+        act(R("sel", sNE, sNE + 8), R("PH"), BIG)
+        act(R("IA"), R("IB"), float(AW))
+        act(R("IAN"), R("IB"), -float(AW))
+        act(R("IG"), R("IB"), HUGE)
+        iota(R("S8"), [[0, 16], [8192, 16]])
+        iota(R("MK"), [[0, 16], [1, 16]])
+        iota(R("IOC"), [[1, 256]], 1)
+        asel(R("UT"), R("OF"), [[1, 128]], OP.is_gt, 0.0, 0, -1)
+        asel(R("TS"), R("BLK"), [[1, 128]], OP.is_gt, 0.0, 0, -1)
+        asel(R("TC"), R("BLK"), [[-1, 128]], OP.is_ge, 0.0, 0, 1)
+        fill("WE", 0, 4096, 0)
+        fill("WE", 8192, 12288, 0)
+        fill("RL", 0, 8192, 0)
+
+    def late_constants_b():
+        for c, terms in ((cE1, ((0, 16.0), (1, -16.0), (2, -1.0), (3, 1 / 32), (4, -4032.0))),
+                         (cE2, ((0, -16.0), (1, 16.0), (2, 1.0), (4, 4032.0), (5, -1.0))),
+                         (cBV, ((1, 256.0), (2, 16.0), (3, -15 / 32), (4, 64256.0))),
+                         (cM, ((0, 1 / 16), (2, 1 / 8192), (3, 32.0))),
+                         (cO, ((0, 1 / 32 - 0.5), (2, 2.0 ** -14 - 0.5))),
+                         (cINV, ((0, -1.0), (2, -1.0)))):
+            for n, (r, w) in enumerate(terms):
+                act(C(c), XMc(r), w, C(c) if n else 0.0)
+        act(R("sel", sE1, sE1 + 8), R("PH"), C(cE1))
+        act(R("sel", sE2, sE2 + 8), R("PH"), C(cE2))
+        act(R("BVW"), R("BLK"), C(cBV))
+        act(R("SX5"), R("SX"), XMc(5))
+        act(R("SXU"), R("SX"), C(cU))
+        act(R("SXT"), R("SX"), C(cT))
+        act(R("CB"), R("IO"), XMc(1), XMc(1))
+        act(R("J16"), R("JW"), 16.0)
+        act(R("CW"), R("JW"), 16.0, 65551.0)
+        act(C(cS4), C(cX), 1.0, 4096.0)
+        act(C(cS16), C(cX), 16.0)
+        act(C(cA), C(cX), 16.0, 16384.0)
+        act(R("sm", 32, 48), R("IO", 0, 16), 256.0, C(cA))
+        act(C(cB_), C(cX), 1.0, 257.0)
+        act(R("sm", 48, 64), R("IO", 0, 16), 16.0, C(cB_))
+        for n in ("LA", "LB", "RL"):
+            act(R(n, 8192, 8208), R("ONE", 0, 16), C(cINV))
+
+    def late_constants_c():
+        P16 = (0, 16, 1)
+        asel(R("KP"), R("ONE"), [[0, 16], [1, 16]], OP.not_equal, 0.0, 0, 0)
+        act(R("RST"), R("KP"), -float(2 ** 23), float(2 ** 23))
+        act(R("K1"), R("KP"), -65536.0, 65536.0)
+        act(R("K2"), R("KP"), 0.5)
+        scan(R("K1"), R("K2"), R("K1"), 0.0, OP.mult, OP.add)
+        act(R("MK"), R("MK"), -1.0, C(cX), AF.Abs)
+        act(R("MK"), R("MK"), -1.0, 1.0, AF.Relu)
+        tt(R("sm", 64, 80), R("K1", 0, 16), R("XM"), OP.mult)
+        add("v", lambda g: g.vector.tensor_reduce(u(C(cPW)), u(R("sm", 64, 80)), AX, OP.add), [C(cPW)], [R("sm", 64, 80)])
+        act(C(cPW), C(cPW), 0.5)
+        act(R("WM"), R("SX"), C(cPW))
+        asel(R("K1", 0, 256, 1, P16), R("K1", 0, 256, 1, P16), [[-1, 16], [0, 16]], OP.is_ge, 1.0, 0, 1)
+        asel(R("K1", 0, 256, 1, P16), R("K1", 0, 256, 1, P16), [[1, 16], [0, 16]], OP.is_ge, float(2 ** 20), 0, -1)
+        asel(R("K2", 0, 128, 1, P16), R("ONE", 0, 128, 1, P16), [[0, 8], [1, 16]], OP.is_equal, 0.0, 0, -1)
+        mm(R("P7", 0, 256), R("K2", 0, 128, 1, P16), R("K1", 0, 256, 1, P16))
+        act(R("THT"), R("P7", 0, 256))
+        iota(R("XS"), [[0, 256]])
+        iota(R("KZ", 0, 256, 1, P1), [[0, 256]])
+        ms(R("SS", 0, 1), 0.0)
+        ms(R("smb", 32, 33), 0.0)
+        ms(R("ZB"), 0.0)
+        ms(R("LTT", 0, 1), 0.0)
+        act(R("LTT", 1, 257), R("LTB"), XMc(5), XMc(4))
+
+    for v in range(3):
+        last = v == 2
+        xt, ak, an = (XT0, A0, A1) if v % 2 == 0 else (XT1, A1, A0)
+        lin, nxt = ("LA", "LB") if v % 2 == 0 else ("LB", "LA")
+        if v > 0:
+            u_bars()
+            for e in (0, 1):
+                mm(R("P1", 256 + 128 * e, 384 + 128 * e), R("NL", 384 * e, 384 * e + 128), R("IH"))
+        new_flags()
+        ts(R("NV"), R("NL", 129, 385), -2047.5, OP.is_lt, 2.0, OP.mult)
+        if v > 0:
+            ts(R("LU"), R("P1", 256, 512), 2063.0, OP.add)
+        if v == 0:
+            gat("f", ("LA", 4096), 0, 4096, R("LB", 0, 4112), "LT_")
+        mm(R("P4", 0, 256), R("OF", 0, 128, 1, P8), R("TM", 0, 256, 1, P8), True, False)
+        mm(R("P4", 0, 256), R("I8"), R("NQ", 1, 257), False, False)
+        mm(R("P4", 0, 256), R("I8"), R("NV"), False, True)
+        lin2bars(("P3", 0), lin, 4096, R("sel", sC, sC + 8))
+        for k in range(8):
+            gat("a", ("XA", xt), 512 * k, 512 * k + 512, R("TN"), "LT_")
+            tt(R("T2", 512 * k, 512 * k + 512), IND(R("TN"), R("LU", 32 * k, 32 * k + 32)), R("XA", xt + 512 * k, xt + 512 * k + 512), OP.mult)
+            if k == 2:
+                act(R("C16", 1, 257), R("P3", 0, 256))
+                act(R("THR"), R("P4", 0, 256))
+                for ps, third in (("P3", R("NQ", 0, 256)), ("P4", R("ONE"))):
+                    mm(R(ps, 256, 512), R("IB"), R("C16", 0, 256), True, False)
+                    mm(R(ps, 256, 512), R("IN"), R("C16", 1, 257), False, False)
+                    mm(R(ps, 256, 512), R("IB"), third, False, True)
+            if k == 3:
+                lin2bars(("P2", 0), "T2", 0, R("sel", sSC, sSC + 8), (0,))
+        lin2bars(("P2", 0), "T2", 0, R("sel", sSC, sSC + 8), (1,))
+        if v == 0:
+            gat("f", ("XA", A0 + 16), 0, 4096, R("XA", XT1, XT1 + 4112), "LK")
+            late_constants_a()
+            act(R("YO", 0, 256), R("f1"), 1.0, -1.0)
+            act(R("YO", 256, 512), R("f0"), 1.0, -1.0)
+            dig("S1", 0, R("YO", 0, 256), act)
+            dig("S1", 1, R("YO", 256, 512), act)
+            act(C(cA), C(cX), 256.0)
+            ts(R("LBK"), R("IO"), C(cA), OP.add)
+            unstage("T1", 0, "S1", FOUR)
+            gat("a", ("LA", 0), 0, 4096, R("LB", 0, 4112), "SL1")
+            stage("S0", "LA", 0, [(4, 5), (5, 6)])
+            unstage("LA", 0, "S0", FOUR)
+            send(0, R("R0"), R("S0"))
+        else:
+            gat("f", ("XA", ak + 16), 2048, 4096, R("XA", *((XT0, BB) if v == 1 else (A1, XT1 + 4112))), "LK")
+        tt(R("NE", 1, 257), R("P2", 0, 256), R("THR"), OP.is_lt)
+        scan(R("Z"), R("P3", 256, 512), R("NE", 0, 256), 0.0, OP.add, OP.mult)
+        for e in (0, 1):
+            o = R("P1", 128 * e, 128 * e + 128)
+            mm(o, R("C16", 1 + 128 * e, 129 + 128 * e), R("IB"), True, False)
+            mm(o, R("NE", 1 + 128 * e, 129 + 128 * e), R("IAN" if v % 2 == 0 else "IA"), False, False)
+            mm(o, R("Z", 128 * e, 128 * e + 128), R("IF"), False, True)
+        scan(R("f0"), R("P4", 256, 512), R("NE", 0, 256), 0.0, OP.add, OP.mult)
+        last_tones(ak)
+        ts(R("LI"), R("P1", 0, 256), float(AW) if v % 2 == 0 else 0.0, OP.add)
+        act(R("THR"), R("NE", 0, 256), HUGE, 4 * BIG)
+        mm(R("P5", 0, 256), R("ONE", 0, 128, 1, P1), R("S8", 0, 256, 1, P1), True, False)
+        mm(R("P5", 0, 256), R("IB"), R("C16", 1, 257), False, False)
+        mm(R("P5", 0, 256), R("IG"), R("NE", 1, 257), False, False)
+        mm(R("P5", 0, 256), R("IF"), R("f0"), False, True)
+        if not last:
+            new_w()
+        if v == 0:
+            gat("a", ("LB", 4096), 0, 4096, R("T1"), "LBK")
+            late_constants_b()
+            stage("S1", "LB", 4096, FOUR)
+            stage("S1", "LA", 4096, [(4, 5), (5, 6)])
+            send(1, R("R1"), R("S1"))
+            unstage("LA", 4096, "S1", FOUR)
+        else:
+            gat("a", (lin, 0), 0, 4096, R(nxt), "LBK")
+            if v == 1:
+                stage("S0", lin, 0, FOUR + [(4, 5)])
+                send(3, R("R3"), R("S0", 0, 1280))
+        if not last:
+            act(R("WK", 1, 257), R("JW"), 1.0, 16.0 + (4096.0 if v % 2 == 0 else 0.0))
+            for k, off in ((0, 0), (1, 4096)) if v == 0 else ((2, 4096), (3, 0)):
+                arrive(k, R("R%d" % k))
+                unstage("RL", off, "R%d" % k, [(r, r) for r in range(6 - v)])
+        win = R("XA", A0, A1) if v % 2 == 0 else R("XA", BB, XT1)
+        for k in range(2):
+            tt(R("T2", 2048 * k, 2048 * k + 2048), IND(win, R("LI", 128 * k, 128 * k + 128)), R("XA", xt + 2048 * k, xt + 2048 * k + 2048), OP.not_equal)
+            lin2bars(("P2", 256), "T2", 0, R("sel", sNE, sNE + 8), (k,))
+        if v == 0:
+            late_constants_c()
+        mm(R("P7", 256, 512), R("IF"), R("J16"), True, False)
+        mm(R("P7", 256, 512), R("IB"), R("LTB"), False, True)
+        act(R("WB", 1, 257), R("P7", 256, 512))
+        scan(R("Z"), R("THR"), R("P2", 256, 512), 4 * BIG, OP.min, OP.max)
+        tt(R("f1"), R("P5", 0, 256), R("Z"), OP.add)
+        scan(R("Z"), R("RST"), R("f1"), 0.0, OP.add, OP.min)
+        spread(R("P4", 256, 512), "Z")
+        tt(R("f1"), R("P4", 256, 512), R("MK"), OP.mult)
+        act(R("f0"), R("P4", 256, 512))
+        for e in (0, 1):
+            mm(R("P6", 384 + 8 * e, 392 + 8 * e), R("f1", 128 * e, 128 * e + 128), R("PH"))
+        for e in (0, 1):
+            mm(R("P3", 128 * e, 128 * e + 128), R("f0", 128 * e, 128 * e + 128), R("IF"))
+        KM = R("P6", 384, 400)
+        cp(R("ism", 0, 16), KM)
+        ts(R("smb", 16, 32), KM, 5 * BIG, OP.is_lt)
+        ts(R("ism", 16, 32), R("ism", 0, 16), 4, OP.arith_shift_right, 511, OP.bitwise_and)
+        cp(R("smb", 0, 16), R("ism", 16, 32))
+        for y in range(16):
+            ts(R("OH", 256 * y, 256 * y + 256), R("IOC"), R("smb", y, y + 1), OP.is_equal, R("smb", 16 + y, 17 + y), OP.mult)
+            mm(R("P7", 0, 256), R("WM", 15 - y, 143 - y), R("OH", 256 * y, 256 * y + 256), y == 0, y == 15)
+        act(R("SS", 1, 257), R("P7", 0, 256))
+        cp(R("LS", 0, 16), R("ism", 16, 32))
+        ts(R("smb", 64, 80), R("smb", 16, 32), -1.0, OP.mult, 1.0, OP.add)
+        tt(R("LG"), IND(R("LTT", 0, 257), R("LS", 0, 16)), R("CB"), OP.add)
+        tt(R("VI"), IND(R("SS", 0, 257), R("LS", 0, 16)), R("THT"), OP.is_ge)
+        for x in range(16):
+            mm(R("P6", 400, 416), R("SX5", 15 - x, 143 - x), R("LG", x, 256, 16), x == 0, x == 15)
+        mm(R("P7", 256, 272), R("IB"), R("smb", 64, 80), True, False)
+        for x in range(16):
+            mm(R("P7", 256, 272), R("SX", 15 - x, 143 - x), R("VI", x, 256, 16), False, x == 15)
+        ts(R("i0"), R("P3", 0, 256), C(cM), OP.mult, C(cO), OP.add)
+        ts(R("i0"), R("i0"), 511, OP.bitwise_and)
+        tt(R("VAL"), R("i0"), R("LG"), OP.add)
+        ts(R("ism", 32, 48), R("ism", 0, 16), 15, OP.bitwise_and)
+        ts(R("ism", 48, 64), R("ism", 0, 16), 13, OP.arith_shift_right, 15, OP.bitwise_and)
+        tt(R("sm", 64, 80), R("ism", 48, 64), R("sm", 32, 48), OP.add)
+        tt(R("sm", 64, 80), R("sm", 64, 80), R("ism", 32, 48), OP.subtract)
+        tt(R("sm", 80, 96), R("P6", 400, 416), R("ism", 32, 48), OP.subtract)
+        ts(R("sm", 96, 112), R("P6", 400, 416), 8193.0, OP.add)
+        mm(R("P4", 0, 256), R("BVW"), R("VAL"))
+        ts(R("sm", 112, 128), R("P7", 256, 272), 0.0, OP.is_equal)
+        tt(R("smb", 33, 49), R("sm", 112, 128), R("sm", 80, 96), OP.mult)
+        mm(R("P6", 416, 432), R("TS"), R("smb", 33, 49), True, False)
+        mm(R("P6", 416, 432), R("TC"), R("smb", 32, 48), False, True)
+        ts(R("sm", 128, 144), R("sm", 112, 128), -16384.0, OP.mult)
+        tt(R("sm", 128, 144), R("sm", 128, 144), R("sm", 64, 80), OP.add)
+        tt(R("sm", 96, 112), R("sm", 96, 112), R("sm", 112, 128), OP.mult)
+        if not last:
+            tt(R("M2"), R("P4", 0, 256), R("CW"), OP.is_le)
+            tt(R("M2"), R("M2"), R("NW"), OP.mult)
+            mm(R("P5", 0, 256), R("TI"), R("M2"))
+            steps(0, 16)
+        scan(R("sm", 144, 160), R("P6", 416, 432), R("ZB", 0, 16), 0.0, OP.add, OP.add)
+        tt(R("sm", 160, 176), R("sm", 144, 160), R("sm", 128, 144), OP.add)
+        cp(R("LS", 16, 32), R("sm", 160, 176))
+        tt(R("sm", 176, 192), R("sm", 160, 176), R("sm", 96, 112), OP.add)
+        cp(IND(R("WE"), R("LS", 16, 32)), R("VAL"))
+        ts(R("LS", 32, 48), R("sm", 176, 192), -8192.0, OP.add)
+        cp(IND(R("WE", 8192, 24576), R("LS", 32, 48)), R("VAL"))
+        mm(R("P6", 0, 256), R("TS", 0, 128, 1, (0, 1, 1)), R("KZ", 0, 256, 1, P1), True, False)
+        for e in (0, 1):
+            for s in range(16):
+                o, a = R("P6", 128 * e + s, 128 * e + 128, 16), 2048 * e + s
+                mm(o, R("WE", a, 2048 * e + 2048, 16), R("sel", sE1, sE1 + 8), False, False)
+        if not last:
+            pos_mm(0, 8)
+        for e in (0, 1):
+            for s in range(16):
+                o, a = R("P6", 128 * e + s, 128 * e + 128, 16), 2048 * e + s
+                mm(o, R("WE", 8192 + a, 10240 + 2048 * e, 16), R("sel", sE2, sE2 + 8), False, e == 1 and s == 15)
+        tt(R("sm", 192, 208), R("ism", 16, 32), R("sm", 48, 64), OP.subtract)
+        tt(R("sm", 192, 208), R("sm", 192, 208), R("sm", 112, 128), OP.mult)
+        tt(R("sm", 192, 208), R("sm", 192, 208), R("sm", 48, 64), OP.add)
+        cp(R("LS", 48, 64), R("sm", 192, 208))
+        act(R("f1"), R("P4", 0, 256), 1.0, C(cS16))
+        cp(IND(R("WB"), R("LS", 48, 64)), R("f1"))
+        if last:
+            cp(R("i1"), R("WB", 1, 257))
+            ts(R("i2"), R("i1"), 4, OP.arith_shift_right)
+            ts(R("i1"), R("i1"), 15, OP.bitwise_and)
+            ts(R("f1"), R("i1"), C(cX), OP.is_lt, 8192.0, OP.mult)
+            tt(R("f1"), R("f1"), R("i2"), OP.add)
+            ts(R("LBK"), R("f1"), 8192.0, OP.min)
+            gat("f", ("T2", 0), 0, 4096, R(lin), "LBK")
+        scan(R("Z"), R("KP"), R("P6", 0, 256), 0.0, OP.mult, OP.add)
+        spread(R("f0"), "Z")
+        o0, o1 = R("P1", 0, 128), R("P2", 0, 128)
+        for e, o in ((0, o0), (1, o1)):
+            mm(o, R("ONE", 0, 128, 1, P1), R("B16", 128 * e, 128 * e + 128, 1, P1), True, False)
+            mm(o, R("Z", 128 * e, 128 * e + 128), R("IF"), False, False)
+        mm(o0, R("f0", 0, 128), R("UT"), False, True)
+        mm(o1, R("f0", 0, 128), R("OF"), False, False)
+        mm(o1, R("f0", 128, 256), R("UT"), False, True)
+        sl = R("SL%d" % (v % 2))
+        ts(R("SL%d" % (v % 2), 0, 128), o0, C(cS4), OP.add, 8192.0, OP.min)
+        ts(R("SL%d" % (v % 2), 128, 256), o1, C(cS4), OP.add, 8192.0, OP.min)
+        if not last:
+            send(4 + v, R("SR%d" % v), sl)
+            pos_mm(8, 16)
+            act(R("f2"), R("P0", 0, 256), 0.5, 8.0 + (0.0 if v % 2 == 0 else float(AW)))
+            cp(R("i1"), R("WB", 1, 257))
+            cp(IND(R("WK"), R("LS", 48, 64)), R("f2"))
+            cp(R("LK"), R("WK", 1, 257))
+            gat("f", ("XA", an + 16), 0, 2048, R("XA", *((XT0, BB) if v == 0 else (A1, XT1 + 4112))), "LK")
+            ts(R("i2"), R("i1"), 4, OP.arith_shift_right)
+            cp(R("LBK"), R("i2"))
+            ts(R("i1"), R("i1"), 15, OP.bitwise_and)
+            cp(R("LTB"), R("i1"))
+            act(R("LTT", 1, 257), R("LTB"), XMc(5), XMc(4))
+            k0 = len(ops)
+            fill("WE", 0, 4096, 0)
+            fill("WE", 8192, 12288, 0)
+            for op in ops[k0:]:
+                op["behind"] = "lo%d" % (4 + v)
+            arrive(4 + v, R("SR%d" % v))
+            gat("f", (nxt, 4096), 0, 4096, R("RL"), "SR%d" % v)
+            names2bars(nxt, 4096)
+            t_list(R("LT_"))
+            if v == 0:
+                stage("S1", nxt, 4096, FOUR + [(4, 5)])
+                send(2, R("R2"), R("S1", 0, 1280))
+        else:
+            gat("f", ("T1", 0), 0, 4096, R(lin), "SL0")
+            for f, w in ((0, "SXU"), (1, "SXT")):
+                for x in range(16):
+                    mm(R("P7" if f == 0 else "P5", 0, 256), R(w, 15 - x, 143 - x), R("T2", 256 * x, 256 * x + 256), x == 0, x == 15)
+            names2bars("T1", 0)
+            act(R("ZO", 0, 256), R("P7", 0, 256))
+            act(R("ZO", 256, 512), R("P5", 0, 256))
+            dma("a", [(X("zu"), R("ZO", 0, 256)), (X("zt"), R("ZO", 256, 512))])
+            ts(R("NL", 0, 512), R("P0"), -2047.0, OP.add)
+            for e in (0, 1):
+                mm(R("P1", 128 * e, 128 * e + 128), R("NL", 384 * e, 384 * e + 128), R("IH"))
+                mm(R("P1", 256 + 128 * e, 384 + 128 * e), R("NL", 128 + 128 * e, 256 + 128 * e), R("IH"))
+            ts(R("YO"), R("P1"), 2047.0, OP.add)
+            dma("s", [(X("yu"), R("YO", 0, 256)), (X("yt"), R("YO", 256, 512))])
+    return ops
+
+
+from concourse.mybir import AxisListType
+AX = AxisListType.X
+PLAN = {}
+
+
+def order(ops, lanes):
+    seen = {}
+    for n, op in enumerate(ops):
+        dep = set()
+        op["soft"] = ()
+        for isw, accs in ((False, op["rd"]), (True, op["wr"])):
+            for name, a, b, pm in accs:
+                psum = SCRATCH[name][0] == "psum"
+                for m, w2, a2, b2, pm2 in seen.get(name, []):
+                    if psum:
+                        dep.add(m)
+                        continue
+                    pad = 0 if op["grp"] is None and ops[m]["grp"] is None else 15
+                    if (isw or w2) and pm & pm2 and (a & ~pad) < ((b2 + pad) & ~pad) and (a2 & ~pad) < ((b + pad) & ~pad):
+                        if op["grp"] is None or ops[m]["grp"] != op["grp"]:
+                            dep.add(m)
+        for isw, accs in ((False, op["rd"]), (True, op["wr"])):
+            for name, a, b, pm in accs:
+                old = seen.get(name, [])
+                if SCRATCH[name][0] == "psum":
+                    old = [x for x in old if ops[x[0]]["q"] != op["q"]]
+                elif isw:
+                    old = [x for x in old if not (a <= x[2] and x[3] <= b and (x[4] & ~pm) == 0 and x[0] in dep)]
+                seen[name] = old + [(n, isw, a, b, pm)]
+        dep.discard(n)
+        op["dep"] = dep
+    members = {}
+    for n, op in enumerate(ops):
+        if op["grp"] is not None:
+            members.setdefault(op["grp"], []).append(n)
+    for op in ops:
+        for m in list(op["dep"]):
+            if ops[m]["grp"] is not None:
+                op["dep"].update(members[ops[m]["grp"]])
+        op["soft"] = set(members[op["behind"]] if "behind" in op else []) - op["dep"]
+        op["pre"] = set(op["dep"]) | set(members[op["after"]] if "after" in op else []) | op["soft"]
+
+    def delay(m, n):
+        if ops[m]["q"] == "t" and ops[n]["q"] == "t":
+            return 0.0
+        return 0.15
+    lat = [0.0 if op["grp"] is None or op["q"] == "x" else (2.0 if op["grp"][0] == "d" else 2.5) for op in ops]
+    succ = [[] for _ in ops]
+    for n, op in enumerate(ops):
+        for m in op["pre"]:
+            succ[m].append(n)
+    hard = [[(m, delay(m, n)) for m in sorted(op["pre"] - op["soft"])] for n, op in enumerate(ops)]
+    where = [sorted(op.get("alt", op["q"])) for op in ops]
+
+    def schedule(bias):
+        tail = [0.0] * len(ops)
+        for n in range(len(ops) - 1, -1, -1):
+            tail[n] = ops[n]["c"] + lat[n] + bias[n] + max([tail[k] for k in succ[n]] or [0.0]) + 0.1
+        left = [len(op["pre"]) for op in ops]
+        ready = {n: 0.0 for n in range(len(ops)) if left[n] == 0}
+        end = [0.0] * len(ops)
+        free = {q: 0.0 for q in "vatpsx"}
+        wire = {"d": 0.0, "l": 0.0, "a": 0.0}
+        seq, on, held, prev = [], {}, {}, {}
+        while ready:
+            best = None
+            for n, t0 in ready.items():
+                for q in where[n]:
+                    st = t0 if t0 > free[q] else free[q]
+                    key = st - SLACK * tail[n]
+                    if best is None or key < best[0]:
+                        best = (key, n, q, st)
+            n, q, st = best[1:]
+            op = ops[n]
+            if st > ready.pop(n) + 1e-9:
+                held[n] = prev[q]
+            on[n] = q
+            prev[q] = n
+            if op["grp"] is None:
+                end[n] = free[q] = st + op["c"]
+            else:
+                w = op["grp"][0]
+                end[n] = wire[w] = max(st + lat[n], wire[w]) + op["c"]
+                free[q] = st + (0.3 if w == "l" else 0.06)
+            seq.append(n)
+            for k in succ[n]:
+                left[k] -= 1
+                if left[k] == 0:
+                    ready[k] = max([end[m] + d for m, d in hard[k]] or [0.0])
+        return max(end), seq, on, held, end
+
+    edge = [[(m, d) for m, d in hard[n]] + [(m, None) for m in sorted(op["soft"])] for n, op in enumerate(ops)]
+    back = [[] for _ in ops]
+    for n in range(len(ops)):
+        for m, d in edge[n]:
+            back[m].append((n, d))
+    shape = []
+    for n, op in enumerate(ops):
+        w = (op["grp"] or " ")[0]
+        shape.append((lat[n], op["c"], 0.0) if w == "d" else ((0.0, 0.3, lat[n] + op["c"]) if w == "l" else (0.0, op["c"], 0.0)))
+
+    def pack(rank, edges, forward):
+        start, end, on, busy = {}, {}, {}, {}
+        for n in rank:
+            t0 = max([(end[m] + d if d is not None else (start[m] + 0.01 if forward else end[m] + 0.01 - sum(shape[n]))) for m, d in edges[n]] + [0.0])
+            x, c, y = shape[n] if forward else shape[n][::-1]
+            best = None
+            for q in (["d"] if (ops[n]["grp"] or " ")[0] == "d" else where[n]):
+                row = busy.setdefault(q, [])
+                t = t0 + x
+                k = len(row)
+                while k > 0 and row[k - 1][1] > t:
+                    k -= 1
+                while k < len(row) and row[k][0] < t + c - 1e-9:
+                    t = max(t, row[k][1])
+                    k += 1
+                if best is None or t < best[0]:
+                    best = (t, q, k)
+            t, q, k = best
+            busy[q].insert(k, (t, t + c))
+            start[n], end[n], on[n] = t - x, t + c + y, q
+        return max(end.values()), start, end, on
+
+    if "seq" not in PLAN:
+        rank = schedule([0.0] * len(ops))[1]
+        top = None
+        rnd = 1
+        for _ in range(ROUNDS):
+            span, start, end, on = pack(rank, edge, True)
+            if top is None or span < top[0]:
+                top = (span, sorted(rank, key=lambda n: (start[n], n)), on)
+                PLAN["dbg"] = (ops, dict(start), dict(end), edge, on)
+            for n in range(len(ops) - 1, -1, -1):
+                end[n] = min([end[n]] + [end[k] - 1e-6 for k, d in back[n]])
+            span, start, end, on = pack(sorted(rank, key=lambda n: (-end[n], -n)), back, False)
+            late = {}
+            for n in range(len(ops)):
+                rnd = (rnd * 1103515245 + 12345) % 2147483648
+                late[n] = max([span - end[n] + (rnd >> 8) % 100 * JITTER] + [late[m] + 1e-6 for m, d in edge[n]])
+            rank = sorted(rank, key=lambda n: (late[n], n))
+        PLAN["seq"], PLAN["on"], PLAN["span"] = top[1], top[2], top[0]
+    seq = PLAN["seq"]
+    for n, op in enumerate(ops):
+        if "alt" in op:
+            op["q"] = PLAN["on"][n]
+            op["fn"] = op["alt"][op["q"]]
+    place = {n: k for k, n in enumerate(seq)}
+    need = set()
+    done = {}
+    for n in seq:
+        op = ops[n]
+        best = {}
+        for m in op["dep"]:
+            if ops[m]["grp"] is None and ops[m]["q"] == op["q"] and op["grp"] is None and op["q"] == "t":
+                continue
+            key = ops[m]["grp"] or ops[m]["q"]
+            if key not in best or place[m] > place[best[key]]:
+                best[key] = m
+        keep = []
+        for key, m in sorted(best.items()):
+            if done.get((op["q"], key), -1) < place[m]:
+                done[(op["q"], key)] = place[m] if ops[m]["grp"] is None else len(ops)
+                keep.append((key, m))
+                need.add(m)
+        op["wait"] = keep
+    total = {}
+    for n in seq:
+        op = ops[n]
+        if op["grp"] is None:
+            if n in need:
+                total["q" + op["q"]] = total.get("q" + op["q"], 0) + 1
+                op["val"] = total["q" + op["q"]]
+        else:
+            total[op["grp"]] = total.get(op["grp"], 0) + (16 if op["grp"][0] == "d" else lanes[op["q"]][op["step"]])
+    return seq, need, total
+
+
+def rank_program(g, core, T, topo):
+    rank = T.rank_of(core)
+    if rank is None:
+        return
+    peer = {k: T.cores[(rank + k) % len(T.cores)] for k in (-2, -1, 1, 2)}
+    lanes = {"p": {k: len(topo.engines(core, c)) for k, c in peer.items()},
+             "x": {k: len(topo.engines(c, core)) for k, c in peer.items()}}
+    ops = build(T)
+    seq, need, total = order(ops, lanes)
+    queue = {"v": g.vector, "a": g.scalar, "t": g.tensor, "p": g, "s": g.sync}
+    for n in seq:
+        op = ops[n]
+        if op["q"] == "x":
+            continue
+        for key, m in op["wait"]:
+            if ops[m]["grp"] is None:
+                queue[op["q"]].wait_ge(T.sem["q" + key], ops[m]["val"])
+            else:
+                queue[op["q"]].wait_ge(T.sem[key], total[key])
+        if "send" in op:
+            k, land, src = op["send"]
+            dst = peer[op["step"]]
+            rid, pid = topo.addr(dst)[:2]
+            g.remote_dma(land, src, T.sem["ar%d" % k], T.sem["lo%d" % k], pid, rid, topo.mask(core, dst))
+        elif op["grp"] is not None:
+            op["fn"](g).then_inc(T.sem[op["grp"]], 16)
+        elif n in need:
+            op["fn"](g).then_inc(T.sem["q" + op["q"]], 1)
+        else:
+            op["fn"](g)
+    for key in sorted(total):
+        g.wait_ge(T.sem[key], total[key])

@@ -1,10 +1,13 @@
-from concourse.mybir import AluOpType as OP, ActivationFunctionType as AF
+from concourse.mybir import AluOpType as OP, ActivationFunctionType as AF, AxisListType
 
-F32, BF, F16, I32, U16 = "float32", "bfloat16", "float16", "int32", "uint16"
-SZ = {F32: 4, BF: 2, F16: 2, I32: 4, U16: 2}
+AX = AxisListType.X
+F32, BF, I32, U16 = "float32", "bfloat16", "int32", "uint16"
+SZ = {F32: 4, BF: 2, I32: 4, U16: 2}
 AW = 4128
 XT0, A0, BB, A1, XT1 = 0, 4096, 4096 + AW, 4096 + 2 * AW, 4096 + 3 * AW
-BIG, HUGE = float(2 ** 17), float(2 ** 22)
+BIG, HUGE = float(2 ** 23), float(2 ** 27)
+NONE = 4 * BIG + 15 * 2.0 ** 19 + 15 * 2.0 ** 14 + 4096
+HW = 144
 
 
 def _s(shape, dt):
@@ -12,43 +15,55 @@ def _s(shape, dt):
 
 
 SCRATCH = {
-    "TN": _s([4112], BF), "XA": _s([XT1 + 4112], BF), "T1": _s([4096], BF), "T2": _s([4096], BF),
-    "LA": _s([8208], BF), "LB": _s([8208], BF), "RL": _s([8208], BF),
-    "WE": _s([24576], BF),
-    "S0": _s([1536], BF), "S1": _s([1536], BF), "R0": _s([1536], BF), "R1": _s([1536], BF),
-    "R2": _s([1280], BF), "R3": _s([1280], BF), "B1": _s([256], BF), "B2": _s([256], BF), "i5": _s([256], I32),
+    "TN": _s([4112], BF), "XA": _s([XT1 + 4112], BF), "T1": _s([4096], BF),
+    "W": _s([16400], BF), "RL": _s([12304], BF), "WE": _s([24576], BF),
+    "S0": _s([1024], BF), "S1": _s([1536], BF), "R0": _s([512], BF), "R1": _s([1536], BF), "R2": _s([1280], BF),
+    "B0": _s([256], BF), "B1": _s([256], BF), "B2": _s([256], BF), "ID": _s([512], BF),
+    "SB": _s([256], U16), "RB": _s([256], U16),
     "SR0": _s([256], U16), "SR1": _s([256], U16), "SL0": _s([256], U16), "SL1": _s([256], U16),
     "i0": _s([256], I32), "i1": _s([256], I32), "i2": _s([256], I32), "i3": _s([256], I32), "i4": _s([256], I32),
+    "i5": _s([256], I32), "X3": _s([2, 8, 16], F32), "X4": _s([2, 8, 16], F32),
     "f0": _s([256], F32), "f1": _s([256], F32), "f2": _s([256], F32), "f3": _s([256], F32),
-    "ism": _s([64], I32), "col": _s([48], F32), "XM": _s([16], F32), "sm": _s([208], F32), "smb": _s([96], BF),
-    "ONE": _s([256], BF), "ZB": _s([16], BF), "K1": _s([256], BF), "K2": _s([256], BF), "KZ": _s([256], BF), "IO": _s([256], F32), "JW": _s([256], F32), "J16": _s([256], F32), "CW": _s([256], F32),
-    "IB": _s([128], BF), "IF": _s([128], F32), "IH": _s([128], F16), "IN": _s([128], BF), "I8": _s([128], BF),
-    "IA": _s([128], BF), "IAN": _s([128], BF), "IG": _s([128], BF), "UT": _s([128], F32),
-    "BLK": _s([128], BF), "TI": _s([128], BF), "TS": _s([128], BF), "TC": _s([128], BF), "BVW": _s([128], BF),
-    "sel": _s([72], BF), "PH": _s([8], F32), "SX": _s([144], BF), "SX5": _s([144], BF), "SXU": _s([144], BF),
-    "SXT": _s([144], BF), "WM": _s([144], BF),
-    "MK": _s([256], F32), "RST": _s([256], F32), "KP": _s([256], BF), "XS": _s([256], F32), "OF": _s([128], F32), "S8": _s([256], BF), "B16": _s([256], BF),
-    "IOC": _s([256], BF), "CB": _s([256], BF), "THT": _s([256], F32), "G8": _s([256], F32), "TM": _s([256], F32),
-    "NL": _s([528], F16), "LT_": _s([256], U16), "LU": _s([256], U16), "LI": _s([256], U16), "LK": _s([256], U16),
-    "LBK": _s([256], U16), "LS": _s([80], U16), "NQ": _s([272], BF), "NV": _s([256], BF), "NE": _s([272], BF),
-    "C16": _s([272], BF), "THR": _s([256], F32), "Z": _s([256], F32), "NW": _s([256], BF),
-    "SS": _s([264], F32), "VI": _s([256], BF),
-    "LTB": _s([256], BF), "LTT": _s([272], BF), "LG": _s([256], BF), "VAL": _s([256], BF), "M2": _s([256], BF),
-    "WK": _s([520], F32), "WB": _s([520], F32), "YO": _s([512], F32), "ZO": _s([512], F32),
+    "ism": _s([32], I32), "col": _s([48], F32), "WT": _s([8], F32), "XM": _s([16], F32), "sm": _s([160], F32),
+    "smb": _s([112], BF), "ONE": _s([256], BF), "ZR": _s([128], F32), "K1": _s([256], BF), "K2": _s([256], BF),
+    "K16": _s([128], F32), "RW": _s([1280], BF), "IO": _s([256], F32), "JW": _s([256], F32),
+    "IB": _s([128], BF), "IF": _s([128], F32), "IN": _s([128], BF), "I8": _s([128], BF), "IA": _s([128], BF),
+    "IAN": _s([128], BF), "IG": _s([128], BF), "IS": _s([128], BF), "IR": _s([128], BF), "D6": _s([128], BF),
+    "DF": _s([128], F32), "UT": _s([128], F32), "OF": _s([128], F32), "G8": _s([128], F32), "G8B": _s([256], BF),
+    "BLK": _s([128], BF), "BLS": _s([128], BF), "TI": _s([128], BF), "TS": _s([128], BF), "TC": _s([128], BF),
+    "TD": _s([128], BF), "BVW": _s([128], BF), "BST": _s([128], BF), "BL3": _s([128], BF), "NR": _s([512], BF),
+    "sel": _s([64], BF), "PH": _s([8], F32), "SX": _s([144], BF), "SXD": _s([144], BF), "SXN": _s([144], BF),
+    "SXF": _s([288], F32), "TB": _s([128], BF), "ST": _s([1024], BF), "TK": _s([256], F32), "SX3": _s([144], BF),
+    "SXU": _s([144], BF), "SXT": _s([144], BF), "WM": _s([144], BF),
+    "MK": _s([128], F32), "RST": _s([128], F32), "KP": _s([128], BF), "IOC": _s([256], BF), "THT": _s([256], F32),
+    "TM": _s([128], F32), "BASE": _s([96], F32),
+    "NT": _s([256], F32), "NU": _s([256], F32), "LT_": _s([256], U16), "LU": _s([256], U16), "LI": _s([256], U16),
+    "LK": _s([256], U16), "LS": _s([96], U16), "NQ": _s([2 * HW], BF), "NV": _s([256], BF), "NE": _s([2 * HW], BF),
+    "C16": _s([2 * HW], BF), "THR": _s([256], F32), "Z": _s([256], F32), "Z2": _s([2 * HW], F32), "NW": _s([256], BF),
+    "SS": _s([264], F32), "VI": _s([256], BF), "LTT": _s([520], BF), "LG": _s([256], BF), "VAL": _s([256], BF),
+    "S5": _s([256], BF), "M2": _s([256], BF), "NC": _s([256], BF), "NRC": _s([256], BF),
+    "WK": _s([520], F32), "YO": _s([512], F32), "ZO": _s([512], F32),
 }
 for _k in range(8):
     SCRATCH["P%d" % _k] = ("psum", [128, 512], F32)
-SEMAPHORES = ["qv", "qa", "qt", "qp"] + ["d%d" % _k for _k in range(40)] + ["ar%d" % _k for _k in range(8)] + ["lo%d" % _k for _k in range(8)]
+SEMAPHORES = (["qv", "qa", "qt", "qp"] + ["d%d" % _k for _k in range(40)] + ["ar%d" % _k for _k in range(10)]
+              + ["lo%d" % _k for _k in range(10)])
 ALLP = (1 << 128) - 1
-CY, PE, CHUNK, SLACK, ROUNDS = 1.04e-3, 0.53e-3, 512, 0.01, 40
-JITTER = 0.0
+CY, PE, ROUNDS = 1.04e-3, 0.53e-3, 2500
+BEGIN = (12.3, 52.0, 90.0)
+SIGNS = ((), (), ())
+HELP = ((), (1, 2, 3, 6, 7), (1, 2, 3, 6, 7))
+ALIAS = {"T2": ("WE", 4096, 4096), "PT": ("W", 12288, 4112), "OH": ("T1", 0, 4096)}
 
 
 def build(T):
     ops = []
+    due = [None]
 
     def R(name, a=0, b=None, st=1, p=None):
-        name = "T1" if name == "OH" else name
+        if name in ALIAS:
+            name, off, size = ALIAS[name]
+            a, b = a + off, (size if b is None else b) + off
         shp, dt = SCRATCH[name][1], SCRATCH[name][2]
         if b is None:
             b = shp[1]
@@ -61,8 +76,13 @@ def build(T):
         return {"ap": ap, "acc": [(name, a * SZ[dt], b * SZ[dt], pm)], "off": [], "n": len(range(a, b, st)), "w": SZ[dt],
                 "ps": SCRATCH[name][0] == "psum", "rows": bin(pm).count("1")}
 
-    def X(name):
-        return {"ap": T[name][:], "acc": [], "off": [], "n": 0, "w": 4, "ps": False, "rows": 0}
+    def Q(name, B=None):
+        acc = [(name, 0, 1024, ALLP)] if B is None else [(name, 512 * h + 64 * B, 512 * h + 64 * B + 64, ALLP) for h in (0, 1)]
+        return {"ap": T[name][:] if B is None else T[name][:, :, B, :], "acc": acc, "off": [], "n": 256 if B is None else 32,
+                "w": 4, "ps": False, "rows": 128}
+
+    def X(name, h=None):
+        return {"ap": T[name][:] if h is None else T[name][h:8:2, :], "acc": [], "off": [], "n": 0, "w": 4, "ps": False, "rows": 0}
 
     def IND(win, off):
         return {"ap": win["ap"].indirect(off["ap"]), "acc": win["acc"], "off": off["acc"], "n": 16 * off["n"], "w": win["w"], "ps": False}
@@ -78,23 +98,23 @@ def build(T):
         o = outs[0]
         n = o["n"]
         if grp is not None:
-            c = max(x["n"] * x["w"] * x["rows"] for x in [o] + views) / 200e3
+            c = max(x["n"] * x["w"] * x["rows"] for x in [o] + views) / DMA
         elif q == "t":
             c = max(64, views[1]["n"]) * PE * (4 if views[0]["w"] == 4 else 1)
         elif q == "p":
-            c = 0.15 + 2 * n * CY
+            c = 0.17 + 2 * n * CY
         elif o["off"]:
-            c = 0.05 + 3.5 * n * CY
+            c = 0.06 + 3.8 * n * CY
         elif views and views[0]["off"]:
-            c = 0.06 + 1.56 * n * CY
+            c = 0.07 + 1.56 * n * CY
         elif q == "a":
             c = 0.1 + max(64, n) * CY
         else:
-            f = 0.5 if all(x["w"] == 2 for x in [o] + views) else 1.0
+            f = 0.5 if all(x["w"] == 2 for x in [o] + views if x["n"] > 1) else 1.0
             if both and not (views[0]["ps"] or views[1]["ps"]):
                 f *= 2
             c = 0.03 + max(64, n * f) * CY
-        ops.append({"q": q, "fn": fn, "rd": rd, "wr": wr, "grp": grp, "c": c})
+        ops.append({"q": q, "fn": fn, "rd": rd, "wr": wr, "grp": grp, "c": c, "due": due[0]})
 
     def u(x):
         return x["ap"] if isinstance(x, dict) else x
@@ -114,6 +134,9 @@ def build(T):
     def ms(o, c):
         add("v", lambda g: g.vector.memset(u(o), c), [o], [])
 
+    def turn(o, i):
+        add("v", lambda g: g.vector.transpose(u(o), u(i)), [o], [i])
+
     def scan(o, d0, d1, init, op0, op1):
         add("v", lambda g: g.vector.tensor_tensor_scan(u(o), u(d0), u(d1), init, op0, op1), [o], [d0, d1])
 
@@ -121,8 +144,41 @@ def build(T):
         f = fn if fn is not None else (AF.Copy if (not isinstance(bias, dict) and bias == 0.0) else AF.Identity)
         add("a", lambda g: g.scalar.activation(u(o), u(i), f, u(bias), u(scale)), [o], [i, scale, bias])
 
+    def either():
+        a = ops.pop()
+        v = ops[-1]
+        v["alt"] = {"v": v["fn"], "a": a["fn"]}
+        v["cq"] = {"v": v["c"], "a": a["c"]}
+        v["rd"] = v["rd"] + [x for x in a["rd"] if x not in v["rd"]]
+
+    def on(q):
+        if q:
+            ops[-1]["first"] = q
+
+    def copy(o, i, bias=0.0):
+        if bias == 0.0:
+            cp(o, i)
+        else:
+            ts(o, i, bias, OP.add)
+        act(o, i, 1.0, bias)
+        either()
+
+    def relu(o, i, bias):
+        ts(o, i, bias, OP.add, 0.0, OP.max)
+        act(o, i, 1.0, bias, AF.Relu)
+        either()
+
+    def relu2(o, i):
+        ts(o, i, -2.0, OP.mult, 0.0, OP.max)
+        act(o, i, -2.0, 0.0, AF.Relu)
+        either()
+
     def mm(o, l, r, st=True, sp=True):
         add("t", lambda g: g.tensor.matmul(u(o), u(l), u(r), st, sp), [o], [l, r])
+
+    def mms(o, pairs):
+        for k, (l, r) in enumerate(pairs):
+            mm(o, l, r, k == 0, k == len(pairs) - 1)
 
     def iota(o, pat, base=0, cm=0, integer=False):
         if integer:
@@ -143,10 +199,11 @@ def build(T):
                 add("s", lambda g, o=o, i=i: g.sync.dma_start(u(o), u(i)), [o], [i], "d%d" % k)
             else:
                 add("a", lambda g, o=o, i=i: g.scalar.dma_start(u(o), u(i)), [o], [i], "d%d" % k)
+        return "d%d" % k
 
     def send(k, land, src, step=1):
         ops.append({"q": "p", "send": (k, u(land), u(src)), "step": step, "rd": src["acc"], "wr": [], "grp": "lo%d" % k,
-                    "c": src["n"] * src["w"] * 128 / 60e3})
+                    "c": src["n"] * src["w"] * 128 / LINK})
 
     def arrive(k, land, step=1):
         ops.append({"q": "x", "step": -step, "rd": [], "wr": land["acc"], "grp": "ar%d" % k, "c": 0.0, "after": "lo%d" % k})
@@ -157,487 +214,563 @@ def build(T):
     def XMc(k):
         return R("XM", k, k + 1)
 
-    def rows(name, r, a, b):
-        return R(name, a, b, 1, (r, 128, 16))
+    def rows(name, r, a):
+        return R(name, a, a + 4096, 1, (r, 128, 16))
 
-    P8 = (0, 8, 1)
-    P1 = (0, 1, 1)
-    cX, cG, cU, cT, cE1, cE2, cBV, cM, cO, cINV, cPW, cN, cTH, cA, cB_, cS4, cS16, cC = range(18)
-    sSC, sNE, sC, sN, sE1, sE2 = 0, 8, 16, 24, 48, 56
+    def stage(dst, src, off, which):
+        return [(R(dst, 256 * k, 256 * k + 256), rows(src, r, off)) for k, r in which]
 
-    dma("s", [(R("i4"), X("bk"))])
-    dma("s", [(R("i2"), X("bt"))])
+    def unstage(dst, off, src, which):
+        return [(rows(dst, r, off), R(src, 256 * k, 256 * k + 256)) for k, r in which]
+
+    def unstage2(dst, off, src, which):
+        return [(R(dst, off, off + 4096, 1, (16 * h + r, 128, 32)), R(src, 256 * k + 128 * h, 256 * k + 128 * h + 128))
+                for k, r in which for h in (0, 1)]
+
+    def gat(dst, k, win, lst, q=None):
+        copy(R(dst[0], dst[1] + 512 * k, dst[1] + 512 * k + 512), IND(win, R(lst, 32 * k, 32 * k + 32)))
+        on(q)
+
+    def fill(name, a, b, c):
+        for a0 in range(a, b, 512):
+            iota(R(name, a0, min(b, a0 + 512)), [[0, min(b, a0 + 512) - a0]], c, 0)
+
+    def spread(name, a, b, c):
+        fill(name, a, a + 512, c)
+        dma("s", [(R(name, a0, min(b, a0 + 512)), R(name, a, a + min(512, b - a0))) for a0 in range(a + 512, b, 512)])
+
+    def diag(name, w):
+        asel(R(name), R("ZR"), [[-1, 128]], OP.not_equal, w, 0, 1)
+
+    def behind(k0, grp):
+        for op in ops[k0:]:
+            op["behind"] = grp
+
+    P1, P8, P16 = (0, 1, 1), (0, 8, 1), (0, 16, 1)
+    cX, cG, cINV, cPW, cN, cTH, cA, cNX, c4X, cN0, cB56, c256 = range(12)
+    E1 = {0: 16, 1: 1, 2: 4096, 4: -16, 5: -1, 6: 1, 7: -64}
+    cW = {n: 16 + k for k, n in enumerate(("E1", "SC", "B0", "U", "T", "C", "M56", "E2", "A", "R3"))}
+    cB1, cB2, cR2, cD6, cST = range(28, 33)
+    sSC, sC, sN, sNE, sE1, sE2 = 0, 8, 16, 32, 40, 48
+    rONE, r64, r256, rS8, rB16, rIO, rX0, rX4 = 0, 128, 256, 384, 512, 768, 1024, 1152
+
+    def row(k, a=0, n=128):
+        return R("RW", k + a, k + a + n, 1, P1)
+
+    def H(name, e, a=0, n=128):
+        w = HW if SCRATCH[name][1][1] == 2 * HW else 128
+        return R(name, w * e + a, w * e + a + n)
+
+    def PA(e, k, n=1):
+        return R("P%d" % e, 128 * k, 128 * (k + n))
+
+    def PB(e, k):
+        return R("P%d" % (2 + e), 128 * k, 128 * k + 128)
+
+    def PC(e, k):
+        return R("P%d" % (4 + e), 128 * k, 128 * k + 128)
+
+    def lin2bars(ps, src, base, sel, n=1):
+        name, a = ps["acc"][0][0], ps["acc"][0][1] // 4
+        for s in range(16):
+            mm(R(name, a + s, a + 128 * n, 16), R(src, base + s, base + 2048, 16), R("sel", sel, sel + 8 * n))
+
+    def to_offers(o, w, src, more=()):
+        mms(o, [(R(w, 15 - x, 143 - x), R(src, x, 256, 16)) for x in range(16)] + list(more))
+
+    def positions(e, t0):
+        ps = R("P3", 256 * e, 256 * e + 128)
+        mm(ps, row(rONE), row(rB16, 128 * e), True, False)
+        mm(ps, R("SXN", 15, 143), H("NC", e), False, False)
+        for k in range(1, 17):
+            o = R("ST", 128 * (k % 8), 128 * (k % 8) + 128)
+            due[0] = t0 + 0.15 * k
+            relu(o, H("NC", e), -float(k))
+            due[0] = None
+            mm(ps, R("SXD", 16 - k, 144 - k) if k < 16 else R("SX", 0, 128), o, False, k == 16)
+
+    def last_tones(aoff):
+        copy(R("S5"), IND(R("XA", aoff, aoff + AW), R("LS", 64, 80)))
+        cp(IND(R("XA", BB, BB + AW), R("LS", 64, 80)), R("S5"))
+
+    def dig(dst, k, s):
+        (cp if s["acc"][0][0][0] == "i" else copy)(R(dst, 512 * k, 512 * k + 256), s)
+        tt(R(dst, 512 * k + 256, 512 * k + 512), s, R(dst, 512 * k, 512 * k + 256), OP.subtract)
+
+    g0 = dma("s", [(R("i2", 128 * h, 128 * h + 128), X("bt", h)) for h in (0, 1)])
     dma("a", [(R("ism", 0, 1, 1, P8), X("pn")), (R("ism", 4, 5, 1, P8), X("th")), (R("i5", 0, 256, 1, P8), X("bl"))])
-    dma("s", [(R("i0"), X("pt")), (R("i1"), X("pu"))])
-    dma("s", [(R("TN", 16, 4112), X("tones"))])
-    dma("s", [(R("i3"), X("bu"))])
-    for k in (1, 3, 4, 5):
-        for op in ops:
-            if op["grp"] == "d%d" % k:
-                op["behind"] = "d%d" % {1: 0, 3: 1, 4: 3, 5: 4}[k]
+    for pairs in ([(R("i4"), X("bk"))], [(R("i0"), X("pt")), (R("i1"), X("pu"))], [(R("TN", 16, 4112), X("tones"))],
+                  [(R("i3", 128 * h, 128 * h + 128), X("bu", h)) for h in (0, 1)]):
+        k0 = len(ops)
+        g1 = dma("s", pairs)
+        behind(k0, g0)
+        g0 = g1
+    ms(R("PT", 0, 2064), 0.0)
+    act(R("PT", 2064, 4112), R("PT", 0, 2048))
+    ms(R("ONE"), 1.0)
+    ms(R("ZR"), 0.0)
+    ms(R("OF"), 1.0)
+    ms(R("TN", 0, 16), 0.0)
     iota(R("ism", 8, 9), [[0, 1]], 0, 1, True)
     iota(R("IO"), [[1, 256]])
-    ms(R("ONE"), 1.0)
-    ms(R("LB", 0, 4112), 0.0)
-    asel(R("IB"), R("ONE", 0, 128), [[-1, 128]], OP.is_equal, 0.0, 0, 1)
-    iota(R("G8", 0, 256, 1, P8), [[0, 2], [1, 8], [0, 16]], 0, -1)
     ts(R("ism", 9, 10), R("ism", 8, 9), 15, OP.bitwise_and)
     ts(R("ism", 10, 11), R("ism", 8, 9), 4, OP.arith_shift_right)
     cp(R("col", cX, cX + 2), R("ism", 9, 11))
     ts(R("XM"), R("IO", 0, 16), C(cX), OP.is_equal)
     ts(R("PH"), R("IO", 0, 8), C(cG), OP.is_equal)
-    ts(R("G8", 0, 256, 1, P8), R("G8", 0, 256, 1, P8), 0.0, OP.is_equal)
-    act(R("IF"), R("IB"))
     act(R("JW"), R("IO"), 16.0, C(cX))
-    act(C(cU), XMc(0), 1.0, XMc(1))
-    act(C(cT), XMc(2), 1.0, XMc(3))
-    act(R("sel", sN, sN + 8), R("PH"), C(cU))
-    act(R("sel", sN + 8, sN + 16), R("PH"), C(cT))
-    act(R("sel", sN + 16, sN + 24), R("PH"), C(cU))
-    cp(R("IH"), R("IB"))
-
-    def dig(dst, k, s, first):
-        first(R(dst, 512 * k, 512 * k + 256), s)
-        tt(R(dst, 512 * k + 256, 512 * k + 512), s, R(dst, 512 * k, 512 * k + 256), OP.subtract)
-
-    def stage(dst, src, off, which):
-        dma("s", [(R(dst, 256 * k, 256 * k + 256), rows(src, r, off, off + 4096)) for k, r in which])
-
-    def unstage(dst, off, src, which, q="s"):
-        dma(q, [(rows(dst, r, off, off + 4096), R(src, 256 * k, 256 * k + 256)) for k, r in which])
-
-    FOUR = [(r, r) for r in range(4)]
-    ts(R("LG"), R("i4"), 1.0, OP.add)
-    send(6, R("B1"), R("LG"), -1)
-    send(7, R("B2"), R("LG"), -2)
-    dig("S0", 1, R("i2"), cp)
-    unstage("LB", 0, "S0", FOUR[2:], "a")
-    dig("S0", 0, R("i3"), cp)
-    ms(R("TN", 0, 16), 0.0)
-    cp(R("sm", 0, 8, 4, P8), R("ism", 0, 8, 4, P8))
-    mm(R("P6", 400, 402), R("G8", 0, 128, 1, P8), R("sm", 0, 8, 4, P8))
-    ts(R("f2"), R("JW"), R("P6", 400, 401), OP.is_lt)
-    ts(R("f0"), R("i0"), 1.0, OP.add)
-    tt(R("f0"), R("f0"), R("f2"), OP.mult)
-    ts(R("LT_"), R("f0"), 15.0, OP.add)
-    ts(R("f1"), R("i1"), 1.0, OP.add)
-    tt(R("f1"), R("f1"), R("f2"), OP.mult)
-    ts(R("LU"), R("f1"), 15.0, OP.add)
+    act(C(cINV), XMc(0), -1.0)
+    act(C(cA), XMc(2), -1.0, C(cINV))
+    act(R("PT", 0, 16), R("ONE", 0, 16), C(cA))
+    act(C(c256), C(cX), 256.0)
+    iota(R("ID", 0, 256), [[16, 16], [0, 16]])
+    act(R("ID", 0, 256), R("ID", 0, 256), 1.0, C(c256))
+    iota(R("ID", 256, 512), [[0, 16], [1, 16]])
+    diag("IF", 1.0)
+    diag("IB", 1.0)
+    asel(R("DF"), R("IF"), [[-1, 128]], OP.not_equal, -1.0, 1, 1)
+    asel(R("DF"), R("DF"), [[-16, 8], [1000, 16]], OP.not_equal, 0.0, 1, 1)
+    asel(R("G8", 0, 128, 1, P8), R("OF", 0, 128, 1, P8), [[1, 8], [0, 16]], OP.is_equal, 0.0, 0, -1)
+    asel(R("BLK"), R("ONE", 0, 128), [[-16, 8], [0, 16]], OP.is_ge, 0.0, 0, 1)
+    asel(R("BLK"), R("BLK"), [[16, 8], [0, 16]], OP.is_ge, 0.0, 15, -1)
+    act(R("BLS"), R("BLK"), -1.0 / 8192)
+    asel(R("TI"), R("BLS"), [[1, 128]], OP.is_ge, 0.0, 0, -1)
+    act(C(cPW), C(cG), 16.0, 15.0)
+    ts(R("SXF", 0, 144), R("IO", 0, 144), C(cPW), OP.is_equal)
+    tt(R("SXF", 145, 288), R("SXF", 1, 144), R("SXF", 0, 143), OP.subtract)
+    act(R("SX"), R("SXF", 0, 144))
+    act(R("SXD", 1, 144), R("SXF", 145, 288))
+    act(R("TB"), R("TI"), 2.0 ** 26)
+    asel(R("TB"), R("TB"), [[-1, 128]], OP.not_equal, 2.0 ** 20 - 8192, 0, 1)
+    for k, c in ((rONE, 1.0), (r64, 64.0), (r256, 256.0)):
+        ms(row(k), c)
+    iota(row(rS8), [[0, 8], [8192, 16]])
+    act(row(rB16, 0, 256), R("IO", 0, 256, 1, P1), 16.0)
+    act(row(rIO, 0, 256), R("IO", 0, 256, 1, P1))
+    asel(row(rX0), row(rONE), [[0, 8], [1, 16]], OP.is_equal, 0.0, 0, 0)
+    asel(row(rX4), row(rONE), [[0, 8], [1, 16]], OP.is_equal, 0.0, -4, 0)
+    asel(R("K16", 0, 128, 1, P16), R("OF", 0, 128, 1, P16), [[0, 8], [1, 16]], OP.is_equal, 0.0, 0, -1)
+    ms(R("WT", 0, 3, 1, P16), 0.0)
+    asel(R("WT", 1, 2, 1, P16), R("OF", 0, 1, 1, P16), [[0, 1]], OP.is_ge, 0.0, 4, -1)
+    for k, ws in enumerate((E1, {5: 2.0 ** -19, 6: 2.0 ** -14}, {5: 64, 6: 2176, 7: 64, 8: 1})):
+        for r, w in ws.items():
+            asel(R("WT", k, k + 1, 1, P16), R("WT", k, k + 1, 1, P16), [[0, 1]], OP.not_equal, float(w), -r, 1)
+    mm(R("P7", 0, 3), R("K16", 0, 128, 1, P16), R("WT", 0, 3, 1, P16))
+    act(R("col", 16, 19), R("P7", 0, 3))
+    for n, r, w, b in (("U", 1, 1.0, 0), ("T", 3, 1.0, 2), ("M56", 6, 1.0, 5), ("A", 6, -1.0, 5), ("R3", 8, -128.0, 6)):
+        act(C(cW[n]), XMc(r), w, XMc(b))
+    act(C(cW["C"]), XMc(4), 16.0)
+    act(C(cW["E2"]), C(cW["E1"]), -1.0, C(cW["R3"]))
+    act(C(cW["E2"]), XMc(3), -1.0, C(cW["E2"]))
     act(R("sel", sSC, sSC + 8), R("PH"))
-    act(C(cC), XMc(4), 16.0)
-    act(R("sel", sC, sC + 8), R("PH"), C(cC))
-    act(R("IN"), R("IB"), -1.0)
-    act(R("I8"), R("IB"), -8192.0)
-    act(R("col", cTH, cTH + 1, 1, P8), R("sm", 4, 5, 1, P8), 1.0, 8192.0)
-    act(R("TM", 0, 256, 1, P8), R("G8", 0, 256, 1, P8), R("col", cTH, cTH + 1, 1, P8))
-    asel(R("TM", 0, 256, 1, P8), R("TM", 0, 256, 1, P8), [[0, 16], [1, 16]], OP.not_equal, -4096.0, -15, 0)
-    iota(R("f3", 0, 128), [[1, 8], [0, 16]])
-    ts(R("BLK"), R("f3", 0, 128), C(cG), OP.is_equal)
-    asel(R("TI"), R("BLK"), [[1, 128]], OP.is_ge, 0.0, 0, -1)
-    iota(R("B16"), [[16, 256]])
-    act(C(cA), C(cG), 16.0, 15.0)
-    ts(R("SX"), R("IO", 0, 144), C(cA), OP.is_equal)
-    ms(R("NQ", 0, 1), 1.0)
-    ms(R("NE", 0, 1), 0.0)
-    ms(R("C16", 0, 1), 0.0)
-    ms(R("OF"), 1.0)
-
-    def spread(dst, src):
-        cp(R("XS", 0, 256, 16), R(src, 15, 256, 16))
-        scan(dst, R("KP"), R("XS"), 0.0, OP.mult, OP.add)
-
-    def lin2bars(ps, src, base, sel, es=(0, 1)):
-        for e in es:
-            for s in range(16):
-                mm(R(ps[0], ps[1] + 128 * e + s, ps[1] + 128 * e + 128, 16), R(src, base + 2048 * e + s, base + 2048 * e + 2048, 16), sel)
-
-    def names2bars(src, base):
-        for e in (0, 1):
-            for s in range(16):
-                mm(R("P0", 256 * e + s, 256 * e + 256, 16), R(src, base + 2048 * e + s, base + 2048 * e + 2048, 16), R("sel", sN + 8 * e, sN + 8 * e + 16))
-
-    def t_list(dst):
-        ts(R("NL", 128, 384), R("P0", 128, 384), -2047.0, OP.add)
-        for e in (0, 1):
-            mm(R("P1", 128 * e, 128 * e + 128), R("NL", 128 + 128 * e, 256 + 128 * e), R("IH"))
-        ts(dst, R("P1", 0, 256), 2063.0, OP.add)
-
-    def u_bars():
-        ts(R("NL", 0, 128), R("P0", 0, 128), -2047.0, OP.add)
-        ts(R("NL", 384, 512), R("P0", 384, 512), -2047.0, OP.add)
-
-    def new_flags():
-        tt(R("NQ", 1, 256), R("NL", 128, 383), R("NL", 129, 384), OP.not_equal)
-        ms(R("NQ", 16, 257, 16), 1.0)
-
-    def new_w():
-        for e in (0, 1):
-            mm(R("P5", 256 + 128 * e, 384 + 128 * e), R("NQ", 128 * e, 128 * e + 128), R("IB"))
-        act(R("NW"), R("P5", 256, 512))
-
-    def steps(k0, k1):
-        for k in range(k0, k1):
-            act(R("OH", 256 * k, 256 * k + 256), R("P5", 0, 256), -1.0, k + 0.5, AF.Sign)
-
-    def pos_mm(k0, k1):
-        if k0 == 0:
-            mm(R("P0", 0, 256), R("ONE", 0, 128, 1, P1), R("B16", 0, 256, 1, P1), True, False)
-            mm(R("P0", 0, 256), R("ONE", 0, 128, 1, P1), R("B16", 0, 256, 1, P1), False, False)
-        for k in range(k0, k1):
-            mm(R("P0", 0, 256), R("SX", 15 - k, 143 - k), R("OH", 256 * k, 256 * k + 256), False, k == 15)
-
-    def gat(q, dst, a, b, win, lst):
-        for a0 in range(a, b, CHUNK):
-            b0 = min(b, a0 + CHUNK)
-            o, i = R(dst[0], dst[1] + a0, dst[1] + b0), IND(win, R(lst, a0 // 16, b0 // 16))
-            if q == "a":
-                act(o, i)
-            else:
-                cp(o, i)
-                if q == "f":
-                    act(o, i)
-                    other = ops.pop()
-                    ops[-1]["alt"] = {"v": ops[-1]["fn"], "a": other["fn"]}
-
-    def fill(name, a, b, c):
-        for a0 in range(a, b, 1024):
-            iota(R(name, a0, min(b, a0 + 1024)), [[0, min(b, a0 + 1024) - a0]], c, 0)
-
-    def last_tones(aoff):
-        act(R("M2"), IND(R("XA", aoff, aoff + AW), R("LS", 64, 80)))
-        cp(IND(R("XA", BB, BB + AW), R("LS", 64, 80)), R("M2"))
-
-    names2bars("LB", 0)
+    act(R("sel", sC, sC + 8), R("PH"), C(cW["C"]))
+    for n, w in (("IN", -1.0), ("I8", -8192.0), ("IAN", -float(AW)), ("IG", HUGE), ("IS", 2.0 ** -19), ("IR", -2.0 ** -14), ("IA", float(AW))):
+        diag(n, w)
+    for n in ("NQ", "NE", "C16", "NV", "Z2", "LTT"):
+        ms(R(n), 0.0)
+    ts(R("B0"), R("i4"), 1.0, OP.add)
+    send(6, R("B1"), R("B0"), -1)
+    send(7, R("B2"), R("B0"), -2)
+    ts(Q("X3"), R("i2"), 16.0, OP.add)
+    for B in range(8):
+        turn(R("f3", B, 256, 8), Q("X3", B))
+    cp(R("SB"), R("f3"))
+    send(0, R("RB"), R("SB"))
+    due[0] = 12.0
+    dig("S0", 0, R("i3"))
+    due[0] = None
+    send(1, R("R0"), R("S0", 0, 512))
+    due[0] = 5.0
+    mm(R("P5", 0, 256), R("DF"), R("f3"))
+    ts(R("NW"), R("P5", 0, 256), 0.0, OP.not_equal)
+    mms(R("P5", 256, 512), [(R("IF"), R("f3")), (R("TB"), R("NW"))])
+    copy(R("NU"), R("P5", 256, 512), -2.0 ** 20)
+    for k in range(16):
+        o = R(("YO", "ZO")[k % 4 // 2], 256 * (k % 2), 256 * (k % 2) + 256)
+        due[0] = 7.0 + 0.6 * k
+        relu(o, R("NU"), 8192.0 * (k + 1))
+        due[0] = None
+        mm(R("P4", 0, 256), R("SXF", 159 - k, 287 - k) if k < 15 else R("SXF", 0, 128), o, k == 0, k == 15)
+    act(C(cB56), C(cX), -8192.0)
+    ts(R("LK"), R("P4", 0, 256), C(cB56), OP.add, 4111.0, OP.min)
+    act(R("G8B", 0, 128, 1, P8), R("G8", 0, 128, 1, P8))
+    asel(R("G8B", 128, 256, 1, P8), R("G8B", 0, 128, 1, P8), [[0, 8], [1, 16]], OP.is_equal, 0.0, -3, 0)
+    cp(R("M2", 0, 256, 1, P8), R("i5", 0, 256, 1, P8))
+    mm(R("P6", 256, 512), R("G8B", 0, 128, 1, P8), R("M2", 0, 256, 1, P8))
+    ts(R("VI"), R("P6", 256, 512), C(cX), OP.is_gt)
+    tt(R("VI"), R("VI"), R("NW"), OP.mult)
+    act(C(cN0), C(cX), 16.0)
+    act(R("BASE", 0, 16), R("IO", 0, 16), 256.0, C(cN0))
+    act(R("BASE", 16, 32), R("BASE", 0, 16), 1.0, 15.0)
+    to_offers(R("P6", 16, 32), "SX", "VI")
+    tt(R("sm", 0, 16), R("P6", 16, 32), R("BASE", 16, 32), OP.add)
+    cp(R("LS", 64, 80), R("sm", 0, 16))
+    mms(R("P7", 256, 512), [(R("G8B", 128, 256, 1, P8), R("M2", 0, 256, 1, P8)), (row(rX0), row(rIO, 0, 256))])
+    act(C(cNX), XMc(3), -1.0)
+    act(R("LTT", 1, 257), R("P7", 256, 512), 1.0, C(cNX))
+    act(C(cNX), C(cX), -1.0)
+    spread("XA", BB - 16, BB + AW + 16, 99)
+    for a in (A0, XT1 - 16, XT1 + 4096):
+        iota(R("XA", a, a + 16), [[0, 16]], 99, 0)
+    due[0] = 3.0
+    cp(R("sm", 16, 24, 4, P8), R("ism", 0, 8, 4, P8))
+    mm(R("P2", 0, 2), R("G8", 0, 128, 1, P8), R("sm", 16, 24, 4, P8))
+    act(C(cN), R("P2", 0, 1), 8192.0, -4097.0)
+    act(R("f2"), R("JW"), -8192.0, C(cN))
+    tt(R("f0"), R("i0"), R("f2"), OP.min)
+    ts(R("LT_"), R("f0"), -1.0, OP.max, 16.0, OP.add)
+    tt(R("f1"), R("i1"), R("f2"), OP.min)
+    ts(R("LU"), R("f1"), -1.0, OP.max, 16.0, OP.add)
+    due[0] = 9.0
+    ts(R("f1"), R("f1"), -1.0, OP.max)
+    for B in range(8):
+        turn(Q("X4", B), R("f1", B, 256, 8))
+    dig("S1", 0, Q("X4"))
+    due[0] = None
+    act(R("col", cTH, cTH + 1, 1, P8), R("sm", 20, 21, 1, P8), 1.0, 8192.0)
+    act(R("TM", 0, 128, 1, P8), R("G8", 0, 128, 1, P8), R("col", cTH, cTH + 1, 1, P8))
+    asel(R("TM", 0, 128, 1, P8), R("TM", 0, 128, 1, P8), [[0, 8], [1, 16]], OP.not_equal, -4096.0, -15, 0)
+    dma("s", unstage("PT", 16, "ID", [(0, 2), (1, 3)]) + unstage("PT", 16, "B0", [(0, 4)]))
     arrive(6, R("B1"), -1)
     arrive(7, R("B2"), -2)
-    dma("s", [(rows("LB", 4 + k, 16, 4112), R(n)) for k, n in enumerate(("LG", "B1", "B2"))])
-    t_list(R("SL1"))
-    gat("f", ("XA", XT1), 0, 4096, R("TN"), "SL1")
-    new_flags()
-    new_w()
-    mm(R("P5", 0, 256), R("TI"), R("NW"))
-    cp(R("THR", 0, 256, 1, P8), R("i5", 0, 256, 1, P8))
-    mm(R("P7", 0, 256), R("G8", 0, 128, 1, P8), R("THR", 0, 256, 1, P8))
-    act(R("LTB"), R("P7", 0, 256), 1.0, -1.0)
-    act(R("M2"), R("P5", 0, 256))
-    for k in range(16):
-        ts(R("OH", 256 * k, 256 * k + 256), R("M2"), k + 0.5, OP.is_lt, 2.0, OP.mult)
-    pos_mm(0, 16)
-    ts(R("LK"), R("P0", 0, 256), 0.5, OP.mult)
-    ts(R("VI"), R("LTB"), C(cX), OP.is_ge)
-    tt(R("VI"), R("VI"), R("NW"), OP.mult)
-    for x in range(16):
-        mm(R("P6", 416, 432), R("SX", 15 - x, 143 - x), R("VI", x, 256, 16), x == 0, x == 15)
-    act(C(cB_), C(cX), 16.0, 15.0)
-    act(R("sm", 16, 32), R("IO", 0, 16), 256.0, C(cB_))
-    tt(R("sm", 16, 32), R("sm", 16, 32), R("P6", 416, 432), OP.add)
-    cp(R("LS", 64, 80), R("sm", 16, 32))
-    fill("XA", BB - 16, BB + AW + 16, 99)
-    iota(R("XA", A0, A0 + 16), [[0, 16]], 99, 0)
-    iota(R("XA", XT1 - 16, XT1), [[0, 16]], 99, 0)
-    iota(R("XA", XT1 + 4096, XT1 + 4112), [[0, 16]], 99, 0)
-    for e in (0, 1):
-        mm(R("P1", 128 * e, 128 * e + 128), R("f0", 128 * e, 128 * e + 128), R("IF"))
-    ts(R("NL", 128, 384), R("P1", 0, 256), -2048.0, OP.add)
-    ms(R("NL", 384, 400), 0.0)
+    dma("s", unstage("PT", 16, "B1", [(0, 5)]) + unstage("PT", 16, "B2", [(0, 6)]))
+    dma("s", [(R("RL", 4096, 8192), R("TN", 16, 4112))])
+    dma("s", [(R("RL", 8192, 12288), R("TN", 16, 4112))])
 
-    def late_constants_a():
+    def late_constants():
         act(R("sel", sNE, sNE + 8), R("PH"), BIG)
-        act(R("IA"), R("IB"), float(AW))
-        act(R("IAN"), R("IB"), -float(AW))
-        act(R("IG"), R("IB"), HUGE)
-        iota(R("S8"), [[0, 16], [8192, 16]])
-        iota(R("MK"), [[0, 16], [1, 16]])
-        iota(R("IOC"), [[1, 256]], 1)
-        asel(R("UT"), R("OF"), [[1, 128]], OP.is_gt, 0.0, 0, -1)
-        asel(R("TS"), R("BLK"), [[1, 128]], OP.is_gt, 0.0, 0, -1)
-        asel(R("TC"), R("BLK"), [[-1, 128]], OP.is_ge, 0.0, 0, 1)
-        fill("WE", 0, 4096, 0)
-        fill("WE", 8192, 12288, 0)
-        fill("RL", 0, 8192, 0)
-
-    def late_constants_b():
-        for c, terms in ((cE1, ((0, 16.0), (1, -16.0), (2, -1.0), (3, 1 / 32), (4, -4032.0))),
-                         (cE2, ((0, -16.0), (1, 16.0), (2, 1.0), (4, 4032.0), (5, -1.0))),
-                         (cBV, ((1, 256.0), (2, 16.0), (3, -15 / 32), (4, 64256.0))),
-                         (cM, ((0, 1 / 16), (2, 1 / 8192), (3, 32.0))),
-                         (cO, ((0, 1 / 32 - 0.5), (2, 2.0 ** -14 - 0.5))),
-                         (cINV, ((0, -1.0), (2, -1.0)))):
-            for n, (r, w) in enumerate(terms):
-                act(C(c), XMc(r), w, C(c) if n else 0.0)
-        act(R("sel", sE1, sE1 + 8), R("PH"), C(cE1))
-        act(R("sel", sE2, sE2 + 8), R("PH"), C(cE2))
-        act(R("BVW"), R("BLK"), C(cBV))
-        act(R("SX5"), R("SX"), XMc(5))
-        act(R("SXU"), R("SX"), C(cU))
-        act(R("SXT"), R("SX"), C(cT))
-        act(R("CB"), R("IO"), XMc(1), XMc(1))
-        act(R("J16"), R("JW"), 16.0)
-        act(R("CW"), R("JW"), 16.0, 65551.0)
-        act(C(cS4), C(cX), 1.0, 4096.0)
-        act(C(cS16), C(cX), 16.0)
-        act(C(cA), C(cX), 16.0, 16384.0)
-        act(R("sm", 32, 48), R("IO", 0, 16), 256.0, C(cA))
-        act(C(cB_), C(cX), 1.0, 257.0)
-        act(R("sm", 48, 64), R("IO", 0, 16), 16.0, C(cB_))
-        for n in ("LA", "LB", "RL"):
-            act(R(n, 8192, 8208), R("ONE", 0, 16), C(cINV))
-
-    def late_constants_c():
-        P16 = (0, 16, 1)
-        asel(R("KP"), R("ONE"), [[0, 16], [1, 16]], OP.not_equal, 0.0, 0, 0)
-        act(R("RST"), R("KP"), -float(2 ** 23), float(2 ** 23))
-        act(R("K1"), R("KP"), -65536.0, 65536.0)
-        act(R("K2"), R("KP"), 0.5)
-        scan(R("K1"), R("K2"), R("K1"), 0.0, OP.mult, OP.add)
-        act(R("MK"), R("MK"), -1.0, C(cX), AF.Abs)
+        act(R("sel", sE1, sE1 + 8), R("PH"), C(cW["E1"]))
+        act(R("sel", sE2, sE2 + 8), R("PH"), C(cW["E2"]))
+        act(R("sel", sN, sN + 8), R("PH"), C(cW["U"]))
+        act(R("sel", sN + 8, sN + 16), R("PH"), C(cW["T"]))
+        iota(R("MK"), [[0, 8], [1, 16]])
+        act(R("MK"), R("MK"), 1.0, C(cNX), AF.Abs)
         act(R("MK"), R("MK"), -1.0, 1.0, AF.Relu)
-        tt(R("sm", 64, 80), R("K1", 0, 16), R("XM"), OP.mult)
-        add("v", lambda g: g.vector.tensor_reduce(u(C(cPW)), u(R("sm", 64, 80)), AX, OP.add), [C(cPW)], [R("sm", 64, 80)])
+        iota(R("IOC"), [[-16, 256]], 4080)
+        asel(R("UT"), R("OF"), [[1, 128]], OP.is_gt, 0.0, 0, -1)
+        asel(R("TS"), R("BLS"), [[1, 128]], OP.is_gt, 0.0, 0, -1)
+        asel(R("TC"), R("BLS"), [[-1, 128]], OP.is_ge, 0.0, 0, 1)
+        asel(R("TD"), R("BLS"), [[-1, 128]], OP.is_gt, 0.0, 0, 1)
+        asel(R("KP"), R("ONE", 0, 128), [[0, 8], [1, 16]], OP.not_equal, 0.0, 0, 0)
+        asel(R("RST"), R("ZR"), [[0, 8], [1, 16]], OP.not_equal, NONE, 0, 0)
+        spread("WE", 0, 4096, 0)
+        dma("s", [(R("WE", 8192, 12288), R("WE", 0, 4096))])
+        act(C(cB56), C(cW["A"]), -16.0)
+        act(R("BVW"), R("BLK"), C(cB56))
+        act(R("SXN"), R("SX"), -1.0)
+        act(R("SX3"), R("SX"), XMc(3))
+        act(C(cD6), XMc(6), -2.0 ** 19)
+        act(R("D6"), R("IB"), C(cD6))
+        act(C(cR2), XMc(7), 1.0 / 64)
+        for k, c in enumerate((XMc(4), C(cW["A"]), C(cR2), C(cW["R3"]))):
+            act(R("NR", 128 * k, 128 * k + 128), R("SX", 15 - k, 143 - k), c)
+        act(C(cB1), XMc(7), 64.0, C(cW["B0"]))
+        act(C(cB2), XMc(7), 128.0, C(cW["B0"]))
+        act(C(cN0), C(cX), 16.0, 1.0)
+        iota(R("ism", 16, 24), [[16, 8]], 15, 0, True)
+        cp(R("LS", 80, 88), R("ism", 16, 24))
+        act(C(cB56), C(cW["M56"]), -113.0, 128.0)
+        act(C(c256), C(cW["M56"]), 16.0)
+        act(R("sm", 24, 32), R("IO", 0, 8), C(c256), C(cB56))
+        cp(R("LS", 88, 96), R("sm", 24, 32))
+        act(R("BASE", 80, 96), R("BASE", 0, 16), 1.0, 16.0 * 257)
+        act(R("BASE", 16, 32), R("BASE", 0, 16), 1.0, 8192.0 - 63)
+        act(R("BASE", 0, 16), R("BASE", 0, 16), 1.0, 16384.0 - 64)
+        iota(R("BASE", 32, 48), [[0, 16]], 4096 + 8192)
+        iota(R("BASE", 48, 80), [[0, 32]])
+        asel(R("K2"), R("ONE"), [[0, 16], [1, 16]], OP.not_equal, 0.0, 0, 0)
+        act(R("K1"), R("K2"), -65536.0, 65536.0)
+        act(R("K2"), R("K2"), 0.5)
+        scan(R("K1"), R("K2"), R("K1"), 0.0, OP.mult, OP.add)
+        tt(R("sm", 32, 48), R("K1", 0, 16), R("XM"), OP.mult)
+        add("v", lambda g: g.vector.tensor_reduce(u(C(cPW)), u(R("sm", 32, 48)), AX, OP.add), [C(cPW)], [R("sm", 32, 48)])
         act(C(cPW), C(cPW), 0.5)
         act(R("WM"), R("SX"), C(cPW))
+        if any(SIGNS):
+            act(R("ID", 0, 144), R("WM"), 0.5)
+            act(R("ID", 144, 288), R("WM"), -0.5)
+            iota(R("SXF", 0, 257), [[-16, 257]], 4088)
         asel(R("K1", 0, 256, 1, P16), R("K1", 0, 256, 1, P16), [[-1, 16], [0, 16]], OP.is_ge, 1.0, 0, 1)
         asel(R("K1", 0, 256, 1, P16), R("K1", 0, 256, 1, P16), [[1, 16], [0, 16]], OP.is_ge, float(2 ** 20), 0, -1)
-        asel(R("K2", 0, 128, 1, P16), R("ONE", 0, 128, 1, P16), [[0, 8], [1, 16]], OP.is_equal, 0.0, 0, -1)
+        act(R("K2", 0, 128, 1, P16), R("K16", 0, 128, 1, P16))
         mm(R("P7", 0, 256), R("K2", 0, 128, 1, P16), R("K1", 0, 256, 1, P16))
         act(R("THT"), R("P7", 0, 256))
-        iota(R("XS"), [[0, 256]])
-        iota(R("KZ", 0, 256, 1, P1), [[0, 256]])
-        ms(R("SS", 0, 1), 0.0)
-        ms(R("smb", 32, 33), 0.0)
-        ms(R("ZB"), 0.0)
-        ms(R("LTT", 0, 1), 0.0)
-        act(R("LTT", 1, 257), R("LTB"), XMc(5), XMc(4))
+        iota(R("SS", 0, 1), [[0, 1]], 2 ** 21)
+        iota(R("smb", 64, 65), [[0, 1]])
+        iota(R("WK", 0, 1), [[0, 1]])
+
+    def last_constants():
+        act(R("SXU"), R("SX"), C(cW["U"]))
+        act(R("SXT"), R("SX"), C(cW["T"]))
+        act(C(cST), C(cW["E1"]), C(cW["U"]))
+        act(C(cST), XMc(2), 4096.0, C(cST))
+        act(R("BST"), R("BLK"), C(cST))
+        act(R("BL3"), R("BLK"), XMc(3))
+        act(C(c4X), C(cX), 4.0)
 
     for v in range(3):
         last = v == 2
-        xt, ak, an = (XT0, A0, A1) if v % 2 == 0 else (XT1, A1, A0)
-        lin, nxt = ("LA", "LB") if v % 2 == 0 else ("LB", "LA")
-        if v > 0:
-            u_bars()
-            for e in (0, 1):
-                mm(R("P1", 256 + 128 * e, 384 + 128 * e), R("NL", 384 * e, 384 * e + 128), R("IH"))
-        new_flags()
-        ts(R("NV"), R("NL", 129, 385), -2047.5, OP.is_lt, 2.0, OP.mult)
-        if v > 0:
-            ts(R("LU"), R("P1", 256, 512), 2063.0, OP.add)
-        if v == 0:
-            gat("f", ("LA", 4096), 0, 4096, R("LB", 0, 4112), "LT_")
-        mm(R("P4", 0, 256), R("OF", 0, 128, 1, P8), R("TM", 0, 256, 1, P8), True, False)
-        mm(R("P4", 0, 256), R("I8"), R("NQ", 1, 257), False, False)
-        mm(R("P4", 0, 256), R("I8"), R("NV"), False, True)
-        lin2bars(("P3", 0), lin, 4096, R("sel", sC, sC + 8))
-        for k in range(8):
-            gat("a", ("XA", xt), 512 * k, 512 * k + 512, R("TN"), "LT_")
-            tt(R("T2", 512 * k, 512 * k + 512), IND(R("TN"), R("LU", 32 * k, 32 * k + 32)), R("XA", xt + 512 * k, xt + 512 * k + 512), OP.mult)
-            if k == 2:
-                act(R("C16", 1, 257), R("P3", 0, 256))
-                act(R("THR"), R("P4", 0, 256))
-                for ps, third in (("P3", R("NQ", 0, 256)), ("P4", R("ONE"))):
-                    mm(R(ps, 256, 512), R("IB"), R("C16", 0, 256), True, False)
-                    mm(R(ps, 256, 512), R("IN"), R("C16", 1, 257), False, False)
-                    mm(R(ps, 256, 512), R("IB"), third, False, True)
-            if k == 3:
-                lin2bars(("P2", 0), "T2", 0, R("sel", sSC, sSC + 8), (0,))
-        lin2bars(("P2", 0), "T2", 0, R("sel", sSC, sSC + 8), (1,))
-        if v == 0:
-            gat("f", ("XA", A0 + 16), 0, 4096, R("XA", XT1, XT1 + 4112), "LK")
-            late_constants_a()
-            act(R("YO", 0, 256), R("f1"), 1.0, -1.0)
-            act(R("YO", 256, 512), R("f0"), 1.0, -1.0)
-            dig("S1", 0, R("YO", 0, 256), act)
-            dig("S1", 1, R("YO", 256, 512), act)
-            act(C(cA), C(cX), 256.0)
-            ts(R("LBK"), R("IO"), C(cA), OP.add)
-            unstage("T1", 0, "S1", FOUR)
-            gat("a", ("LA", 0), 0, 4096, R("LB", 0, 4112), "SL1")
-            stage("S0", "LA", 0, [(4, 5), (5, 6)])
-            unstage("LA", 0, "S0", FOUR)
-            send(0, R("R0"), R("S0"))
-        else:
-            gat("f", ("XA", ak + 16), 2048, 4096, R("XA", *((XT0, BB) if v == 1 else (A1, XT1 + 4112))), "LK")
-        tt(R("NE", 1, 257), R("P2", 0, 256), R("THR"), OP.is_lt)
-        scan(R("Z"), R("P3", 256, 512), R("NE", 0, 256), 0.0, OP.add, OP.mult)
-        for e in (0, 1):
-            o = R("P1", 128 * e, 128 * e + 128)
-            mm(o, R("C16", 1 + 128 * e, 129 + 128 * e), R("IB"), True, False)
-            mm(o, R("NE", 1 + 128 * e, 129 + 128 * e), R("IAN" if v % 2 == 0 else "IA"), False, False)
-            mm(o, R("Z", 128 * e, 128 * e + 128), R("IF"), False, True)
-        scan(R("f0"), R("P4", 256, 512), R("NE", 0, 256), 0.0, OP.add, OP.mult)
-        last_tones(ak)
-        ts(R("LI"), R("P1", 0, 256), float(AW) if v % 2 == 0 else 0.0, OP.add)
-        act(R("THR"), R("NE", 0, 256), HUGE, 4 * BIG)
-        mm(R("P5", 0, 256), R("ONE", 0, 128, 1, P1), R("S8", 0, 256, 1, P1), True, False)
-        mm(R("P5", 0, 256), R("IB"), R("C16", 1, 257), False, False)
-        mm(R("P5", 0, 256), R("IG"), R("NE", 1, 257), False, False)
-        mm(R("P5", 0, 256), R("IF"), R("f0"), False, True)
-        if not last:
-            new_w()
-        if v == 0:
-            gat("a", ("LB", 4096), 0, 4096, R("T1"), "LBK")
-            late_constants_b()
-            stage("S1", "LB", 4096, FOUR)
-            stage("S1", "LA", 4096, [(4, 5), (5, 6)])
-            send(1, R("R1"), R("S1"))
-            unstage("LA", 4096, "S1", FOUR)
-        else:
-            gat("a", (lin, 0), 0, 4096, R(nxt), "LBK")
-            if v == 1:
-                stage("S0", lin, 0, FOUR + [(4, 5)])
-                send(3, R("R3"), R("S0", 0, 1280))
-        if not last:
-            act(R("WK", 1, 257), R("JW"), 1.0, 16.0 + (4096.0 if v % 2 == 0 else 0.0))
-            for k, off in ((0, 0), (1, 4096)) if v == 0 else ((2, 4096), (3, 0)):
-                arrive(k, R("R%d" % k))
-                unstage("RL", off, "R%d" % k, [(r, r) for r in range(6 - v)])
+        xt, xo, ak, an = (XT0, XT1, A0, A1) if v % 2 == 0 else (XT1, XT0, A1, A0)
+        pv = 4096 * (v + 1)
         win = R("XA", A0, A1) if v % 2 == 0 else R("XA", BB, XT1)
-        for k in range(2):
-            tt(R("T2", 2048 * k, 2048 * k + 2048), IND(win, R("LI", 128 * k, 128 * k + 128)), R("XA", xt + 2048 * k, xt + 2048 * k + 2048), OP.not_equal)
-            lin2bars(("P2", 256), "T2", 0, R("sel", sNE, sNE + 8), (k,))
+        helped, signs = HELP[v], SIGNS[v]
+
+        def at(t, t0=None):
+            due[0] = None if t is None else (t0 if v == 0 and t0 is not None else BEGIN[v] + t)
+        for e in (0, 1):
+            if v == 0:
+                at(None)
+                mm(PA(e, 1), R("f0", 128 * e, 128 * e + 128), R("IF"))
+                copy(H("NT", e), PA(e, 1))
+                for k in range(4 * e, 4 * e + 4):
+                    at(0, (10.0, 13.6, 14.5, 14.6, 15.4, 15.5, 20.0, 20.9)[k])
+                    gat(("W", pv), k, R("PT"), "LT_")
+            else:
+                arrive(4 * v + e, H("SR%d" % (v - 1), e))
+                for k in range(4 * e, 4 * e + 4):
+                    at((0.0, 0.0, 0.9, 0.9, 1.8, 1.8, 2.7, 3.9)[k])
+                    gat(("W", pv), k, R("RL", 0, pv + 16), "SR%d" % (v - 1), "vavavaav"[k])
+                at(None)
+                lin2bars(PA(e, 0), "W", pv + 2048 * e, sN, 2)
+                at(2.6 + 3 * e)
+                copy(H("NT", e), PA(e, 1))
+                on("v")
+                copy(H("NU", e), PA(e, 0))
+                on("v")
+            at(2.9 + 3 * e, 8.0)
+            tt(H("NQ", e, 1, 127), R("P%d" % e, 129, 256), H("NT", e, 0, 127), OP.not_equal)
+            relu2(H("NV", e, 0, 127), R("P%d" % e, 129, 256))
+            if v > 0:
+                at(None)
+                mm(PC(e, 2), H("NT", e), R("IF"))
+                at(3.4 + 3 * e)
+                ts(H("LT_", e), PC(e, 2), 16.0, OP.add)
+                at(None)
+                mm(PC(e, 3), H("NU", e), R("IF"))
+                at(3.7 + 3 * e)
+                ts(H("LU", e), PC(e, 3), 16.0, OP.add)
+            at(None)
+            lin2bars(PB(e, 0), "W", pv + 2048 * e, sC)
+            copy(H("C16", e, 1), PB(e, 0))
+            on("a")
+            mms(PB(e, 1), [(R("OF", 0, 128, 1, P8), R("TM", 0, 128, 1, P8)), (R("I8"), H("NQ", e, 1)), (R("I8"), H("NV", e))])
+            copy(H("THR", e), PB(e, 1))
+            on("a")
+            mms(PB(e, 2), [(R("IB"), H("C16", e)), (R("IN"), H("C16", e, 1)), (R("IB"), H("NQ", e))])
+            mms(PB(e, 3), [(R("IN"), H("C16", e)), (R("IB"), H("C16", e, 1)), (row(r64), row(r256))])
+        for e in (0, 1):
+            for k in range(4 * e, 4 * e + 4):
+                at(3.7 + 0.9 * k + 0.7 * e, 10.0 + 0.9 * k + 2.9 * e)
+                gat(("XA", xt), k, R("TN"), "LT_", "a")
+                at(4.8 + 1.1 * k, 11.0 + 0.9 * k + 2.9 * e)
+                tt(R("T2", 512 * k, 512 * k + 512), IND(R("TN"), R("LU", 32 * k, 32 * k + 32)), R("XA", xt + 512 * k, xt + 512 * k + 512), OP.mult)
+            at(None)
+            lin2bars(PC(e, 0), "T2", 2048 * e, sSC)
         if v == 0:
-            late_constants_c()
-        mm(R("P7", 256, 512), R("IF"), R("J16"), True, False)
-        mm(R("P7", 256, 512), R("IB"), R("LTB"), False, True)
-        act(R("WB", 1, 257), R("P7", 256, 512))
-        scan(R("Z"), R("THR"), R("P2", 256, 512), 4 * BIG, OP.min, OP.max)
-        tt(R("f1"), R("P5", 0, 256), R("Z"), OP.add)
-        scan(R("Z"), R("RST"), R("f1"), 0.0, OP.add, OP.min)
-        spread(R("P4", 256, 512), "Z")
-        tt(R("f1"), R("P4", 256, 512), R("MK"), OP.mult)
-        act(R("f0"), R("P4", 256, 512))
+            for k in range(8):
+                at(0, (16.4, 17.3, 21.2, 21.8, 22.1, 22.7, 23.0, 23.6)[k])
+                gat(("XA", A0 + 16), k, R("TN"), "LK")
+            at(0, 30.0)
+            late_constants()
+            at(None)
+            dma("s", stage("S1", "W", pv, [(2, 2), (3, 3), (4, 5), (5, 6)]))
+            send(2, R("R1"), R("S1"))
+            dma("s", unstage2("W", pv, "S1", [(0, 0), (1, 1)]))
+            arrive(2, R("R1"))
+            dma("s", unstage2("RL", 4096, "R1", [(0, 0), (1, 1)]) + unstage("RL", 4096, "R1", [(k, k) for k in range(2, 6)]))
+            arrive(0, R("RB"))
+            for k in range(8):
+                at(0, 30.5 + 1.5 * k)
+                gat(("RL", 0), k, R("PT"), "RB", "a")
+            at(None)
+            arrive(1, R("R0"))
+            dma("s", unstage2("RL", 0, "R0", [(0, 0), (1, 1)]))
+            for n, a in (("RL", 8192), ("RL", 12288), ("W", 16384)):
+                act(R(n, a, a + 16), R("ONE", 0, 16), C(cA))
+        elif v == 1:
+            dma("s", stage("S1", "W", pv, [(0, 0), (1, 1), (2, 2), (3, 3), (4, 5)]))
+            send(3, R("R2"), R("S1", 0, 1280))
+            arrive(3, R("R2"))
+            dma("s", unstage("RL", 8192, "R2", [(k, k) for k in range(5)]))
+        at(-0.5, 24.5)
+        last_tones(ak)
         for e in (0, 1):
-            mm(R("P6", 384 + 8 * e, 392 + 8 * e), R("f1", 128 * e, 128 * e + 128), R("PH"))
+            at(10.0 + 4.3 * e, 22.0 + 2 * e)
+            tt(H("NE", e, 1), PC(e, 0), H("THR", e), OP.is_lt)
+            scan(H("Z", e), PB(e, 2), H("NE", e), 0.0, OP.add, OP.mult)
+            at(None)
+            mms(PC(e, 3), [(H("C16", e, 1), R("IB")), (H("NE", e, 1), R("IAN" if v % 2 == 0 else "IA")), (H("Z", e), R("IF"))])
+            at(10.9 + 4.3 * e, 23.0 + 2 * e)
+            ts(H("LI", e), PC(e, 3), float(AW) if v % 2 == 0 else 0.0, OP.add)
+            scan(H("f0", e), PB(e, 3), H("NE", e), 0.0, OP.add, OP.mult)
+            act(H("THR", e), H("NE", e), HUGE, 4 * BIG)
+            if not last:
+                act(H("NW", e), H("NQ", e), 1.0, -16.0)
+                at(12.0 + 4.3 * e, 25.5 + 2 * e)
+                scan(H("TK", e), H("NW", e), H("NE", e), 0.0, OP.add, OP.mult)
+            at(None)
+            mms(PC(e, 2), [(row(r64), row(rS8)), (row(r64), row(r64)), (R("IN"), H("C16", e, 1)), (R("IG"), H("NE", e, 1)), (R("IF"), H("f0", e))])
         for e in (0, 1):
-            mm(R("P3", 128 * e, 128 * e + 128), R("f0", 128 * e, 128 * e + 128), R("IF"))
-        KM = R("P6", 384, 400)
-        cp(R("ism", 0, 16), KM)
-        ts(R("smb", 16, 32), KM, 5 * BIG, OP.is_lt)
-        ts(R("ism", 16, 32), R("ism", 0, 16), 4, OP.arith_shift_right, 511, OP.bitwise_and)
-        cp(R("smb", 0, 16), R("ism", 16, 32))
-        for y in range(16):
-            ts(R("OH", 256 * y, 256 * y + 256), R("IOC"), R("smb", y, y + 1), OP.is_equal, R("smb", 16 + y, 17 + y), OP.mult)
-            mm(R("P7", 0, 256), R("WM", 15 - y, 143 - y), R("OH", 256 * y, 256 * y + 256), y == 0, y == 15)
+            for k in range(4 * e, 4 * e + 4):
+                o, x, keys = R("T2", 512 * k, 512 * k + 512), R("XA", xt + 512 * k, xt + 512 * k + 512), IND(win, R("LI", 32 * k, 32 * k + 32))
+                if k in helped:
+                    at(12.3 + 0.9 * helped.index(k))
+                    act(R("XA", xo + 512 * k, xo + 512 * k + 512), keys)
+                    keys = R("XA", xo + 512 * k, xo + 512 * k + 512)
+                at(13.7 + 0.9 * k + 0.5 * e + (k > 4))
+                tt(o, keys, x, OP.not_equal)
+            at(None)
+            lin2bars(PC(e, 1), "T2", 2048 * e, sNE)
+            at(17.9 + 4.5 * e)
+            scan(H("Z", e), H("THR", e), PC(e, 1), 4 * BIG, OP.min, OP.max)
+            tt(H("f1", e), PC(e, 2), H("Z", e), OP.add)
+            scan(H("Z2", e), R("RST"), H("f1", e), 0.0, OP.max, OP.min)
+            tt(H("f1", e), IND(H("Z2", e, 0, HW), R("LS", 80, 88)), R("MK"), OP.mult)
+            km = R("P6", 8 * e, 8 * e + 8)
+            at(None)
+            mm(km, H("f1", e), R("PH"))
+            t1, c16, t2, r16 = R("sm", 48 + 8 * e, 56 + 8 * e), R("smb", 8 * e, 8 * e + 8), R("smb", 16 + 8 * e, 24 + 8 * e), R("smb", 32 + 8 * e, 40 + 8 * e)
+            at(19.3 + 4.7 * e)
+            ts(t1, km, 1.5 * 2.0 ** 37, OP.add, 1.5 * 2.0 ** 37, OP.subtract)
+            tt(c16, km, t1, OP.subtract)
+            ts(R("LS", 8 * e, 8 * e + 8), c16, -1.0 / 16, OP.mult, 256.0, OP.add)
+            for y in range(8 * e, 8 * e + 8):
+                if y in signs:
+                    o = 272 * (signs.index(y) % 7)
+                    at(19.8 + 4.8 * e + 0.37 * len([z for z in signs if 8 * e <= z < y]))
+                    act(R("OH", o, o + 257), R("SXF", 0, 257), -1.0, R("smb", y, y + 1), AF.Sign)
+                    at(None)
+                    mm(R("P7", 0, 256), R("ID", 15 - y, 143 - y), R("OH", o + 1, o + 257), y == 0, False)
+                    mm(R("P7", 0, 256), R("ID", 159 - y, 287 - y), R("OH", o, o + 256), False, y == 15)
+                    continue
+                o = 2048 + 256 * (y % 8)
+                at(21.8 + 2.8 * e + 0.01 * y)
+                ts(R("OH", o, o + 256), R("IOC"), R("smb", y, y + 1), OP.is_equal)
+                at(None)
+                mm(R("P7", 0, 256), R("WM", 15 - y, 143 - y), R("OH", o, o + 256), y == 0, y == 15)
+            at(22.2 + 3.6 * e)
+            ts(t2, t1, 1.5 * 2.0 ** 42, OP.add, 1.5 * 2.0 ** 42, OP.subtract)
+            tt(r16, t1, t2, OP.subtract)
+            at(18.8 + 4.6 * e)
+            act(H("f2", e), IND(H("Z2", e, 0, HW), R("LS", 88, 96)))
+            mm(R("P2", 256 + 128 * e, 384 + 128 * e), H("f2", e), R("IF"))
+            act(H("S5", e), R("P2", 256 + 128 * e, 384 + 128 * e), 2.0 ** -19, 64.0)
+            at(19.7 + 4.8 * e)
+            act(H("LG", e), IND(R("LTT", 0, 257), R("LS", 8 * e, 8 * e + 8)))
+            mms(R("P2", 128 * e, 128 * e + 128), [(H("f2", e), R("IF")), (row(rX4), row(rIO, 128 * e)), (R("IB"), H("LG", e)), (R("D6"), H("S5", e))])
+            at(20.5 + 5.0 * e)
+            act(H("VAL", e), R("P2", 128 * e, 128 * e + 128), C(cW["SC"]), C((cW["B0"], cB1, cB2)[v]))
+            if not last:
+                ps = R("P3", 256 * e + 128, 256 * e + 256)
+                at(22.5 + 4.5 * e)
+                mms(ps, [(H("TK", e), R("IF")), (R("BVW"), H("VAL", e))])
+                relu(H("NC", e), ps, C(cN0))
+                on("a")
+                positions(e, BEGIN[v] + 26.5 + 2.2 * e)
+                act(H("f3", e), R("P3", 256 * e, 256 * e + 128), 1.0, 16.0 if v % 2 == 0 else 16.0 + AW)
+        if not last:
+            at(14.0)
+            act(R("WK", 1, 257), R("JW"), 1.0, 16.0 + (4096.0 if v % 2 == 0 else 0.0))
+        c16, t2, r16, tk = R("smb", 0, 16), R("smb", 16, 32), R("smb", 32, 48), R("smb", 48, 64)
+        at(26.0)
         act(R("SS", 1, 257), R("P7", 0, 256))
-        cp(R("LS", 0, 16), R("ism", 16, 32))
-        ts(R("smb", 64, 80), R("smb", 16, 32), -1.0, OP.mult, 1.0, OP.add)
-        tt(R("LG"), IND(R("LTT", 0, 257), R("LS", 0, 16)), R("CB"), OP.add)
+        at(None)
+        to_offers(R("P6", 16, 32), "SX3", "LG", [(R("IR"), r16)])
+        mm(R("P4", 0, 80), R("IF"), R("BASE", 0, 80), True, False)
+        for a, l, r in ((0, "IS", t2), (16, "IS", t2), (0, "IR", r16), (32, "IN", c16)):
+            mm(R("P4", a, a + 16), R(l), r, False, False)
+        at(28.0)
+        mms(R("P5", 256, 512), [(R("NR", 128 * k, 128 * k + 128), R("VAL")) for k in range(4)])
+        act(R("NRC"), R("P5", 256, 512))
+        at(26.6)
         tt(R("VI"), IND(R("SS", 0, 257), R("LS", 0, 16)), R("THT"), OP.is_ge)
-        for x in range(16):
-            mm(R("P6", 400, 416), R("SX5", 15 - x, 143 - x), R("LG", x, 256, 16), x == 0, x == 15)
-        mm(R("P7", 256, 272), R("IB"), R("smb", 64, 80), True, False)
-        for x in range(16):
-            mm(R("P7", 256, 272), R("SX", 15 - x, 143 - x), R("VI", x, 256, 16), False, x == 15)
-        ts(R("i0"), R("P3", 0, 256), C(cM), OP.mult, C(cO), OP.add)
-        ts(R("i0"), R("i0"), 511, OP.bitwise_and)
-        tt(R("VAL"), R("i0"), R("LG"), OP.add)
-        ts(R("ism", 32, 48), R("ism", 0, 16), 15, OP.bitwise_and)
-        ts(R("ism", 48, 64), R("ism", 0, 16), 13, OP.arith_shift_right, 15, OP.bitwise_and)
-        tt(R("sm", 64, 80), R("ism", 48, 64), R("sm", 32, 48), OP.add)
-        tt(R("sm", 64, 80), R("sm", 64, 80), R("ism", 32, 48), OP.subtract)
-        tt(R("sm", 80, 96), R("P6", 400, 416), R("ism", 32, 48), OP.subtract)
-        ts(R("sm", 96, 112), R("P6", 400, 416), 8193.0, OP.add)
-        mm(R("P4", 0, 256), R("BVW"), R("VAL"))
-        ts(R("sm", 112, 128), R("P7", 256, 272), 0.0, OP.is_equal)
-        tt(R("smb", 33, 49), R("sm", 112, 128), R("sm", 80, 96), OP.mult)
-        mm(R("P6", 416, 432), R("TS"), R("smb", 33, 49), True, False)
-        mm(R("P6", 416, 432), R("TC"), R("smb", 32, 48), False, True)
-        ts(R("sm", 128, 144), R("sm", 112, 128), -16384.0, OP.mult)
-        tt(R("sm", 128, 144), R("sm", 128, 144), R("sm", 64, 80), OP.add)
-        tt(R("sm", 96, 112), R("sm", 96, 112), R("sm", 112, 128), OP.mult)
-        if not last:
-            tt(R("M2"), R("P4", 0, 256), R("CW"), OP.is_le)
-            tt(R("M2"), R("M2"), R("NW"), OP.mult)
-            mm(R("P5", 0, 256), R("TI"), R("M2"))
-            steps(0, 16)
-        scan(R("sm", 144, 160), R("P6", 416, 432), R("ZB", 0, 16), 0.0, OP.add, OP.add)
-        tt(R("sm", 160, 176), R("sm", 144, 160), R("sm", 128, 144), OP.add)
-        cp(R("LS", 16, 32), R("sm", 160, 176))
-        tt(R("sm", 176, 192), R("sm", 160, 176), R("sm", 96, 112), OP.add)
+        to_offers(R("P7", 256, 272), "SX", "VI")
+        at(27.9)
+        ts(tk, R("P7", 256, 272), 0.0, OP.is_equal, -8192.0, OP.mult)
+        tt(R("smb", 65, 81), R("P6", 16, 32), tk, OP.mult)
+        for a in (0, 0, 16, 32):
+            mm(R("P4", a, a + 16), R("IB"), tk, False, False)
+        for a, l, b in ((48, "TS", 65), (48, "TC", 64), (64, "TI", 65), (64, "TD", 64)):
+            mm(R("P4", a, a + 16), R(l), R("smb", b, b + 16), False, l == "TD")
+        at(28.7)
+        scan(R("sm", 64, 96), R("KP", 0, 32), R("P4", 48, 80), 0.0, OP.mult, OP.add)
+        tt(R("sm", 96, 128), R("P4", 0, 32), R("sm", 64, 96), OP.add)
+        cp(R("LS", 16, 48), R("sm", 96, 128))
         cp(IND(R("WE"), R("LS", 16, 32)), R("VAL"))
-        ts(R("LS", 32, 48), R("sm", 176, 192), -8192.0, OP.add)
+        at(30.0)
         cp(IND(R("WE", 8192, 24576), R("LS", 32, 48)), R("VAL"))
-        mm(R("P6", 0, 256), R("TS", 0, 128, 1, (0, 1, 1)), R("KZ", 0, 256, 1, P1), True, False)
+        at(28.6 if last else 30.1)
+        tt(R("sm", 128, 144), R("P4", 32, 48), R("BASE", 80, 96), OP.min)
+        ts(R("LS", 48, 64), R("sm", 128, 144), 1.0 / 16, OP.mult)
+        sl = "SL%d" % (v % 2)
+        at(None)
+        for w, sel in ((0, sE1), (8192, sE2)):
+            for e in (0, 1):
+                if w == 0:
+                    mm(PA(e, 0), R("TS", 0, 128, 1, P1), R("TD", 0, 128, 1, P1), True, False)
+                for s in range(16):
+                    mm(R("P%d" % e, s, 128, 16), R("WE", w + 2048 * e + s, w + 2048 * e + 2048, 16), R("sel", sel, sel + 8), False, w > 0 and s == 15)
         for e in (0, 1):
-            for s in range(16):
-                o, a = R("P6", 128 * e + s, 128 * e + 128, 16), 2048 * e + s
-                mm(o, R("WE", a, 2048 * e + 2048, 16), R("sel", sE1, sE1 + 8), False, False)
+            at(32.4 + 0.6 * e)
+            scan(H("Z2", e), R("KP"), PA(e, 0), 0.0, OP.mult, OP.add)
+            copy(H("f1", e), IND(H("Z2", e, 0, HW), R("LS", 80, 88)))
+            at(None)
+            mms(PA(e, 1), [(row(rONE), row(rB16, 128 * e))] + [(row(r64), row(r64))] * (v + 1) + [(H("Z2", e), R("IF"))]
+                + [(H("f1", 0), R("OF"))] * e + [(H("f1", e), R("UT"))])
+            at(33.6 + 0.8 * e)
+            ts(H(sl, e), PA(e, 1), C(cX), OP.add, pv + 4096.0, OP.min)
+            if not last:
+                send(4 * v + 4 + e, H("SR%d" % v, e), H(sl, e))
         if not last:
-            pos_mm(0, 8)
-        for e in (0, 1):
-            for s in range(16):
-                o, a = R("P6", 128 * e + s, 128 * e + 128, 16), 2048 * e + s
-                mm(o, R("WE", 8192 + a, 10240 + 2048 * e, 16), R("sel", sE2, sE2 + 8), False, e == 1 and s == 15)
-        tt(R("sm", 192, 208), R("ism", 16, 32), R("sm", 48, 64), OP.subtract)
-        tt(R("sm", 192, 208), R("sm", 192, 208), R("sm", 112, 128), OP.mult)
-        tt(R("sm", 192, 208), R("sm", 192, 208), R("sm", 48, 64), OP.add)
-        cp(R("LS", 48, 64), R("sm", 192, 208))
-        act(R("f1"), R("P4", 0, 256), 1.0, C(cS16))
-        cp(IND(R("WB"), R("LS", 48, 64)), R("f1"))
-        if last:
-            cp(R("i1"), R("WB", 1, 257))
-            ts(R("i2"), R("i1"), 4, OP.arith_shift_right)
-            ts(R("i1"), R("i1"), 15, OP.bitwise_and)
-            ts(R("f1"), R("i1"), C(cX), OP.is_lt, 8192.0, OP.mult)
-            tt(R("f1"), R("f1"), R("i2"), OP.add)
-            ts(R("LBK"), R("f1"), 8192.0, OP.min)
-            gat("f", ("T2", 0), 0, 4096, R(lin), "LBK")
-        scan(R("Z"), R("KP"), R("P6", 0, 256), 0.0, OP.mult, OP.add)
-        spread(R("f0"), "Z")
-        o0, o1 = R("P1", 0, 128), R("P2", 0, 128)
-        for e, o in ((0, o0), (1, o1)):
-            mm(o, R("ONE", 0, 128, 1, P1), R("B16", 128 * e, 128 * e + 128, 1, P1), True, False)
-            mm(o, R("Z", 128 * e, 128 * e + 128), R("IF"), False, False)
-        mm(o0, R("f0", 0, 128), R("UT"), False, True)
-        mm(o1, R("f0", 0, 128), R("OF"), False, False)
-        mm(o1, R("f0", 128, 256), R("UT"), False, True)
-        sl = R("SL%d" % (v % 2))
-        ts(R("SL%d" % (v % 2), 0, 128), o0, C(cS4), OP.add, 8192.0, OP.min)
-        ts(R("SL%d" % (v % 2), 128, 256), o1, C(cS4), OP.add, 8192.0, OP.min)
-        if not last:
-            send(4 + v, R("SR%d" % v), sl)
-            pos_mm(8, 16)
-            act(R("f2"), R("P0", 0, 256), 0.5, 8.0 + (0.0 if v % 2 == 0 else float(AW)))
-            cp(R("i1"), R("WB", 1, 257))
-            cp(IND(R("WK"), R("LS", 48, 64)), R("f2"))
+            at(31.7)
+            cp(IND(R("WK"), R("LS", 48, 64)), R("f3"))
+            at(33.2)
             cp(R("LK"), R("WK", 1, 257))
-            gat("f", ("XA", an + 16), 0, 2048, R("XA", *((XT0, BB) if v == 0 else (A1, XT1 + 4112))), "LK")
-            ts(R("i2"), R("i1"), 4, OP.arith_shift_right)
-            cp(R("LBK"), R("i2"))
-            ts(R("i1"), R("i1"), 15, OP.bitwise_and)
-            cp(R("LTB"), R("i1"))
-            act(R("LTT", 1, 257), R("LTB"), XMc(5), XMc(4))
+            for k in range(8):
+                at(33.7 + 0.5 * k)
+                gat(("XA", an + 16), k, R("XA", *((XT0, BB) if v == 0 else (A1, XT1 + 4112))), "LK")
+            at(38.0)
+            cp(IND(R("LTT"), R("LS", 48, 64)), R("NRC"))
+            at(None)
             k0 = len(ops)
             fill("WE", 0, 4096, 0)
             fill("WE", 8192, 12288, 0)
-            for op in ops[k0:]:
-                op["behind"] = "lo%d" % (4 + v)
-            arrive(4 + v, R("SR%d" % v))
-            gat("f", (nxt, 4096), 0, 4096, R("RL"), "SR%d" % v)
-            names2bars(nxt, 4096)
-            t_list(R("LT_"))
+            behind(k0, "lo%d" % (4 * v + 5))
             if v == 0:
-                stage("S1", nxt, 4096, FOUR + [(4, 5)])
-                send(2, R("R2"), R("S1", 0, 1280))
+                last_constants()
+                fill("W", 0, 4096, 0)
+                dig("S0", 1, R("i2"))
+                behind(len(ops) - 2, "lo5")
+                dma("s", unstage2("W", 0, "S0", [(k, k) for k in range(4)]))
         else:
-            gat("f", ("T1", 0), 0, 4096, R(lin), "SL0")
+            at(28.65)
+            cp(IND(R("LTT"), R("LS", 48, 64)), R("NRC"))
+            at(None)
+            mm(R("P7", 256, 512), R("BL3"), R("LTT", 1, 257))
+            act(R("M2"), R("P7", 256, 512), -4.0, C(c4X), AF.Relu)
+            mms(R("P7", 0, 256), [(R("BST"), R("LTT", 1, 257)), (R("IA"), R("M2"))])
+            ts(R("LK"), R("P7", 0, 256), C(cX), OP.add, 16384.0, OP.min)
+            for k in range(8):
+                at(31.5 + 0.9 * k)
+                gat(("T1", 0), k, R("W"), "LK", "a")
+            at(None)
             for f, w in ((0, "SXU"), (1, "SXT")):
-                for x in range(16):
-                    mm(R("P7" if f == 0 else "P5", 0, 256), R(w, 15 - x, 143 - x), R("T2", 256 * x, 256 * x + 256), x == 0, x == 15)
-            names2bars("T1", 0)
-            act(R("ZO", 0, 256), R("P7", 0, 256))
-            act(R("ZO", 256, 512), R("P5", 0, 256))
+                mms(R("P%d" % (6 + f), 0, 256), [(R(w, 15 - x, 143 - x), R("T1", 256 * x, 256 * x + 256)) for x in range(16)])
+                copy(R("ZO", 256 * f, 256 * f + 256), R("P%d" % (6 + f), 0, 256))
             dma("a", [(X("zu"), R("ZO", 0, 256)), (X("zt"), R("ZO", 256, 512))])
-            ts(R("NL", 0, 512), R("P0"), -2047.0, OP.add)
-            for e in (0, 1):
-                mm(R("P1", 128 * e, 128 * e + 128), R("NL", 384 * e, 384 * e + 128), R("IH"))
-                mm(R("P1", 256 + 128 * e, 384 + 128 * e), R("NL", 128 + 128 * e, 256 + 128 * e), R("IH"))
-            ts(R("YO"), R("P1"), 2047.0, OP.add)
+            for q in range(4):
+                for k in (2 * q, 2 * q + 1):
+                    at(35.0 + 0.7 * k)
+                    gat(("XA", XT1), k, R("W"), sl, "v" if k < 5 else None)
+                at(None)
+                for f, w in ((0, "SXU"), (1, "SXT")):
+                    o = R("P%d" % (2 + q), 64 * f, 64 * f + 64)
+                    mms(o, [(R(w, 15 - s, 143 - s), R("XA", XT1 + 1024 * q + s, XT1 + 1024 * q + 1024, 16)) for s in range(16)])
+                    copy(R("YO", 256 * f + 64 * q, 256 * f + 64 * q + 64), o)
             dma("s", [(X("yu"), R("YO", 0, 256)), (X("yt"), R("YO", 256, 512))])
     return ops
 
 
-from concourse.mybir import AxisListType
-AX = AxisListType.X
 PLAN = {}
 
 
@@ -645,7 +778,6 @@ def order(ops, lanes):
     seen = {}
     for n, op in enumerate(ops):
         dep = set()
-        op["soft"] = ()
         for isw, accs in ((False, op["rd"]), (True, op["wr"])):
             for name, a, b, pm in accs:
                 psum = SCRATCH[name][0] == "psum"
@@ -661,7 +793,7 @@ def order(ops, lanes):
             for name, a, b, pm in accs:
                 old = seen.get(name, [])
                 if SCRATCH[name][0] == "psum":
-                    old = [x for x in old if ops[x[0]]["q"] != op["q"]]
+                    old = []
                 elif isw:
                     old = [x for x in old if not (a <= x[2] and x[3] <= b and (x[4] & ~pm) == 0 and x[0] in dep)]
                 seen[name] = old + [(n, isw, a, b, pm)]
@@ -677,106 +809,8 @@ def order(ops, lanes):
                 op["dep"].update(members[ops[m]["grp"]])
         op["soft"] = set(members[op["behind"]] if "behind" in op else []) - op["dep"]
         op["pre"] = set(op["dep"]) | set(members[op["after"]] if "after" in op else []) | op["soft"]
-
-    def delay(m, n):
-        if ops[m]["q"] == "t" and ops[n]["q"] == "t":
-            return 0.0
-        return 0.15
-    lat = [0.0 if op["grp"] is None or op["q"] == "x" else (2.0 if op["grp"][0] == "d" else 2.5) for op in ops]
-    succ = [[] for _ in ops]
-    for n, op in enumerate(ops):
-        for m in op["pre"]:
-            succ[m].append(n)
-    hard = [[(m, delay(m, n)) for m in sorted(op["pre"] - op["soft"])] for n, op in enumerate(ops)]
-    where = [sorted(op.get("alt", op["q"])) for op in ops]
-
-    def schedule(bias):
-        tail = [0.0] * len(ops)
-        for n in range(len(ops) - 1, -1, -1):
-            tail[n] = ops[n]["c"] + lat[n] + bias[n] + max([tail[k] for k in succ[n]] or [0.0]) + 0.1
-        left = [len(op["pre"]) for op in ops]
-        ready = {n: 0.0 for n in range(len(ops)) if left[n] == 0}
-        end = [0.0] * len(ops)
-        free = {q: 0.0 for q in "vatpsx"}
-        wire = {"d": 0.0, "l": 0.0, "a": 0.0}
-        seq, on, held, prev = [], {}, {}, {}
-        while ready:
-            best = None
-            for n, t0 in ready.items():
-                for q in where[n]:
-                    st = t0 if t0 > free[q] else free[q]
-                    key = st - SLACK * tail[n]
-                    if best is None or key < best[0]:
-                        best = (key, n, q, st)
-            n, q, st = best[1:]
-            op = ops[n]
-            if st > ready.pop(n) + 1e-9:
-                held[n] = prev[q]
-            on[n] = q
-            prev[q] = n
-            if op["grp"] is None:
-                end[n] = free[q] = st + op["c"]
-            else:
-                w = op["grp"][0]
-                end[n] = wire[w] = max(st + lat[n], wire[w]) + op["c"]
-                free[q] = st + (0.3 if w == "l" else 0.06)
-            seq.append(n)
-            for k in succ[n]:
-                left[k] -= 1
-                if left[k] == 0:
-                    ready[k] = max([end[m] + d for m, d in hard[k]] or [0.0])
-        return max(end), seq, on, held, end
-
-    edge = [[(m, d) for m, d in hard[n]] + [(m, None) for m in sorted(op["soft"])] for n, op in enumerate(ops)]
-    back = [[] for _ in ops]
-    for n in range(len(ops)):
-        for m, d in edge[n]:
-            back[m].append((n, d))
-    shape = []
-    for n, op in enumerate(ops):
-        w = (op["grp"] or " ")[0]
-        shape.append((lat[n], op["c"], 0.0) if w == "d" else ((0.0, 0.3, lat[n] + op["c"]) if w == "l" else (0.0, op["c"], 0.0)))
-
-    def pack(rank, edges, forward):
-        start, end, on, busy = {}, {}, {}, {}
-        for n in rank:
-            t0 = max([(end[m] + d if d is not None else (start[m] + 0.01 if forward else end[m] + 0.01 - sum(shape[n]))) for m, d in edges[n]] + [0.0])
-            x, c, y = shape[n] if forward else shape[n][::-1]
-            best = None
-            for q in (["d"] if (ops[n]["grp"] or " ")[0] == "d" else where[n]):
-                row = busy.setdefault(q, [])
-                t = t0 + x
-                k = len(row)
-                while k > 0 and row[k - 1][1] > t:
-                    k -= 1
-                while k < len(row) and row[k][0] < t + c - 1e-9:
-                    t = max(t, row[k][1])
-                    k += 1
-                if best is None or t < best[0]:
-                    best = (t, q, k)
-            t, q, k = best
-            busy[q].insert(k, (t, t + c))
-            start[n], end[n], on[n] = t - x, t + c + y, q
-        return max(end.values()), start, end, on
-
     if "seq" not in PLAN:
-        rank = schedule([0.0] * len(ops))[1]
-        top = None
-        rnd = 1
-        for _ in range(ROUNDS):
-            span, start, end, on = pack(rank, edge, True)
-            if top is None or span < top[0]:
-                top = (span, sorted(rank, key=lambda n: (start[n], n)), on)
-                PLAN["dbg"] = (ops, dict(start), dict(end), edge, on)
-            for n in range(len(ops) - 1, -1, -1):
-                end[n] = min([end[n]] + [end[k] - 1e-6 for k, d in back[n]])
-            span, start, end, on = pack(sorted(rank, key=lambda n: (-end[n], -n)), back, False)
-            late = {}
-            for n in range(len(ops)):
-                rnd = (rnd * 1103515245 + 12345) % 2147483648
-                late[n] = max([span - end[n] + (rnd >> 8) % 100 * JITTER] + [late[m] + 1e-6 for m, d in edge[n]])
-            rank = sorted(rank, key=lambda n: (late[n], n))
-        PLAN["seq"], PLAN["on"], PLAN["span"] = top[1], top[2], top[0]
+        plan(ops)
     seq = PLAN["seq"]
     for n, op in enumerate(ops):
         if "alt" in op:
@@ -811,6 +845,135 @@ def order(ops, lanes):
         else:
             total[op["grp"]] = total.get(op["grp"], 0) + (16 if op["grp"][0] == "d" else lanes[op["q"]][op["step"]])
     return seq, need, total
+
+
+HOP, LAT_D, LAT_R, ISSUE, DMA, LINK = 0.15, 2.0, 2.5, 0.3, 200e3, 60e3
+SEED, HEAT, THETA, LEAN, END, AHEAD = 1, 0.3, 0.15, 0.5, 135.0, 1.0
+
+
+def plan(ops):
+    def delay(m, n):
+        return 0.0 if ops[m]["q"] == "t" and ops[n]["q"] == "t" else HOP
+    N = len(ops)
+    kind = [(op["grp"] or " ")[0] for op in ops]
+    edge = [[(m, delay(m, n)) for m in sorted(op["pre"] - op["soft"])] + [(m, None) for m in sorted(op["soft"])]
+            for n, op in enumerate(ops)]
+    back = [[] for _ in ops]
+    for n in range(N):
+        for m, d in edge[n]:
+            back[m].append((n, d))
+    whole = []
+    for n, op in enumerate(ops):
+        if kind[n] == "d":
+            whole.append({"d": (LAT_D, op["c"], 0.0)})
+        elif kind[n] == "l":
+            whole.append({"p": (0.0, ISSUE, LAT_R + op["c"])})
+        else:
+            whole.append({q: (0.0, c, 0.0) for q, c in sorted(op.get("cq", {op["q"]: op["c"]}).items())})
+    least = [sum(min(w.values())) for w in whole]
+    gate = {op["grp"]: n for n, op in enumerate(ops) if op["grp"]}
+    marks = [gate[k] for k in ("ar5", "ar9")]
+
+    def walk(shape, boost):
+        tail = [0.0] * N
+        for n in range(N - 1, -1, -1):
+            t = 0.0
+            for k, d in back[n]:
+                if tail[k] > t:
+                    t = tail[k]
+            t += least[n] + HOP
+            if ops[n].get("due") is not None:
+                t = END - ops[n]["due"]
+            tail[n] = t + boost[n]
+        left = [len(e) for e in edge]
+        pool = {q: {} for q in "vatpd"}
+        start, end, on, at, held = [0.0] * N, [0.0] * N, [""] * N, {q: 0.0 for q in "vatpd"}, {}
+        prev = {}
+
+        def enter(n):
+            t = 0.0
+            for m, d in edge[n]:
+                x = end[m] + d if d is not None else start[m] + 0.01
+                if x > t:
+                    t = x
+            if "x" in shape[n]:
+                start[n], end[n], on[n] = t, t, "x"
+                leave(n)
+                return
+            for q, sh in shape[n].items():
+                pool[q][n] = t + sh[0]
+
+        def leave(n):
+            for k, d in back[n]:
+                left[k] -= 1
+                if not left[k]:
+                    enter(k)
+        for n in range(N):
+            if not edge[n]:
+                enter(n)
+        while any(pool.values()):
+            t, q = min([(max(at[q], min(p.values())), q) for q, p in pool.items() if p])
+            p = pool[q]
+            n = f = None
+            for m, r in p.items():
+                if r <= t + AHEAD:
+                    w = (tail[m] - (LEAN if q == "v" and len(shape[m]) > 1 else 0.0), -m)
+                    if n is None or w > n:
+                        n = w
+                    if r <= t and (f is None or w > f):
+                        f = w
+            n, f = -n[1], -f[1]
+            if p[n] > t and t + shape[f][q][1] + tail[n] <= max(p[n] + tail[n], p[n] + shape[n][q][1] + tail[f]) + THETA:
+                n = f
+            x, c, y = shape[n][q]
+            if p[n] < at[q] - 1e-9:
+                held[n] = prev[q]
+            t = max(t, p[n])
+            start[n], end[n], on[n], at[q], prev[q] = t - x, t + c + y, q, t + c, n
+            for r in shape[n]:
+                del pool[r][n]
+            leave(n)
+        return max(end) + 0.2 * sum(end[n] for n in marks), start, end, on, held
+
+    rnd = [SEED]
+
+    def draw(k):
+        rnd[0] = (rnd[0] * 1103515245 + 12345) % 2147483648
+        return (rnd[0] >> 8) % k
+
+    shape = [{op["first"]: w[op["first"]]} if "first" in op else w for op, w in zip(ops, whole)]
+    boost = [0.0] * N
+    top = now = walk(shape, boost)
+    for k in range(ROUNDS):
+        span, start, end, on, held = now
+        n = (marks + [end.index(max(end))])[draw(len(marks) + 1)]
+        pairs = []
+        while n is not None:
+            if n in held:
+                pairs.append((n, held[n]))
+                n = held[n]
+            else:
+                n = max([(end[m], m) for m, d in edge[n] if d is not None] + [(-1.0, None)], key=lambda x: x[0])[1]
+        s2, b2 = list(shape), list(boost)
+        for _ in range(1 + draw(2)):
+            n, m = pairs[draw(len(pairs))]
+            move = draw(5)
+            x = m if len(whole[m]) > 1 and (draw(2) or len(whole[n]) == 1) else n
+            if move >= 3 and len(whole[x]) > 1:
+                q = "v" if on[x] == "a" else "a"
+                s2[x] = {q: whole[x][q]}
+            elif move % 2:
+                b2[m] -= (1 + draw(30)) * 0.1
+            else:
+                b2[n] += (1 + draw(30)) * 0.1
+        new = walk(s2, b2)
+        if new[0] <= span + HEAT * (1.0 - k / ROUNDS) * draw(100) / 100:
+            now, shape, boost = new, s2, b2
+            if new[0] < top[0]:
+                top = new
+    PLAN["dbg"] = (ops, top[1], top[2], edge, top[3])
+    PLAN["seq"], PLAN["on"], PLAN["span"] = sorted(range(N), key=lambda n: (top[1][n], n)), top[3], max(top[2])
+    PLAN["marks"] = [top[2][n] for n in marks]
 
 
 def rank_program(g, core, T, topo):

@@ -1,12 +1,13 @@
 from concourse.mybir import AluOpType as OP, ActivationFunctionType as AF, AxisListType
+from concourse.bass import DstId, RemoteDMATransfer
 
 AX = AxisListType.X
 F32, BF, I32, U16 = "float32", "bfloat16", "int32", "uint16"
 SZ = {F32: 4, BF: 2, I32: 4, U16: 2}
 AW = 4128
-XT0, A0, BB, A1, XT1 = 0, 4096, 4096 + AW, 4096 + 2 * AW, 4096 + 3 * AW
-BIG, HUGE = float(2 ** 23), float(2 ** 27)
-NONE = 4 * BIG + 15 * 2.0 ** 19 + 15 * 2.0 ** 14 + 4096
+XT0, A0, BB, A1, XT1 = 0, 4096, 4096 + AW, 4352 + 2 * AW, 4352 + 3 * AW
+BIG, HUGE = float(2 ** 24), float(2 ** 27)
+NONE = 15 * 2.0 ** 19 + 4103.5
 HW = 144
 
 
@@ -24,21 +25,22 @@ SCRATCH = {
     "i0": _s([256], I32), "i1": _s([256], I32), "i2": _s([256], I32), "i3": _s([256], I32), "i4": _s([256], I32),
     "i5": _s([256], I32), "X3": _s([2, 8, 16], F32), "X4": _s([2, 8, 16], F32),
     "f0": _s([256], F32), "f1": _s([256], F32), "f2": _s([256], F32), "f3": _s([256], F32),
-    "ism": _s([32], I32), "col": _s([48], F32), "WT": _s([8], F32), "XM": _s([16], F32), "sm": _s([160], F32),
-    "smb": _s([112], BF), "ONE": _s([256], BF), "ZR": _s([128], F32), "K1": _s([256], BF), "K2": _s([256], BF),
-    "K16": _s([128], F32), "RW": _s([1280], BF), "IO": _s([256], F32), "JW": _s([256], F32),
+    "ism": _s([32], I32), "col": _s([48], F32), "WT": _s([8], F32), "XM": _s([16], F32), "sm": _s([176], F32),
+    "smb": _s([112], BF), "ONE": _s([256], BF), "ZR": _s([128], F32), "ZB": _s([256], BF),
+    "K16": _s([128], F32), "RW": _s([1424], BF), "IO": _s([256], F32), "JW": _s([256], F32),
     "IB": _s([128], BF), "IF": _s([128], F32), "IN": _s([128], BF), "I8": _s([128], BF), "IA": _s([128], BF),
-    "IAN": _s([128], BF), "IG": _s([128], BF), "IS": _s([128], BF), "IR": _s([128], BF), "D6": _s([128], BF),
-    "DF": _s([128], F32), "UT": _s([128], F32), "OF": _s([128], F32), "G8": _s([128], F32), "G8B": _s([256], BF),
+    "IAN": _s([128], BF), "IG": _s([384], BF), "IFN": _s([128], F32), "KK": _s([256], BF), "IS": _s([256], BF),
+    "IR": _s([256], BF), "D6": _s([128], BF),
+    "UT": _s([128], F32), "OF": _s([128], F32), "G8": _s([128], F32), "G8B": _s([256], BF),
     "BLK": _s([128], BF), "BLS": _s([128], BF), "TI": _s([128], BF), "TS": _s([128], BF), "TC": _s([128], BF),
-    "TD": _s([128], BF), "BVW": _s([128], BF), "BST": _s([128], BF), "BL3": _s([128], BF), "NR": _s([512], BF),
+    "TD": _s([128], BF), "BVW": _s([128], BF), "BST": _s([128], BF), "BL3": _s([128], BF), "NR": _s([128], BF),
     "sel": _s([64], BF), "PH": _s([8], F32), "SX": _s([144], BF), "SXD": _s([144], BF), "SXN": _s([144], BF),
-    "SXF": _s([288], F32), "TB": _s([128], BF), "ST": _s([1024], BF), "TK": _s([256], F32), "SX3": _s([144], BF),
+    "SXF": _s([288], F32), "TB": _s([128], BF), "ST": _s([1024], BF), "SX3": _s([144], BF),
     "SXU": _s([144], BF), "SXT": _s([144], BF), "WM": _s([144], BF),
     "MK": _s([128], F32), "RST": _s([128], F32), "KP": _s([128], BF), "IOC": _s([256], BF), "THT": _s([256], F32),
-    "TM": _s([128], F32), "BASE": _s([96], F32),
+    "TM": _s([128], F32), "TMB": _s([256], BF), "BASE": _s([144], F32),
     "NT": _s([256], F32), "NU": _s([256], F32), "LT_": _s([256], U16), "LU": _s([256], U16), "LI": _s([256], U16),
-    "LK": _s([256], U16), "LS": _s([96], U16), "NQ": _s([2 * HW], BF), "NV": _s([256], BF), "NE": _s([2 * HW], BF),
+    "LK": _s([256], U16), "LS": _s([128], U16), "NQ": _s([2 * HW], BF), "NV": _s([256], BF), "NE": _s([2 * HW], BF),
     "C16": _s([2 * HW], BF), "THR": _s([256], F32), "Z": _s([256], F32), "Z2": _s([2 * HW], F32), "NW": _s([256], BF),
     "SS": _s([264], F32), "VI": _s([256], BF), "LTT": _s([520], BF), "LG": _s([256], BF), "VAL": _s([256], BF),
     "S5": _s([256], BF), "M2": _s([256], BF), "NC": _s([256], BF), "NRC": _s([256], BF),
@@ -48,12 +50,20 @@ for _k in range(8):
     SCRATCH["P%d" % _k] = ("psum", [128, 512], F32)
 SEMAPHORES = (["qv", "qa", "qt", "qp"] + ["d%d" % _k for _k in range(40)] + ["ar%d" % _k for _k in range(10)]
               + ["lo%d" % _k for _k in range(10)])
+ALIAS = {"T2": ("WE", 4096, 4096), "PT": ("RL", 8192, 4112), "OH": ("T1", 0, 4096),
+         "K1": ("NRC", 0, 256), "K2": ("VAL", 0, 256), "DF": ("UT", 0, 128)}
 ALLP = (1 << 128) - 1
-CY, PE, ROUNDS = 1.04e-3, 0.53e-3, 2500
+HELP = ((6,), (0, 1, 2, 3, 5, 6, 7), (0, 1, 2, 3, 5, 6, 7))
+CUT = {"pp": "121121", "rl": "211211", "t": "11111111", "k": "112112", "pb": "4121", "c": "11111111", "rn": "112211",
+       "fb": "11111111", "fp": "112112"}
+CY, PE = 1.04e-3, 0.53e-3
 BEGIN = (12.3, 52.0, 90.0)
-SIGNS = ((), (), ())
-HELP = ((), (1, 2, 3, 6, 7), (1, 2, 3, 6, 7))
-ALIAS = {"T2": ("WE", 4096, 4096), "PT": ("W", 12288, 4112), "OH": ("T1", 0, 4096)}
+TM = {"pw": 8.93, "v1": 20.5, "v2": 24.13, "v3": 28.69, "n0": 21.03, "n1": 27.77, "lsl": 15.5, "ltl": 21.49, "fb": 29.47,
+      "nrc": 37.69, "t0": 8.75, "t1": 0.29, "dig": 25.33, "late": 30.77, "x4": 17.4, "st0": 1.7, "st1": 0.37, "pb0": 31.99,
+      "pb1": 2.92, "pp0": 15.21, "pp1": 1.18, "pp2": -3.87, "k0": 17.59, "k1": 1.29, "bb": 46.15, "l2": 29.57, "ls": 24.55,
+      "wk0": 30.48, "wk1": 32.93, "lk": 25.49, "bb0": 15.46, "ltt": 39.97, "ps0": 31.47, "ps1": 5.71, "oh0": 27.55, "ne": 16.35,
+      "rn0": 46.06, "rn1": 0.04}
+ENG, RLE = "avvv", "vaaavaaa"
 
 
 def build(T):
@@ -81,8 +91,9 @@ def build(T):
         return {"ap": T[name][:] if B is None else T[name][:, :, B, :], "acc": acc, "off": [], "n": 256 if B is None else 32,
                 "w": 4, "ps": False, "rows": 128}
 
-    def X(name, h=None):
-        return {"ap": T[name][:] if h is None else T[name][h:8:2, :], "acc": [], "off": [], "n": 0, "w": 4, "ps": False, "rows": 0}
+    def X(name, h=None, cols=None):
+        return {"ap": T[name][:, cols[0]:cols[1]] if cols else T[name][:] if h is None else T[name][h:8:2, :],
+                "acc": [], "off": [], "n": 0, "w": 4, "ps": False, "rows": 0}
 
     def IND(win, off):
         return {"ap": win["ap"].indirect(off["ap"]), "acc": win["acc"], "off": off["acc"], "n": 16 * off["n"], "w": win["w"], "ps": False}
@@ -114,7 +125,8 @@ def build(T):
             if both and not (views[0]["ps"] or views[1]["ps"]):
                 f *= 2
             c = 0.03 + max(64, n * f) * CY
-        ops.append({"q": q, "fn": fn, "rd": rd, "wr": wr, "grp": grp, "c": c, "due": due[0]})
+        ops.append({"q": q, "fn": fn, "rd": rd, "wr": wr, "grp": grp, "c": c, "long": bool(views and views[0]["off"]),
+                    "due": None if q == "p" else due[0]})
 
     def u(x):
         return x["ap"] if isinstance(x, dict) else x
@@ -144,12 +156,12 @@ def build(T):
         f = fn if fn is not None else (AF.Copy if (not isinstance(bias, dict) and bias == 0.0) else AF.Identity)
         add("a", lambda g: g.scalar.activation(u(o), u(i), f, u(bias), u(scale)), [o], [i, scale, bias])
 
-    def either():
-        a = ops.pop()
+    def either(n=2):
+        same = [ops.pop() for _ in range(n - 1)] + [ops[-1]]
         v = ops[-1]
-        v["alt"] = {"v": v["fn"], "a": a["fn"]}
-        v["cq"] = {"v": v["c"], "a": a["c"]}
-        v["rd"] = v["rd"] + [x for x in a["rd"] if x not in v["rd"]]
+        v["alt"] = {a["q"]: a["fn"] for a in same}
+        v["cq"] = {a["q"]: a["c"] for a in same}
+        v["rd"] = [x for a in same for x in a["rd"]]
 
     def on(q):
         if q:
@@ -167,6 +179,7 @@ def build(T):
         ts(o, i, bias, OP.add, 0.0, OP.max)
         act(o, i, 1.0, bias, AF.Relu)
         either()
+        ops[-1]["lax"] = True
 
     def relu2(o, i):
         ts(o, i, -2.0, OP.mult, 0.0, OP.max)
@@ -201,12 +214,13 @@ def build(T):
                 add("a", lambda g, o=o, i=i: g.scalar.dma_start(u(o), u(i)), [o], [i], "d%d" % k)
         return "d%d" % k
 
-    def send(k, land, src, step=1):
-        ops.append({"q": "p", "send": (k, u(land), u(src)), "step": step, "rd": src["acc"], "wr": [], "grp": "lo%d" % k,
-                    "c": src["n"] * src["w"] * 128 / LINK})
+    def send(k, src, *to):
+        ops.append({"q": "p", "send": (k, u(src), [u(x) for x, s in to]), "steps": [s for x, s in to], "rd": src["acc"], "wr": [],
+                    "grp": "lo%d" % k, "c": src["n"] * src["w"] * 128 / LINK})
 
-    def arrive(k, land, step=1):
-        ops.append({"q": "x", "step": -step, "rd": [], "wr": land["acc"], "grp": "ar%d" % k, "c": 0.0, "after": "lo%d" % k})
+    def arrive(k, *to):
+        ops.append({"q": "x", "steps": [s for x, s in to], "rd": [], "wr": [a for x, s in to for a in x["acc"]], "grp": "ar%d" % k,
+                    "c": 0.0, "after": "lo%d" % k})
 
     def C(k):
         return R("col", k, k + 1)
@@ -227,20 +241,42 @@ def build(T):
         return [(R(dst, off, off + 4096, 1, (16 * h + r, 128, 32)), R(src, 256 * k + 128 * h, 256 * k + 128 * h + 128))
                 for k, r in which for h in (0, 1)]
 
-    def gat(dst, k, win, lst, q=None):
-        copy(R(dst[0], dst[1] + 512 * k, dst[1] + 512 * k + 512), IND(win, R(lst, 32 * k, 32 * k + 32)))
+    def gat(dst, k, n, win, lst, q=None):
+        copy(R(dst[0], dst[1] + 512 * k, dst[1] + 512 * (k + n)), IND(win, R(lst, 32 * k, 32 * (k + n))))
         on(q)
 
+    def cut(name, e=None):
+        out, k = [], 0
+        for n in CUT[name]:
+            if e is None or k // 4 == e:
+                out.append((k, int(n)))
+            k += int(n)
+        return out
+
     def fill(name, a, b, c):
-        for a0 in range(a, b, 512):
-            iota(R(name, a0, min(b, a0 + 512)), [[0, min(b, a0 + 512) - a0]], c, 0)
+        iota(R(name, a, b), [[0, b - a]], c, 0)
 
-    def spread(name, a, b, c):
-        fill(name, a, a + 512, c)
-        dma("s", [(R(name, a0, min(b, a0 + 512)), R(name, a, a + min(512, b - a0))) for a0 in range(a + 512, b, 512)])
+    def diag(name, w, a=0):
+        asel(R(name, a, a + 128), R("ZR"), [[-1, 128]], OP.not_equal, w, 0, 1)
+        if name not in ("IF", "IB"):
+            ts(R(name, a, a + 128), R("IB"), w, OP.mult)
+            act(R(name, a, a + 128), R("IB"), w)
+            either(3)
+            on("v")
 
-    def diag(name, w):
-        asel(R(name), R("ZR"), [[-1, 128]], OP.not_equal, w, 0, 1)
+    def one_row(name, pat, src, r, s, w):
+        entries(R(name), pat, {(r, s): w})
+        ts(R(name), R(src), XMc(r), OP.mult, w, OP.mult)
+        either()
+        on("v")
+
+    def entries(o, pat, ws):
+        src = R("ZB", 0, o["n"])
+        for (r, s), w in ws.items():
+            asel(o, src, pat, OP.not_equal, float(w), -r - 1000 * (s or 0), 1)
+            src = o
+
+    BY_G, BY_GS, BY_ROW, WIDE = [[-16, 8]], [[-16, 8], [1000, 16]], [[-16, 8], [0, 16]], [[-16, 9], [1000, 16]]
 
     def behind(k0, grp):
         for op in ops[k0:]:
@@ -248,11 +284,11 @@ def build(T):
 
     P1, P8, P16 = (0, 1, 1), (0, 8, 1), (0, 16, 1)
     cX, cG, cINV, cPW, cN, cTH, cA, cNX, c4X, cN0, cB56, c256 = range(12)
-    E1 = {0: 16, 1: 1, 2: 4096, 4: -16, 5: -1, 6: 1, 7: -64}
-    cW = {n: 16 + k for k, n in enumerate(("E1", "SC", "B0", "U", "T", "C", "M56", "E2", "A", "R3"))}
-    cB1, cB2, cR2, cD6, cST = range(28, 33)
+    E1 = {0: 16, 1: 1, 3: 64, 4: -16, 5: -1, 7: -64}
+    E2 = {0: -16, 1: -1, 2: -1, 3: -64, 4: 16, 5: 1, 6: 1, 7: 64}
+    cM56, cSC, cB0, cB1, cB2, cPV = range(16, 22)
     sSC, sC, sN, sNE, sE1, sE2 = 0, 8, 16, 32, 40, 48
-    rONE, r64, r256, rS8, rB16, rIO, rX0, rX4 = 0, 128, 256, 384, 512, 768, 1024, 1152
+    rONE, r64, r7, rS8, rB16, rIO, rX0, rX4, rM45, rM2 = 0, 128, 256, 384, 512, 768, 1024, 1152, 1280, 1408
 
     def row(k, a=0, n=128):
         return R("RW", k + a, k + a + n, 1, P1)
@@ -270,10 +306,12 @@ def build(T):
     def PC(e, k):
         return R("P%d" % (4 + e), 128 * k, 128 * k + 128)
 
-    def lin2bars(ps, src, base, sel, n=1):
+    def lin2bars(ps, src, base, sel, n=1, first=None):
         name, a = ps["acc"][0][0], ps["acc"][0][1] // 4
+        if first:
+            mm(ps, first[0], first[1], True, False)
         for s in range(16):
-            mm(R(name, a + s, a + 128 * n, 16), R(src, base + s, base + 2048, 16), R("sel", sel, sel + 8 * n))
+            mm(R(name, a + s, a + 128 * n, 16), R(src, base + s, base + 2048, 16), R("sel", sel, sel + 8 * n), not first, not first or s == 15)
 
     def to_offers(o, w, src, more=()):
         mms(o, [(R(w, 15 - x, 143 - x), R(src, x, 256, 16)) for x in range(16)] + list(more))
@@ -289,13 +327,14 @@ def build(T):
             due[0] = None
             mm(ps, R("SXD", 16 - k, 144 - k) if k < 16 else R("SX", 0, 128), o, False, k == 16)
 
-    def last_tones(aoff):
-        copy(R("S5"), IND(R("XA", aoff, aoff + AW), R("LS", 64, 80)))
-        cp(IND(R("XA", BB, BB + AW), R("LS", 64, 80)), R("S5"))
-
-    def dig(dst, k, s):
-        (cp if s["acc"][0][0][0] == "i" else copy)(R(dst, 512 * k, 512 * k + 256), s)
-        tt(R(dst, 512 * k + 256, 512 * k + 512), s, R(dst, 512 * k, 512 * k + 256), OP.subtract)
+    def dig(dst, k, s, f, bank):
+        if f is not s:
+            cp(f, s)
+        copy(R(dst, 512 * k, 512 * k + 256), f)
+        on("a")
+        mms(R(bank, 0, 256), [(R("IF"), f), (R("IN"), R(dst, 512 * k, 512 * k + 256))])
+        copy(R(dst, 512 * k + 256, 512 * k + 512), R(bank, 0, 256))
+        on("a")
 
     g0 = dma("s", [(R("i2", 128 * h, 128 * h + 128), X("bt", h)) for h in (0, 1)])
     dma("a", [(R("ism", 0, 1, 1, P8), X("pn")), (R("ism", 4, 5, 1, P8), X("th")), (R("i5", 0, 256, 1, P8), X("bl"))])
@@ -309,6 +348,7 @@ def build(T):
     act(R("PT", 2064, 4112), R("PT", 0, 2048))
     ms(R("ONE"), 1.0)
     ms(R("ZR"), 0.0)
+    ms(R("ZB"), 0.0)
     ms(R("OF"), 1.0)
     ms(R("TN", 0, 16), 0.0)
     iota(R("ism", 8, 9), [[0, 1]], 0, 1, True)
@@ -329,9 +369,9 @@ def build(T):
     diag("IF", 1.0)
     diag("IB", 1.0)
     asel(R("DF"), R("IF"), [[-1, 128]], OP.not_equal, -1.0, 1, 1)
-    asel(R("DF"), R("DF"), [[-16, 8], [1000, 16]], OP.not_equal, 0.0, 1, 1)
+    asel(R("DF"), R("DF"), BY_GS, OP.not_equal, 0.0, 1, 1)
     asel(R("G8", 0, 128, 1, P8), R("OF", 0, 128, 1, P8), [[1, 8], [0, 16]], OP.is_equal, 0.0, 0, -1)
-    asel(R("BLK"), R("ONE", 0, 128), [[-16, 8], [0, 16]], OP.is_ge, 0.0, 0, 1)
+    asel(R("BLK"), R("ONE", 0, 128), BY_ROW, OP.is_ge, 0.0, 0, 1)
     asel(R("BLK"), R("BLK"), [[16, 8], [0, 16]], OP.is_ge, 0.0, 15, -1)
     act(R("BLS"), R("BLK"), -1.0 / 8192)
     asel(R("TI"), R("BLS"), [[1, 128]], OP.is_ge, 0.0, 0, -1)
@@ -342,8 +382,9 @@ def build(T):
     act(R("SXD", 1, 144), R("SXF", 145, 288))
     act(R("TB"), R("TI"), 2.0 ** 26)
     asel(R("TB"), R("TB"), [[-1, 128]], OP.not_equal, 2.0 ** 20 - 8192, 0, 1)
-    for k, c in ((rONE, 1.0), (r64, 64.0), (r256, 256.0)):
+    for k, c in ((rONE, 1.0), (r64, 64.0), (r7, 7.5), (rM45, -4.5 * BIG / 64)):
         ms(row(k), c)
+    ms(row(rM2, 0, 16), -2.0)
     iota(row(rS8), [[0, 8], [8192, 16]])
     act(row(rB16, 0, 256), R("IO", 0, 256, 1, P1), 16.0)
     act(row(rIO, 0, 256), R("IO", 0, 256, 1, P1))
@@ -352,168 +393,160 @@ def build(T):
     asel(R("K16", 0, 128, 1, P16), R("OF", 0, 128, 1, P16), [[0, 8], [1, 16]], OP.is_equal, 0.0, 0, -1)
     ms(R("WT", 0, 3, 1, P16), 0.0)
     asel(R("WT", 1, 2, 1, P16), R("OF", 0, 1, 1, P16), [[0, 1]], OP.is_ge, 0.0, 4, -1)
-    for k, ws in enumerate((E1, {5: 2.0 ** -19, 6: 2.0 ** -14}, {5: 64, 6: 2176, 7: 64, 8: 1})):
+    for k, ws in enumerate(({5: 1, 6: 1}, {5: 2.0 ** -19, 6: 2.0 ** -14}, {5: 128, 6: 4224, 7: 64})):
         for r, w in ws.items():
             asel(R("WT", k, k + 1, 1, P16), R("WT", k, k + 1, 1, P16), [[0, 1]], OP.not_equal, float(w), -r, 1)
     mm(R("P7", 0, 3), R("K16", 0, 128, 1, P16), R("WT", 0, 3, 1, P16))
-    act(R("col", 16, 19), R("P7", 0, 3))
-    for n, r, w, b in (("U", 1, 1.0, 0), ("T", 3, 1.0, 2), ("M56", 6, 1.0, 5), ("A", 6, -1.0, 5), ("R3", 8, -128.0, 6)):
-        act(C(cW[n]), XMc(r), w, XMc(b))
-    act(C(cW["C"]), XMc(4), 16.0)
-    act(C(cW["E2"]), C(cW["E1"]), -1.0, C(cW["R3"]))
-    act(C(cW["E2"]), XMc(3), -1.0, C(cW["E2"]))
+    act(R("col", cM56, cM56 + 3), R("P7", 0, 3))
     act(R("sel", sSC, sSC + 8), R("PH"))
-    act(R("sel", sC, sC + 8), R("PH"), C(cW["C"]))
-    for n, w in (("IN", -1.0), ("I8", -8192.0), ("IAN", -float(AW)), ("IG", HUGE), ("IS", 2.0 ** -19), ("IR", -2.0 ** -14), ("IA", float(AW))):
-        diag(n, w)
+    entries(R("sel", sC, sC + 8), BY_G, {(4, None): 16})
+    for n, w, a in (("IN", -1.0, 0), ("I8", -8192.0, 0), ("IAN", -float(AW), 0), ("IG", HUGE, 0), ("IS", 2.0 ** -19, 0),
+                    ("IR", -2.0 ** -14, 0), ("IA", float(A1 - BB), 0), ("IS", -1.0 / 16, 128), ("IG", 2.0 ** 14 - 2.0 ** 19, 128),
+                    ("IR", 2.0 ** -14, 128), ("IG", -16.0, 256), ("IFN", -1.0, 0)):
+        diag(n, w, a)
     for n in ("NQ", "NE", "C16", "NV", "Z2", "LTT"):
         ms(R(n), 0.0)
     ts(R("B0"), R("i4"), 1.0, OP.add)
-    send(6, R("B1"), R("B0"), -1)
-    send(7, R("B2"), R("B0"), -2)
+    send(6, R("B0"), (R("B1"), -1), (R("B2"), -2))
     ts(Q("X3"), R("i2"), 16.0, OP.add)
     for B in range(8):
         turn(R("f3", B, 256, 8), Q("X3", B))
     cp(R("SB"), R("f3"))
-    send(0, R("RB"), R("SB"))
-    due[0] = 12.0
-    dig("S0", 0, R("i3"))
-    due[0] = None
-    send(1, R("R0"), R("S0", 0, 512))
-    due[0] = 5.0
+    send(0, R("SB"), (R("RB"), 1))
+    due[0] = 2.0
     mm(R("P5", 0, 256), R("DF"), R("f3"))
     ts(R("NW"), R("P5", 0, 256), 0.0, OP.not_equal)
     mms(R("P5", 256, 512), [(R("IF"), R("f3")), (R("TB"), R("NW"))])
     copy(R("NU"), R("P5", 256, 512), -2.0 ** 20)
     for k in range(16):
         o = R(("YO", "ZO")[k % 4 // 2], 256 * (k % 2), 256 * (k % 2) + 256)
-        due[0] = 7.0 + 0.6 * k
+        due[0] = TM["st0"] + TM["st1"] * k
         relu(o, R("NU"), 8192.0 * (k + 1))
         due[0] = None
         mm(R("P4", 0, 256), R("SXF", 159 - k, 287 - k) if k < 15 else R("SXF", 0, 128), o, k == 0, k == 15)
     act(C(cB56), C(cX), -8192.0)
     ts(R("LK"), R("P4", 0, 256), C(cB56), OP.add, 4111.0, OP.min)
     act(R("G8B", 0, 128, 1, P8), R("G8", 0, 128, 1, P8))
-    asel(R("G8B", 128, 256, 1, P8), R("G8B", 0, 128, 1, P8), [[0, 8], [1, 16]], OP.is_equal, 0.0, -3, 0)
+    asel(R("G8B", 128, 256, 1, P8), R("G8B", 0, 128, 1, P8), [[0, 8], [1, 16]], OP.is_equal, 0.0, -2, 0)
     cp(R("M2", 0, 256, 1, P8), R("i5", 0, 256, 1, P8))
     mm(R("P6", 256, 512), R("G8B", 0, 128, 1, P8), R("M2", 0, 256, 1, P8))
     ts(R("VI"), R("P6", 256, 512), C(cX), OP.is_gt)
     tt(R("VI"), R("VI"), R("NW"), OP.mult)
     act(C(cN0), C(cX), 16.0)
-    act(R("BASE", 0, 16), R("IO", 0, 16), 256.0, C(cN0))
-    act(R("BASE", 16, 32), R("BASE", 0, 16), 1.0, 15.0)
+    act(R("BASE", 128, 144), R("IO", 0, 16), 256.0, C(cN0))
+    act(R("sm", 48, 64), R("BASE", 128, 144), 1.0, 15.0)
     to_offers(R("P6", 16, 32), "SX", "VI")
-    tt(R("sm", 0, 16), R("P6", 16, 32), R("BASE", 16, 32), OP.add)
+    tt(R("sm", 0, 16), R("P6", 16, 32), R("sm", 48, 64), OP.add)
     cp(R("LS", 64, 80), R("sm", 0, 16))
     mms(R("P7", 256, 512), [(R("G8B", 128, 256, 1, P8), R("M2", 0, 256, 1, P8)), (row(rX0), row(rIO, 0, 256))])
-    act(C(cNX), XMc(3), -1.0)
+    act(C(cNX), XMc(1), 128.0)
+    act(C(cNX), XMc(2), 127.0, C(cNX))
     act(R("LTT", 1, 257), R("P7", 256, 512), 1.0, C(cNX))
     act(C(cNX), C(cX), -1.0)
-    spread("XA", BB - 16, BB + AW + 16, 99)
+    fill("XA", BB - 16, BB + 1088, 99)
     for a in (A0, XT1 - 16, XT1 + 4096):
         iota(R("XA", a, a + 16), [[0, 16]], 99, 0)
     due[0] = 3.0
     cp(R("sm", 16, 24, 4, P8), R("ism", 0, 8, 4, P8))
     mm(R("P2", 0, 2), R("G8", 0, 128, 1, P8), R("sm", 16, 24, 4, P8))
     act(C(cN), R("P2", 0, 1), 8192.0, -4097.0)
-    act(R("f2"), R("JW"), -8192.0, C(cN))
-    tt(R("f0"), R("i0"), R("f2"), OP.min)
+    act(R("P2", 256, 512), R("JW"), -8192.0, C(cN))
+    tt(R("f0"), R("i0"), R("P2", 256, 512), OP.min)
     ts(R("LT_"), R("f0"), -1.0, OP.max, 16.0, OP.add)
-    tt(R("f1"), R("i1"), R("f2"), OP.min)
+    tt(R("f1"), R("i1"), R("P2", 256, 512), OP.min)
     ts(R("LU"), R("f1"), -1.0, OP.max, 16.0, OP.add)
-    due[0] = 9.0
+    due[0] = TM["x4"]
     ts(R("f1"), R("f1"), -1.0, OP.max)
     for B in range(8):
         turn(Q("X4", B), R("f1", B, 256, 8))
-    dig("S1", 0, Q("X4"))
     due[0] = None
     act(R("col", cTH, cTH + 1, 1, P8), R("sm", 20, 21, 1, P8), 1.0, 8192.0)
     act(R("TM", 0, 128, 1, P8), R("G8", 0, 128, 1, P8), R("col", cTH, cTH + 1, 1, P8))
     asel(R("TM", 0, 128, 1, P8), R("TM", 0, 128, 1, P8), [[0, 8], [1, 16]], OP.not_equal, -4096.0, -15, 0)
+    act(R("TMB", 0, 128, 1, P8), R("TM", 0, 128, 1, P8))
+    tt(R("TMB", 128, 256, 1, P8), R("TM", 0, 128, 1, P8), R("TMB", 0, 128, 1, P8), OP.subtract)
     dma("s", unstage("PT", 16, "ID", [(0, 2), (1, 3)]) + unstage("PT", 16, "B0", [(0, 4)]))
-    arrive(6, R("B1"), -1)
-    arrive(7, R("B2"), -2)
-    dma("s", unstage("PT", 16, "B1", [(0, 5)]) + unstage("PT", 16, "B2", [(0, 6)]))
+    arrive(6, (R("B1"), -1), (R("B2"), -2))
+    gp = dma("s", unstage("PT", 16, "B1", [(0, 5)]) + unstage("PT", 16, "B2", [(0, 6)]))
+    fill("WE", 0, 1024, 0)
+    k0 = len(ops)
+    dma("s", [(R("XA", a, a + 1104), R("XA", BB - 16, BB + 1088)) for a in range(BB + 1088, A1, 1104)])
+    dma("s", [(R("WE", a, a + 1024), R("WE", 0, 1024)) for a in range(1024, 12288, 1024) if a < 4096 or a >= 8192])
+    behind(k0, gp)
     dma("s", [(R("RL", 4096, 8192), R("TN", 16, 4112))])
-    dma("s", [(R("RL", 8192, 12288), R("TN", 16, 4112))])
 
     def late_constants():
         act(R("sel", sNE, sNE + 8), R("PH"), BIG)
-        act(R("sel", sE1, sE1 + 8), R("PH"), C(cW["E1"]))
-        act(R("sel", sE2, sE2 + 8), R("PH"), C(cW["E2"]))
-        act(R("sel", sN, sN + 8), R("PH"), C(cW["U"]))
-        act(R("sel", sN + 8, sN + 16), R("PH"), C(cW["T"]))
         iota(R("MK"), [[0, 8], [1, 16]])
         act(R("MK"), R("MK"), 1.0, C(cNX), AF.Abs)
         act(R("MK"), R("MK"), -1.0, 1.0, AF.Relu)
         iota(R("IOC"), [[-16, 256]], 4080)
+        ts(R("IOC"), R("IO"), -16.0, OP.mult, 4080.0, OP.add)
+        act(R("IOC"), R("IO"), -16.0, 4080.0)
+        either(3)
+        iota(R("ism", 16, 24), [[16, 8]], 15, 0, True)
+        cp(R("LS", 80, 88), R("ism", 16, 24))
+        act(C(cB56), C(cM56), -113.0, 128.0)
+        act(C(c256), C(cM56), 16.0)
+        act(R("sm", 24, 32), R("IO", 0, 8), C(c256), C(cB56))
+        cp(R("LS", 88, 96), R("sm", 24, 32))
+        keep, due[0] = due[0], TM["pw"]
+        ms(R("K2"), 0.5)
+        asel(R("K2"), R("K2"), [[0, 16], [1, 16]], OP.not_equal, 0.0, 0, 0)
+        asel(R("K1"), R("ZB"), [[0, 16], [1, 16]], OP.not_equal, 65536.0, 0, 0)
+        scan(R("K1"), R("K2"), R("K1"), 0.0, OP.mult, OP.add)
+        tt(R("sm", 32, 48), R("K1", 0, 16), R("XM"), OP.mult)
+        add("v", lambda g: g.vector.tensor_reduce(u(C(cPW)), u(R("sm", 32, 48)), AX, OP.add), [C(cPW)], [R("sm", 32, 48)])
+        ts(R("WM"), R("SX"), C(cPW), OP.mult, 0.5, OP.mult)
+        asel(R("K1", 0, 256, 1, P16), R("K1", 0, 256, 1, P16), [[-1, 16], [0, 16]], OP.is_ge, 1.0, 0, 1)
+        asel(R("K1", 0, 256, 1, P16), R("K1", 0, 256, 1, P16), [[1, 16], [0, 16]], OP.is_ge, float(2 ** 20), 0, -1)
+        act(R("K2", 0, 128, 1, P16), R("K16", 0, 128, 1, P16))
+        mm(R("P7", 0, 256), R("K2", 0, 128, 1, P16), R("K1", 0, 256, 1, P16))
+        act(R("THT"), R("P7", 0, 256))
+        due[0] = keep
+        iota(R("SS", 0, 1), [[0, 1]], 2 ** 21)
+        iota(R("smb", 64, 65), [[0, 1]])
+        iota(R("WK", 0, 1), [[0, 1]])
         asel(R("UT"), R("OF"), [[1, 128]], OP.is_gt, 0.0, 0, -1)
         asel(R("TS"), R("BLS"), [[1, 128]], OP.is_gt, 0.0, 0, -1)
         asel(R("TC"), R("BLS"), [[-1, 128]], OP.is_ge, 0.0, 0, 1)
         asel(R("TD"), R("BLS"), [[-1, 128]], OP.is_gt, 0.0, 0, 1)
         asel(R("KP"), R("ONE", 0, 128), [[0, 8], [1, 16]], OP.not_equal, 0.0, 0, 0)
         asel(R("RST"), R("ZR"), [[0, 8], [1, 16]], OP.not_equal, NONE, 0, 0)
-        spread("WE", 0, 4096, 0)
-        dma("s", [(R("WE", 8192, 12288), R("WE", 0, 4096))])
-        act(C(cB56), C(cW["A"]), -16.0)
-        act(R("BVW"), R("BLK"), C(cB56))
+        one_row("BVW", BY_ROW, "BLK", 5, None, -16.0)
         act(R("SXN"), R("SX"), -1.0)
-        act(R("SX3"), R("SX"), XMc(3))
-        act(C(cD6), XMc(6), -2.0 ** 19)
-        act(R("D6"), R("IB"), C(cD6))
-        act(C(cR2), XMc(7), 1.0 / 64)
-        for k, c in enumerate((XMc(4), C(cW["A"]), C(cR2), C(cW["R3"]))):
-            act(R("NR", 128 * k, 128 * k + 128), R("SX", 15 - k, 143 - k), c)
-        act(C(cB1), XMc(7), 64.0, C(cW["B0"]))
-        act(C(cB2), XMc(7), 128.0, C(cW["B0"]))
-        act(C(cN0), C(cX), 16.0, 1.0)
-        iota(R("ism", 16, 24), [[16, 8]], 15, 0, True)
-        cp(R("LS", 80, 88), R("ism", 16, 24))
-        act(C(cB56), C(cW["M56"]), -113.0, 128.0)
-        act(C(c256), C(cW["M56"]), 16.0)
-        act(R("sm", 24, 32), R("IO", 0, 8), C(c256), C(cB56))
-        cp(R("LS", 88, 96), R("sm", 24, 32))
-        act(R("BASE", 80, 96), R("BASE", 0, 16), 1.0, 16.0 * 257)
-        act(R("BASE", 16, 32), R("BASE", 0, 16), 1.0, 8192.0 - 63)
-        act(R("BASE", 0, 16), R("BASE", 0, 16), 1.0, 16384.0 - 64)
-        iota(R("BASE", 32, 48), [[0, 16]], 4096 + 8192)
-        iota(R("BASE", 48, 80), [[0, 32]])
-        asel(R("K2"), R("ONE"), [[0, 16], [1, 16]], OP.not_equal, 0.0, 0, 0)
-        act(R("K1"), R("K2"), -65536.0, 65536.0)
-        act(R("K2"), R("K2"), 0.5)
-        scan(R("K1"), R("K2"), R("K1"), 0.0, OP.mult, OP.add)
-        tt(R("sm", 32, 48), R("K1", 0, 16), R("XM"), OP.mult)
-        add("v", lambda g: g.vector.tensor_reduce(u(C(cPW)), u(R("sm", 32, 48)), AX, OP.add), [C(cPW)], [R("sm", 32, 48)])
-        act(C(cPW), C(cPW), 0.5)
-        act(R("WM"), R("SX"), C(cPW))
-        if any(SIGNS):
-            act(R("ID", 0, 144), R("WM"), 0.5)
-            act(R("ID", 144, 288), R("WM"), -0.5)
-            iota(R("SXF", 0, 257), [[-16, 257]], 4088)
-        asel(R("K1", 0, 256, 1, P16), R("K1", 0, 256, 1, P16), [[-1, 16], [0, 16]], OP.is_ge, 1.0, 0, 1)
-        asel(R("K1", 0, 256, 1, P16), R("K1", 0, 256, 1, P16), [[1, 16], [0, 16]], OP.is_ge, float(2 ** 20), 0, -1)
-        act(R("K2", 0, 128, 1, P16), R("K16", 0, 128, 1, P16))
-        mm(R("P7", 0, 256), R("K2", 0, 128, 1, P16), R("K1", 0, 256, 1, P16))
-        act(R("THT"), R("P7", 0, 256))
-        iota(R("SS", 0, 1), [[0, 1]], 2 ** 21)
-        iota(R("smb", 64, 65), [[0, 1]])
-        iota(R("WK", 0, 1), [[0, 1]])
+        one_row("SX3", WIDE, "SX", 2, 15, 1.0)
+        one_row("D6", BY_GS, "IB", 6, 6, -2.0 ** 19)
+        asel(R("NR"), R("ONE", 0, 128), [[-1, 128]], OP.is_equal, 0.0, -4, 1)
+        asel(R("NR"), R("NR"), [[0, 8], [-1, 16]], OP.is_ge, 0.0, 3, 0)
+        act(C(cB1), XMc(7), 64.0, C(cB0))
+        act(C(cB2), XMc(7), 128.0, C(cB0))
+        act(C(cN0), C(cX), 16.0, 2049.0)
+        act(R("col", cPV, cPV + 3), R("IO", 1, 4), 4096.0, C(cX))
+        act(C(c4X), C(cX), 16.0, 1.0)
+        iota(R("BASE", 0, 32), [[-8191, 2], [256, 16]], 16383)
+        act(R("BASE", 0, 32), R("BASE", 0, 32), 1.0, C(c4X))
+        iota(R("BASE", 96, 128), [[AW - 257, 2], [16, 16]], 257)
+        act(R("BASE", 96, 128), R("BASE", 96, 128), 1.0, C(cX))
+        iota(R("BASE", 32, 48), [[0, 16]], 256 + 8192)
+        ms(R("BASE", 48, 64), 4103.5 + 8192)
+        iota(R("BASE", 64, 96), [[0, 32]])
+        for a, ws in ((sE1, E1), (sE2, E2), (sN, {0: 1, 1: 1}), (sN + 8, {2: 1, 3: 1})):
+            entries(R("sel", a, a + 8), BY_G, {(r, None): w for r, w in ws.items()})
 
     def last_constants():
-        act(R("SXU"), R("SX"), C(cW["U"]))
-        act(R("SXT"), R("SX"), C(cW["T"]))
-        act(C(cST), C(cW["E1"]), C(cW["U"]))
-        act(C(cST), XMc(2), 4096.0, C(cST))
-        act(R("BST"), R("BLK"), C(cST))
-        act(R("BL3"), R("BLK"), XMc(3))
-        act(C(c4X), C(cX), 4.0)
+        entries(R("SXU"), WIDE, {(0, 15): 1, (1, 15): 1})
+        entries(R("SXT"), WIDE, {(2, 15): 1, (3, 15): 1})
+        entries(R("BST"), BY_ROW, {(0, None): 16, (1, None): 1, (3, None): 64})
+        entries(R("BL3"), BY_ROW, {(2, None): 1})
+        act(C(c4X), C(cX), 4.0, 512.0)
+        act(C(cINV), C(cX), 1.0, -128.0)
 
     for v in range(3):
         last = v == 2
-        xt, xo, ak, an = (XT0, XT1, A0, A1) if v % 2 == 0 else (XT1, XT0, A1, A0)
+        xt, xo, an = (XT0, XT1, A1) if v % 2 == 0 else (XT1, XT0, A0)
         pv = 4096 * (v + 1)
         win = R("XA", A0, A1) if v % 2 == 0 else R("XA", BB, XT1)
-        helped, signs = HELP[v], SIGNS[v]
 
         def at(t, t0=None):
             due[0] = None if t is None else (t0 if v == 0 and t0 is not None else BEGIN[v] + t)
@@ -522,21 +555,21 @@ def build(T):
                 at(None)
                 mm(PA(e, 1), R("f0", 128 * e, 128 * e + 128), R("IF"))
                 copy(H("NT", e), PA(e, 1))
-                for k in range(4 * e, 4 * e + 4):
-                    at(0, (10.0, 13.6, 14.5, 14.6, 15.4, 15.5, 20.0, 20.9)[k])
-                    gat(("W", pv), k, R("PT"), "LT_")
+                for k, n in cut("pp", e):
+                    at(0, TM["pp0"] + TM["pp1"] * k + TM["pp2"] * e)
+                    gat(("W", pv), k, n, R("PT"), "LT_")
             else:
-                arrive(4 * v + e, H("SR%d" % (v - 1), e))
-                for k in range(4 * e, 4 * e + 4):
+                arrive(4 * v + e, (H("SR%d" % (v - 1), e), 1))
+                for k, n in cut("rl", e):
                     at((0.0, 0.0, 0.9, 0.9, 1.8, 1.8, 2.7, 3.9)[k])
-                    gat(("W", pv), k, R("RL", 0, pv + 16), "SR%d" % (v - 1), "vavavaav"[k])
+                    gat(("W", pv), k, n, R("RL", 0, pv + 16), "SR%d" % (v - 1), RLE[k])
                 at(None)
                 lin2bars(PA(e, 0), "W", pv + 2048 * e, sN, 2)
                 at(2.6 + 3 * e)
                 copy(H("NT", e), PA(e, 1))
-                on("v")
+                on(ENG[e])
                 copy(H("NU", e), PA(e, 0))
-                on("v")
+                on(ENG[2 + e])
             at(2.9 + 3 * e, 8.0)
             tt(H("NQ", e, 1, 127), R("P%d" % e, 129, 256), H("NT", e, 0, 127), OP.not_equal)
             relu2(H("NV", e, 0, 127), R("P%d" % e, 129, 256))
@@ -553,120 +586,131 @@ def build(T):
             lin2bars(PB(e, 0), "W", pv + 2048 * e, sC)
             copy(H("C16", e, 1), PB(e, 0))
             on("a")
-            mms(PB(e, 1), [(R("OF", 0, 128, 1, P8), R("TM", 0, 128, 1, P8)), (R("I8"), H("NQ", e, 1)), (R("I8"), H("NV", e))])
+            mms(PB(e, 1), [(R("ONE", 0, 128, 1, P8), R("TMB", 0, 128, 1, P8)), (R("ONE", 0, 128, 1, P8), R("TMB", 128, 256, 1, P8)),
+                           (R("I8"), H("NQ", e, 1)), (R("I8"), H("NV", e))])
             copy(H("THR", e), PB(e, 1))
             on("a")
             mms(PB(e, 2), [(R("IB"), H("C16", e)), (R("IN"), H("C16", e, 1)), (R("IB"), H("NQ", e))])
-            mms(PB(e, 3), [(R("IN"), H("C16", e)), (R("IB"), H("C16", e, 1)), (row(r64), row(r256))])
         for e in (0, 1):
-            for k in range(4 * e, 4 * e + 4):
-                at(3.7 + 0.9 * k + 0.7 * e, 10.0 + 0.9 * k + 2.9 * e)
-                gat(("XA", xt), k, R("TN"), "LT_", "a")
-                at(4.8 + 1.1 * k, 11.0 + 0.9 * k + 2.9 * e)
-                tt(R("T2", 512 * k, 512 * k + 512), IND(R("TN"), R("LU", 32 * k, 32 * k + 32)), R("XA", xt + 512 * k, xt + 512 * k + 512), OP.mult)
+            for k, n in cut("t", e):
+                a, b = 512 * k, 512 * (k + n)
+                at(3.7 + 0.9 * k + 0.7 * e, TM["t0"] + TM["t1"] * k)
+                gat(("XA", xt), k, n, R("TN"), "LT_", "a")
+                at(4.8 + 1.1 * k, TM["t0"] + 1 + TM["t1"] * k)
+                tt(R("T2", a, b), IND(R("TN"), R("LU", a // 16, b // 16)), R("XA", xt + a, xt + b), OP.mult)
             at(None)
             lin2bars(PC(e, 0), "T2", 2048 * e, sSC)
         if v == 0:
-            for k in range(8):
-                at(0, (16.4, 17.3, 21.2, 21.8, 22.1, 22.7, 23.0, 23.6)[k])
-                gat(("XA", A0 + 16), k, R("TN"), "LK")
-            at(0, 30.0)
+            for k, n in cut("k"):
+                at(0, TM["k0"] + TM["k1"] * k)
+                gat(("XA", A0 + 16), k, n, R("TN"), "LK")
+            at(0, TM["dig"])
+            x4 = Q("X4")
+            dig("S1", 0, x4, x4, "P0")
+            dig("S0", 0, R("i3"), R("f2"), "P1")
+            send(1, R("S0", 0, 512), (R("R0"), 1))
+            at(0, TM["late"])
             late_constants()
             at(None)
             dma("s", stage("S1", "W", pv, [(2, 2), (3, 3), (4, 5), (5, 6)]))
-            send(2, R("R1"), R("S1"))
+            send(2, R("S1"), (R("R1"), 1))
             dma("s", unstage2("W", pv, "S1", [(0, 0), (1, 1)]))
-            arrive(2, R("R1"))
+            arrive(2, (R("R1"), 1))
             dma("s", unstage2("RL", 4096, "R1", [(0, 0), (1, 1)]) + unstage("RL", 4096, "R1", [(k, k) for k in range(2, 6)]))
-            arrive(0, R("RB"))
-            for k in range(8):
-                at(0, 30.5 + 1.5 * k)
-                gat(("RL", 0), k, R("PT"), "RB", "a")
+            arrive(0, (R("RB"), 1))
+            for k, n in cut("pb"):
+                at(0, TM["pb0"] + TM["pb1"] * k)
+                gat(("RL", 0), k, n, R("PT"), "RB", "a")
             at(None)
-            arrive(1, R("R0"))
+            arrive(1, (R("R0"), 1))
             dma("s", unstage2("RL", 0, "R0", [(0, 0), (1, 1)]))
             for n, a in (("RL", 8192), ("RL", 12288), ("W", 16384)):
                 act(R(n, a, a + 16), R("ONE", 0, 16), C(cA))
+            at(0, TM["bb0"])
+            copy(R("S5"), IND(R("XA", A0, BB), R("LS", 64, 80)))
+            cp(IND(R("XA", BB, BB + AW), R("LS", 64, 80)), R("S5"))
         elif v == 1:
             dma("s", stage("S1", "W", pv, [(0, 0), (1, 1), (2, 2), (3, 3), (4, 5)]))
-            send(3, R("R2"), R("S1", 0, 1280))
-            arrive(3, R("R2"))
+            send(3, R("S1", 0, 1280), (R("R2"), 1))
+            arrive(3, (R("R2"), 1))
             dma("s", unstage("RL", 8192, "R2", [(k, k) for k in range(5)]))
-        at(-0.5, 24.5)
-        last_tones(ak)
+        if v > 0:
+            k0 = len(ops)
+            dma("s", [(rows("WE", r, w), R("ZB")) for w in (0, 8192) for r in range(8)])
+            if v == 1:
+                dma("s", [(R("W", 0, 4096), R("TN", 16, 4112))])
+            for op in ops[k0:]:
+                op["rd"] = op["rd"] + R("SR%d" % (v - 1))["acc"]
+            if v == 1:
+                dma("s", unstage2("W", 0, "S0", [(k, k) for k in range(4)]))
         for e in (0, 1):
-            at(10.0 + 4.3 * e, 22.0 + 2 * e)
+            at(10.0 + 4.3 * e, TM["ne"] + 2 * e)
             tt(H("NE", e, 1), PC(e, 0), H("THR", e), OP.is_lt)
             scan(H("Z", e), PB(e, 2), H("NE", e), 0.0, OP.add, OP.mult)
             at(None)
             mms(PC(e, 3), [(H("C16", e, 1), R("IB")), (H("NE", e, 1), R("IAN" if v % 2 == 0 else "IA")), (H("Z", e), R("IF"))])
-            at(10.9 + 4.3 * e, 23.0 + 2 * e)
+            at(10.9 + 4.3 * e, TM["ne"] + 1 + 2 * e)
             ts(H("LI", e), PC(e, 3), float(AW) if v % 2 == 0 else 0.0, OP.add)
-            scan(H("f0", e), PB(e, 3), H("NE", e), 0.0, OP.add, OP.mult)
-            act(H("THR", e), H("NE", e), HUGE, 4 * BIG)
+            scan(H("NW", e), R("ONE", 0, 128), H("NE", e), 0.0, OP.add, OP.mult)
             if not last:
-                act(H("NW", e), H("NQ", e), 1.0, -16.0)
                 at(12.0 + 4.3 * e, 25.5 + 2 * e)
-                scan(H("TK", e), H("NW", e), H("NE", e), 0.0, OP.add, OP.mult)
+                scan(H("KK", e), H("NQ", e), H("NE", e), 0.0, OP.add, OP.mult)
             at(None)
-            mms(PC(e, 2), [(row(r64), row(rS8)), (row(r64), row(r64)), (R("IN"), H("C16", e, 1)), (R("IG"), H("NE", e, 1)), (R("IF"), H("f0", e))])
+            mms(PC(e, 2), [(row(r64), row(rS8)), (row(r64), row(r64)), (row(rONE), row(r7)), (R("IN"), H("C16", e, 1)),
+                           (R("IG", 0, 128), H("NE", e, 1)), (R("IG", 128, 256), H("NW", e)), (R("IFN"), H("Z", e))])
         for e in (0, 1):
-            for k in range(4 * e, 4 * e + 4):
-                o, x, keys = R("T2", 512 * k, 512 * k + 512), R("XA", xt + 512 * k, xt + 512 * k + 512), IND(win, R("LI", 32 * k, 32 * k + 32))
-                if k in helped:
-                    at(12.3 + 0.9 * helped.index(k))
-                    act(R("XA", xo + 512 * k, xo + 512 * k + 512), keys)
-                    keys = R("XA", xo + 512 * k, xo + 512 * k + 512)
+            for k, n in cut("c", e):
+                a, b = 512 * k, 512 * (k + n)
+                o, x, keys = R("T2", a, b), R("XA", xt + a, xt + b), IND(win, R("LI", a // 16, b // 16))
+                if k in HELP[v]:
+                    at(12.3 + 0.9 * HELP[v].index(k))
+                    act(R("XA", xo + a, xo + b), keys)
+                    keys = R("XA", xo + a, xo + b)
                 at(13.7 + 0.9 * k + 0.5 * e + (k > 4))
                 tt(o, keys, x, OP.not_equal)
             at(None)
-            lin2bars(PC(e, 1), "T2", 2048 * e, sNE)
+            lin2bars(PC(e, 1), "T2", 2048 * e, sNE, 1, (row(r64), row(rM45)))
             at(17.9 + 4.5 * e)
-            scan(H("Z", e), H("THR", e), PC(e, 1), 4 * BIG, OP.min, OP.max)
+            scan(H("Z", e), H("NE", e), PC(e, 1), 0.0, OP.mult, OP.max)
             tt(H("f1", e), PC(e, 2), H("Z", e), OP.add)
             scan(H("Z2", e), R("RST"), H("f1", e), 0.0, OP.max, OP.min)
             tt(H("f1", e), IND(H("Z2", e, 0, HW), R("LS", 80, 88)), R("MK"), OP.mult)
             km = R("P6", 8 * e, 8 * e + 8)
             at(None)
             mm(km, H("f1", e), R("PH"))
-            t1, c16, t2, r16 = R("sm", 48 + 8 * e, 56 + 8 * e), R("smb", 8 * e, 8 * e + 8), R("smb", 16 + 8 * e, 24 + 8 * e), R("smb", 32 + 8 * e, 40 + 8 * e)
+            t1, t0 = R("sm", 48 + 8 * e, 56 + 8 * e), R("sm", 160 + 8 * e, 168 + 8 * e)
+            c16, t2, r16 = (R("smb", a + 8 * e, a + 8 * e + 8) for a in (0, 16, 32))
             at(19.3 + 4.7 * e)
             ts(t1, km, 1.5 * 2.0 ** 37, OP.add, 1.5 * 2.0 ** 37, OP.subtract)
-            tt(c16, km, t1, OP.subtract)
+            ts(t0, km, 1.5 * 2.0 ** 27, OP.add, 1.5 * 2.0 ** 27, OP.subtract)
+            tt(c16, t0, t1, OP.subtract)
             ts(R("LS", 8 * e, 8 * e + 8), c16, -1.0 / 16, OP.mult, 256.0, OP.add)
             for y in range(8 * e, 8 * e + 8):
-                if y in signs:
-                    o = 272 * (signs.index(y) % 7)
-                    at(19.8 + 4.8 * e + 0.37 * len([z for z in signs if 8 * e <= z < y]))
-                    act(R("OH", o, o + 257), R("SXF", 0, 257), -1.0, R("smb", y, y + 1), AF.Sign)
-                    at(None)
-                    mm(R("P7", 0, 256), R("ID", 15 - y, 143 - y), R("OH", o + 1, o + 257), y == 0, False)
-                    mm(R("P7", 0, 256), R("ID", 159 - y, 287 - y), R("OH", o, o + 256), False, y == 15)
-                    continue
-                o = 2048 + 256 * (y % 8)
-                at(21.8 + 2.8 * e + 0.01 * y)
-                ts(R("OH", o, o + 256), R("IOC"), R("smb", y, y + 1), OP.is_equal)
-                at(None)
-                mm(R("P7", 0, 256), R("WM", 15 - y, 143 - y), R("OH", o, o + 256), y == 0, y == 15)
+                o = R("OH", 256 * y, 256 * y + 256)
+                at((TM["oh0"], 24.6)[e] + 0.01 * y)
+                ts(o, R("IOC"), R("smb", y, y + 1), OP.is_equal)
+                mm(R("P7", 0, 256), R("WM", 15 - y, 143 - y), o, y == 0, y == 15)
             at(22.2 + 3.6 * e)
             ts(t2, t1, 1.5 * 2.0 ** 42, OP.add, 1.5 * 2.0 ** 42, OP.subtract)
             tt(r16, t1, t2, OP.subtract)
-            at(18.8 + 4.6 * e)
+            if not last:
+                tt(R("smb", 88 + 8 * e, 96 + 8 * e), km, t0, OP.subtract)
+            at((18.8, TM["v1"])[e])
             act(H("f2", e), IND(H("Z2", e, 0, HW), R("LS", 88, 96)))
             mm(R("P2", 256 + 128 * e, 384 + 128 * e), H("f2", e), R("IF"))
-            act(H("S5", e), R("P2", 256 + 128 * e, 384 + 128 * e), 2.0 ** -19, 64.0)
-            at(19.7 + 4.8 * e)
+            act(H("S5", e), R("P2", 256 + 128 * e, 384 + 128 * e), 2.0 ** -19, 128.0)
+            at((19.7, TM["v2"])[e])
             act(H("LG", e), IND(R("LTT", 0, 257), R("LS", 8 * e, 8 * e + 8)))
             mms(R("P2", 128 * e, 128 * e + 128), [(H("f2", e), R("IF")), (row(rX4), row(rIO, 128 * e)), (R("IB"), H("LG", e)), (R("D6"), H("S5", e))])
-            at(20.5 + 5.0 * e)
-            act(H("VAL", e), R("P2", 128 * e, 128 * e + 128), C(cW["SC"]), C((cW["B0"], cB1, cB2)[v]))
+            at((20.5, TM["v3"])[e])
+            act(H("VAL", e), R("P2", 128 * e, 128 * e + 128), C(cSC), C((cB0, cB1, cB2)[v]))
             if not last:
                 ps = R("P3", 256 * e + 128, 256 * e + 256)
-                at(22.5 + 4.5 * e)
-                mms(ps, [(H("TK", e), R("IF")), (R("BVW"), H("VAL", e))])
+                at((TM["n0"], TM["n1"])[e])
+                mms(ps, [(H("KK", e), R("IB")), (H("NW", e), R("IG", 256, 384)), (R("BVW"), H("S5", e))])
                 relu(H("NC", e), ps, C(cN0))
                 on("a")
-                positions(e, BEGIN[v] + 26.5 + 2.2 * e)
+                positions(e, BEGIN[v] + TM["ps0"] + TM["ps1"] * e)
                 act(H("f3", e), R("P3", 256 * e, 256 * e + 128), 1.0, 16.0 if v % 2 == 0 else 16.0 + AW)
         if not last:
             at(14.0)
@@ -675,12 +719,18 @@ def build(T):
         at(26.0)
         act(R("SS", 1, 257), R("P7", 0, 256))
         at(None)
-        to_offers(R("P6", 16, 32), "SX3", "LG", [(R("IR"), r16)])
-        mm(R("P4", 0, 80), R("IF"), R("BASE", 0, 80), True, False)
-        for a, l, r in ((0, "IS", t2), (16, "IS", t2), (0, "IR", r16), (32, "IN", c16)):
-            mm(R("P4", a, a + 16), R(l), r, False, False)
-        at(28.0)
-        mms(R("P5", 256, 512), [(R("NR", 128 * k, 128 * k + 128), R("VAL")) for k in range(4)])
+        to_offers(R("P6", 16, 32), "SX3", "LG", [(R("IR", 0, 128), r16), (row(r64), row(rM2, 0, 16))])
+        mm(R("P4", 0, 96), R("IF"), R("BASE", 0, 96), True, False)
+        for a, l, r in ((0, R("IS", 0, 128), t2), (16, R("IS", 0, 128), t2), (16, R("IR", 128, 256), r16), (32, R("IS", 128, 256), c16), (48, R("IN"), c16)):
+            mm(R("P4", a, a + 16), l, r, False, False)
+        if not last:
+            mm(R("P4", 48, 64), R("IN"), R("smb", 88, 104), False, False)
+            mms(R("P6", 32, 48), [(R("IF"), R("BASE", 128, 144)), (R("IS", 0, 128), t2), (R("IR", 128, 256), r16)])
+            at(TM["l2"])
+            cp(R("LS", 96, 112), R("P6", 32, 48))
+            act(R("M2"), IND(R("XA", xt, xt + 4096), R("LS", 96, 112)))
+        at(TM["nrc"])
+        mm(R("P5", 256, 512), R("NR"), R("VAL"))
         act(R("NRC"), R("P5", 256, 512))
         at(26.6)
         tt(R("VI"), IND(R("SS", 0, 257), R("LS", 0, 16)), R("THT"), OP.is_ge)
@@ -688,26 +738,27 @@ def build(T):
         at(27.9)
         ts(tk, R("P7", 256, 272), 0.0, OP.is_equal, -8192.0, OP.mult)
         tt(R("smb", 65, 81), R("P6", 16, 32), tk, OP.mult)
-        for a in (0, 0, 16, 32):
+        for a in (0, 0, 16, 32, 48):
             mm(R("P4", a, a + 16), R("IB"), tk, False, False)
-        for a, l, b in ((48, "TS", 65), (48, "TC", 64), (64, "TI", 65), (64, "TD", 64)):
+        for a, l, b in ((64, "TS", 65), (64, "TC", 64), (80, "TI", 65), (80, "TD", 64)):
             mm(R("P4", a, a + 16), R(l), R("smb", b, b + 16), False, l == "TD")
         at(28.7)
-        scan(R("sm", 64, 96), R("KP", 0, 32), R("P4", 48, 80), 0.0, OP.mult, OP.add)
+        scan(R("sm", 64, 96), R("KP", 0, 32), R("P4", 64, 96), 0.0, OP.mult, OP.add)
         tt(R("sm", 96, 128), R("P4", 0, 32), R("sm", 64, 96), OP.add)
         cp(R("LS", 16, 48), R("sm", 96, 128))
         cp(IND(R("WE"), R("LS", 16, 32)), R("VAL"))
         at(30.0)
         cp(IND(R("WE", 8192, 24576), R("LS", 32, 48)), R("VAL"))
-        at(28.6 if last else 30.1)
-        tt(R("sm", 128, 144), R("P4", 32, 48), R("BASE", 80, 96), OP.min)
-        ts(R("LS", 48, 64), R("sm", 128, 144), 1.0 / 16, OP.mult)
+        at(TM["lsl"] if last else TM["ls"])
+        tt(R("sm", 128, 160), R("P4", 32, 64), R("BASE", 96, 128), OP.min)
+        cp(R("LS", 48, 80), R("sm", 128, 160))
         sl = "SL%d" % (v % 2)
         at(None)
         for w, sel in ((0, sE1), (8192, sE2)):
             for e in (0, 1):
                 if w == 0:
                     mm(PA(e, 0), R("TS", 0, 128, 1, P1), R("TD", 0, 128, 1, P1), True, False)
+                at(30.6 + 0.6 * e + w / 8192)
                 for s in range(16):
                     mm(R("P%d" % e, s, 128, 16), R("WE", w + 2048 * e + s, w + 2048 * e + 2048, 16), R("sel", sel, sel + 8), False, w > 0 and s == 15)
         for e in (0, 1):
@@ -715,59 +766,64 @@ def build(T):
             scan(H("Z2", e), R("KP"), PA(e, 0), 0.0, OP.mult, OP.add)
             copy(H("f1", e), IND(H("Z2", e, 0, HW), R("LS", 80, 88)))
             at(None)
-            mms(PA(e, 1), [(row(rONE), row(rB16, 128 * e))] + [(row(r64), row(r64))] * (v + 1) + [(H("Z2", e), R("IF"))]
-                + [(H("f1", 0), R("OF"))] * e + [(H("f1", e), R("UT"))])
+            mms(PA(e, 1), [(row(rONE), row(rB16, 128 * e)), (H("Z2", e), R("IF"))] + [(H("f1", 0), R("OF"))] * e + [(H("f1", e), R("UT"))])
             at(33.6 + 0.8 * e)
-            ts(H(sl, e), PA(e, 1), C(cX), OP.add, pv + 4096.0, OP.min)
+            ts(H(sl, e), PA(e, 1), C(cPV + v), OP.add, pv + 4096.0, OP.min)
             if not last:
-                send(4 * v + 4 + e, H("SR%d" % v, e), H(sl, e))
+                send(4 * v + 4 + e, H(sl, e), (H("SR%d" % v, e), 1))
         if not last:
-            at(31.7)
-            cp(IND(R("WK"), R("LS", 48, 64)), R("f3"))
-            at(33.2)
+            for e in (0, 1):
+                at(TM["wk%d" % e])
+                cp(IND(R("WK"), R("LS", 48 + 8 * e, 56 + 8 * e)), H("f3", e))
+            at(TM["bb"])
+            cp(IND(R("XA", BB, A1), R("LS", 64, 80)), R("M2"))
+            at(TM["lk"])
             cp(R("LK"), R("WK", 1, 257))
-            for k in range(8):
-                at(33.7 + 0.5 * k)
-                gat(("XA", an + 16), k, R("XA", *((XT0, BB) if v == 0 else (A1, XT1 + 4112))), "LK")
-            at(38.0)
+            for k, n in cut("rn"):
+                at(TM["rn0"] + TM["rn1"] * k)
+                gat(("XA", an + 16), k, n, R("XA", *((XT0, BB) if v == 0 else (A1, XT1 + 4112))), "LK")
+            at(TM["ltt"])
             cp(IND(R("LTT"), R("LS", 48, 64)), R("NRC"))
             at(None)
-            k0 = len(ops)
-            fill("WE", 0, 4096, 0)
-            fill("WE", 8192, 12288, 0)
-            behind(k0, "lo%d" % (4 * v + 5))
             if v == 0:
+                k0 = len(ops)
+                dig("S0", 1, R("i2"), R("f0"), "P7")
+                behind(k0, "lo5")
                 last_constants()
-                fill("W", 0, 4096, 0)
-                dig("S0", 1, R("i2"))
-                behind(len(ops) - 2, "lo5")
-                dma("s", unstage2("W", 0, "S0", [(k, k) for k in range(4)]))
         else:
-            at(28.65)
+            at(TM["ltl"])
             cp(IND(R("LTT"), R("LS", 48, 64)), R("NRC"))
             at(None)
             mm(R("P7", 256, 512), R("BL3"), R("LTT", 1, 257))
             act(R("M2"), R("P7", 256, 512), -4.0, C(c4X), AF.Relu)
             mms(R("P7", 0, 256), [(R("BST"), R("LTT", 1, 257)), (R("IA"), R("M2"))])
-            ts(R("LK"), R("P7", 0, 256), C(cX), OP.add, 16384.0, OP.min)
-            for k in range(8):
-                at(31.5 + 0.9 * k)
-                gat(("T1", 0), k, R("W"), "LK", "a")
+            ts(R("LK"), R("P7", 0, 256), C(cINV), OP.add, 16384.0, OP.min)
+            for k, n in cut("fb"):
+                at(TM["fb"] + 0.9 * k)
+                gat(("T1", 0), k, n, R("W"), "LK", "a")
             at(None)
             for f, w in ((0, "SXU"), (1, "SXT")):
                 mms(R("P%d" % (6 + f), 0, 256), [(R(w, 15 - x, 143 - x), R("T1", 256 * x, 256 * x + 256)) for x in range(16)])
                 copy(R("ZO", 256 * f, 256 * f + 256), R("P%d" % (6 + f), 0, 256))
-            dma("a", [(X("zu"), R("ZO", 0, 256)), (X("zt"), R("ZO", 256, 512))])
+                dma("s", [(X(("zu", "zt")[f]), R("ZO", 256 * f, 256 * f + 256))])
             for q in range(4):
-                for k in (2 * q, 2 * q + 1):
+                for k, n in [x for x in cut("fp") if x[0] // 2 == q]:
                     at(35.0 + 0.7 * k)
-                    gat(("XA", XT1), k, R("W"), sl, "v" if k < 5 else None)
+                    gat(("XA", XT1), k, n, R("W"), sl, "v" if k < 5 else None)
                 at(None)
-                for f, w in ((0, "SXU"), (1, "SXT")):
+                if q == 1:
+                    lin2bars(R("P2", 0, 128), "XA", XT1, sN, 2)
+                    copy(R("NT"), R("P2", 0, 256))
+                    for f in (0, 1):
+                        mm(R("P3", 128 * f, 128 * f + 128), H("NT", f), R("IF"))
+                        copy(R("YO", 256 * f, 256 * f + 128), R("P3", 128 * f, 128 * f + 128))
+                for f, w in ((0, "SXU"), (1, "SXT")) if q > 1 else ():
                     o = R("P%d" % (2 + q), 64 * f, 64 * f + 64)
                     mms(o, [(R(w, 15 - s, 143 - s), R("XA", XT1 + 1024 * q + s, XT1 + 1024 * q + 1024, 16)) for s in range(16)])
                     copy(R("YO", 256 * f + 64 * q, 256 * f + 64 * q + 64), o)
-            dma("s", [(X("yu"), R("YO", 0, 256)), (X("yt"), R("YO", 256, 512))])
+                if q:
+                    a, b = 64 * q * (q > 1), 64 * q + 64
+                    dma("s", [(X(("yu", "yt")[f], None, (a, b)), R("YO", 256 * f + a, 256 * f + b)) for f in (0, 1)])
     return ops
 
 
@@ -843,21 +899,20 @@ def order(ops, lanes):
                 total["q" + op["q"]] = total.get("q" + op["q"], 0) + 1
                 op["val"] = total["q" + op["q"]]
         else:
-            total[op["grp"]] = total.get(op["grp"], 0) + (16 if op["grp"][0] == "d" else lanes[op["q"]][op["step"]])
+            total[op["grp"]] = total.get(op["grp"], 0) + (16 if op["grp"][0] == "d" else lanes(op))
     return seq, need, total
 
 
 HOP, LAT_D, LAT_R, ISSUE, DMA, LINK = 0.15, 2.0, 2.5, 0.3, 200e3, 60e3
-SEED, HEAT, THETA, LEAN, END, AHEAD = 1, 0.3, 0.15, 0.5, 135.0, 1.0
+SEED, ROUNDS, HEAT, EVEN, FREE, SLOW, QUICK = 1, 10000, 0.04, 0.001, 1, 0.8, 0.67
+SEND, THETA, LEAN, END, AHEAD = 10.0, 0.2, 0.5, 135.0, 1.0
 
 
 def plan(ops):
-    def delay(m, n):
-        return 0.0 if ops[m]["q"] == "t" and ops[n]["q"] == "t" else HOP
     N = len(ops)
     kind = [(op["grp"] or " ")[0] for op in ops]
-    edge = [[(m, delay(m, n)) for m in sorted(op["pre"] - op["soft"])] + [(m, None) for m in sorted(op["soft"])]
-            for n, op in enumerate(ops)]
+    edge = [[(m, 0.0 if ops[m]["q"] == op["q"] == "t" else HOP) for m in sorted(op["pre"] - op["soft"])]
+            + [(m, None) for m in sorted(op["soft"])] for op in ops]
     back = [[] for _ in ops]
     for n in range(N):
         for m, d in edge[n]:
@@ -870,32 +925,21 @@ def plan(ops):
             whole.append({"p": (0.0, ISSUE, LAT_R + op["c"])})
         else:
             whole.append({q: (0.0, c, 0.0) for q, c in sorted(op.get("cq", {op["q"]: op["c"]}).items())})
-    least = [sum(min(w.values())) for w in whole]
-    gate = {op["grp"]: n for n, op in enumerate(ops) if op["grp"]}
-    marks = [gate[k] for k in ("ar5", "ar9")]
+    marks = [n for n, op in enumerate(ops) if op["grp"] in ("ar5", "ar9")]
 
-    def walk(shape, boost):
+    def walk(shape):
         tail = [0.0] * N
         for n in range(N - 1, -1, -1):
-            t = 0.0
-            for k, d in back[n]:
-                if tail[k] > t:
-                    t = tail[k]
-            t += least[n] + HOP
+            t = max([tail[k] for k, d in back[n]] + [0.0]) + sum(min(whole[n].values())) + HOP
             if ops[n].get("due") is not None:
                 t = END - ops[n]["due"]
-            tail[n] = t + boost[n]
+            tail[n] = t + (SEND if kind[n] == "l" else 0.0)
         left = [len(e) for e in edge]
         pool = {q: {} for q in "vatpd"}
-        start, end, on, at, held = [0.0] * N, [0.0] * N, [""] * N, {q: 0.0 for q in "vatpd"}, {}
-        prev = {}
+        start, end, on, at = [0.0] * N, [0.0] * N, [""] * N, {q: 0.0 for q in "vatpd"}
 
         def enter(n):
-            t = 0.0
-            for m, d in edge[n]:
-                x = end[m] + d if d is not None else start[m] + 0.01
-                if x > t:
-                    t = x
+            t = max([end[m] + d if d is not None else start[m] + 0.01 for m, d in edge[n]] + [0.0])
             if "x" in shape[n]:
                 start[n], end[n], on[n] = t, t, "x"
                 leave(n)
@@ -914,26 +958,19 @@ def plan(ops):
         while any(pool.values()):
             t, q = min([(max(at[q], min(p.values())), q) for q, p in pool.items() if p])
             p = pool[q]
-            n = f = None
-            for m, r in p.items():
-                if r <= t + AHEAD:
-                    w = (tail[m] - (LEAN if q == "v" and len(shape[m]) > 1 else 0.0), -m)
-                    if n is None or w > n:
-                        n = w
-                    if r <= t and (f is None or w > f):
-                        f = w
-            n, f = -n[1], -f[1]
-            if p[n] > t and t + shape[f][q][1] + tail[n] <= max(p[n] + tail[n], p[n] + shape[n][q][1] + tail[f]) + THETA:
+            rank = {m: (tail[m] - (LEAN if q == "v" and len(shape[m]) > 1 else 0.0), -m) for m, r in p.items() if r <= t + AHEAD}
+            n = max(rank, key=rank.get)
+            f = max([m for m in rank if p[m] <= t], key=rank.get)
+            if p[n] > t and t + shape[f][q][1] + tail[n] <= (max(p[n] + tail[n], p[n] + shape[n][q][1] + tail[f])
+                                                           + (1.0 if "lax" in ops[n] else THETA)):
                 n = f
             x, c, y = shape[n][q]
-            if p[n] < at[q] - 1e-9:
-                held[n] = prev[q]
             t = max(t, p[n])
-            start[n], end[n], on[n], at[q], prev[q] = t - x, t + c + y, q, t + c, n
+            start[n], end[n], on[n], at[q] = t - x, t + c + y, q, t + c
             for r in shape[n]:
                 del pool[r][n]
             leave(n)
-        return max(end) + 0.2 * sum(end[n] for n in marks), start, end, on, held
+        return start, on
 
     rnd = [SEED]
 
@@ -941,48 +978,160 @@ def plan(ops):
         rnd[0] = (rnd[0] * 1103515245 + 12345) % 2147483648
         return (rnd[0] >> 8) % k
 
-    shape = [{op["first"]: w[op["first"]]} if "first" in op else w for op, w in zip(ops, whole)]
-    boost = [0.0] * N
-    top = now = walk(shape, boost)
+    start, on = walk([{op["first"]: w[op["first"]]} if "first" in op else w for op, w in zip(ops, whole)])
+    seq = sorted(range(N), key=lambda n: (start[n], n))
+    on = [ops[n]["q"] if kind[n] in "dl" else on[n] for n in range(N)]
+    hard = [[(m, d) for m, d in e if d is not None] for e in edge]
+    cost = [0.0 if kind[n] in "dl" else whole[n][on[n]][1] for n in range(N)]
+
+    quick = [QUICK if op.get("long") else 1.0 for op in ops]
+    reach = [N] * N
+
+    def run(seq, k0, k1, end, slow):
+        free = {}
+        for n in seq[k0 - 1::-1] if k0 else ():
+            if on[n] not in free:
+                free[on[n]] = end[n + N]
+            if kind[n] in "dl" and kind[n] not in free:
+                free[kind[n]] = end[n]
+            if len(free) == 8:
+                break
+        old, end = end, list(end)
+        moved, k2 = set("vap"), k1
+        for j in range(k0, N):
+            n = seq[j]
+            q = on[n]
+            t = free.get(q, 0.0)
+            for m, d in hard[n]:
+                if end[m] + d > t:
+                    t = end[m] + d
+            k = kind[n]
+            if k == " ":
+                t += cost[n] * (1.3 if q == "p" else quick[n]) if slow else cost[n]
+                end[n] = end[n + N] = free[q] = t
+                if t != old[n] or j <= k2:
+                    moved.add(q)
+                    if t != old[n] and reach[n] > k1:
+                        k1 = reach[n]
+                elif moved:
+                    moved.discard(q)
+                elif j > k1:
+                    break
+                continue
+            if k == "a":
+                end[n] = end[n + N] = t
+                free[q] = 0.0
+            elif k == "d":
+                end[n + N] = free[q] = t + 0.06
+                end[n] = free[k] = max(t + LAT_D + 0.5 * slow, free.get(k, 0.0)) + ops[n]["c"] * (1 + 0.4 * slow)
+            else:
+                t += (0.7 + 4.0 * (k not in free)) if slow else ISSUE
+                end[n + N] = free[q] = t
+                end[n] = free[k] = max(t + LAT_R + slow, free.get(k, 0.0)) + ops[n]["c"] * (1 + slow)
+            if end[n] != old[n] and reach[n] > k1:
+                k1 = reach[n]
+            if k != "a":
+                if end[n] != old[n] or end[n + N] != old[n + N] or j <= k2:
+                    moved.update((q, k))
+                else:
+                    moved.difference_update((q, k))
+        return end
+
+    def worth(a, b):
+        return max(a[:N]) + 0.2 * sum(a[n] for n in marks) + SLOW * max(b[:N]) + EVEN * sum(a[:N])
+
+    now = [run(seq, 0, N, [0.0] * (2 * N), s) for s in (0, 1)]
+    best = level = worth(*now)
+    top = (list(seq), list(on), now[0])
+    pairs = None
     for k in range(ROUNDS):
-        span, start, end, on, held = now
-        n = (marks + [end.index(max(end))])[draw(len(marks) + 1)]
-        pairs = []
-        while n is not None:
-            if n in held:
-                pairs.append((n, held[n]))
-                n = held[n]
-            else:
-                n = max([(end[m], m) for m, d in edge[n] if d is not None] + [(-1.0, None)], key=lambda x: x[0])[1]
-        s2, b2 = list(shape), list(boost)
-        for _ in range(1 + draw(2)):
-            n, m = pairs[draw(len(pairs))]
-            move = draw(5)
-            x = m if len(whole[m]) > 1 and (draw(2) or len(whole[n]) == 1) else n
-            if move >= 3 and len(whole[x]) > 1:
-                q = "v" if on[x] == "a" else "a"
-                s2[x] = {q: whole[x][q]}
-            elif move % 2:
-                b2[m] -= (1 + draw(30)) * 0.1
-            else:
-                b2[n] += (1 + draw(30)) * 0.1
-        new = walk(s2, b2)
-        if new[0] <= span + HEAT * (1.0 - k / ROUNDS) * draw(100) / 100:
-            now, shape, boost = new, s2, b2
-            if new[0] < top[0]:
-                top = new
-    PLAN["dbg"] = (ops, top[1], top[2], edge, top[3])
-    PLAN["seq"], PLAN["on"], PLAN["span"] = sorted(range(N), key=lambda n: (top[1][n], n)), top[3], max(top[2])
-    PLAN["marks"] = [top[2][n] for n in marks]
+        if pairs is None:
+            place, prev, last = [0] * N, [None] * N, {}
+            for j, n in enumerate(seq):
+                place[n], prev[n], last[on[n]], reach[n] = j, last.get(on[n]), n, 0
+                for m, d in hard[n]:
+                    reach[m] = j
+            pairs = []
+            for end in (now[0], now[0], now[1]):
+                n = (marks + [end.index(max(end[:N]))])[draw(len(marks) + 1)]
+                while n is not None:
+                    t, m = -1.0, None
+                    for x, d in hard[n]:
+                        if end[x] + d > t:
+                            t, m = end[x] + d, x
+                    if prev[n] is not None and on[n] != "x" and end[prev[n] + N] > t + 1e-9:
+                        m = prev[n]
+                        pairs.append((n, m))
+                    n = m
+        n, m = pairs[draw(len(pairs))]
+        move = draw(8)
+        if draw(10) < FREE:
+            n = seq[draw(N)]
+            m = prev[n]
+            if m is None or on[n] == "x":
+                continue
+        for _ in range(draw(3) * draw(3)):
+            m = prev[m] if prev[m] is not None else m
+        x = None
+        if move < 2 and len(whole[n]) + len(whole[m]) > 2:
+            x = m if len(whole[m]) > 1 and (move or len(whole[n]) == 1) else n
+            was = on[x]
+            on[x] = [q for q in whole[x] if q != was][draw(len(whole[x]) - 1)]
+            cost[x] = whole[x][on[x]][1]
+            new, k0, k1 = seq, place[x], place[x]
+        elif move % 2:
+            k0 = place[m]
+            k1 = min(N - 1, place[n] + draw(2) * draw(40))
+            late = {m}
+            for y in seq[k0 + 1:k1 + 1]:
+                if any(z in late for z, d in edge[y]):
+                    late.add(y)
+            if n in late:
+                continue
+            part = seq[k0:k1 + 1]
+            new = seq[:k0] + [y for y in part if y not in late] + [y for y in part if y in late] + seq[k1 + 1:]
+        else:
+            k0, k1 = place[m], place[n]
+            soon = {n}
+            for y in seq[k1 - 1:k0 - 1 if k0 else None:-1]:
+                if any(z in soon for z, d in back[y]):
+                    soon.add(y)
+            if m in soon:
+                continue
+            part = seq[k0:k1 + 1]
+            new = seq[:k0] + [y for y in part if y in soon] + [y for y in part if y not in soon] + seq[k1 + 1:]
+        a = run(new, k0, k1, now[0], 0)
+        bar = level + HEAT * (1.0 - k / ROUNDS) * draw(100) / 100
+        b = run(new, k0, k1, now[1], 1) if worth(a, now[1]) <= bar + 0.5 else None
+        if b is not None and worth(a, b) <= bar:
+            seq, now, level, pairs = new, [a, b], worth(a, b), None
+            if level < best:
+                best, top = level, (list(seq), list(on), a)
+        elif x is not None:
+            on[x] = was
+            cost[x] = whole[x][on[x]][1]
+    seq, on, end = top
+    PLAN["seq"], PLAN["on"], PLAN["span"], PLAN["marks"] = seq, on, max(end[:N]), [end[n] for n in marks]
+    PLAN["dbg"] = (ops, [end[n] - whole[n].get(on[n], (0, ops[n]["c"]))[1] for n in range(N)], end[:N], edge, on)
 
 
 def rank_program(g, core, T, topo):
     rank = T.rank_of(core)
     if rank is None:
         return
-    peer = {k: T.cores[(rank + k) % len(T.cores)] for k in (-2, -1, 1, 2)}
-    lanes = {"p": {k: len(topo.engines(core, c)) for k, c in peer.items()},
-             "x": {k: len(topo.engines(c, core)) for k, c in peer.items()}}
+
+    def peer(r):
+        return T.cores[r % len(T.cores)]
+
+    def mask(r, steps):
+        m = -1
+        for s in steps:
+            m &= topo.mask(peer(r), peer(r + s))
+        return m
+
+    def lanes(op):
+        senders = [rank] if op["q"] == "p" else [rank - s for s in op["steps"]]
+        return sum(bin(mask(r, op["steps"])).count("1") for r in senders)
     ops = build(T)
     seq, need, total = order(ops, lanes)
     queue = {"v": g.vector, "a": g.scalar, "t": g.tensor, "p": g, "s": g.sync}
@@ -996,10 +1145,14 @@ def rank_program(g, core, T, topo):
             else:
                 queue[op["q"]].wait_ge(T.sem[key], total[key])
         if "send" in op:
-            k, land, src = op["send"]
-            dst = peer[op["step"]]
-            rid, pid = topo.addr(dst)[:2]
-            g.remote_dma(land, src, T.sem["ar%d" % k], T.sem["lo%d" % k], pid, rid, topo.mask(core, dst))
+            k, src, lands = op["send"]
+            to = [topo.addr(peer(rank + s)) for s in op["steps"]]
+            if len(to) == 1:
+                g.remote_dma(lands[0], src, T.sem["ar%d" % k], T.sem["lo%d" % k], to[0][1], to[0][0], mask(rank, op["steps"]))
+            else:
+                g.remote_dma_fused([RemoteDMATransfer(dst_ids=[DstId(rid=a[0], pnc=a[1]) for a in to],
+                                                      dma_engine_mask=mask(rank, op["steps"]), remote_sem=T.sem["ar%d" % k],
+                                                      srcs=[src], dsts=lands)], local_sem=T.sem["lo%d" % k])
         elif op["grp"] is not None:
             op["fn"](g).then_inc(T.sem[op["grp"]], 16)
         elif n in need:

from concourse.mybir import AluOpType as OP, ActivationFunctionType as AF, AxisListType
from concourse.bass import DstId, RemoteDMATransfer

AX = AxisListType.X
F32, BF, I32, U16 = "float32", "bfloat16", "int32", "uint16"
SZ = {F32: 4, BF: 2, I32: 4, U16: 2}
AW = 4128
XT0, A0, BB, A1, XT1 = 0, 4096, 4096 + AW, 4352 + 2 * AW, 4352 + 3 * AW
BIG, HUGE = float(2 ** 24), float(2 ** 27)
NONE = 15 * 2.0 ** 19 + 4103.5
HW = 144


def _s(shape, dt):
    return ("sbuf", [128] + list(shape), dt)


SCRATCH = {
    "TN": _s([4112], BF), "XA": _s([XT1 + 4112], BF), "T1": _s([4096], BF),
    "W": _s([16400], BF), "RL": _s([12304], BF), "WE": _s([24576], BF),
    "S0": _s([1024], BF), "S1": _s([1536], BF), "R0": _s([512], BF), "R1": _s([1536], BF), "R2": _s([1280], BF),
    "B0": _s([256], BF), "B1": _s([256], BF), "B2": _s([256], BF), "ID": _s([512], BF),
    "SB": _s([256], U16), "RB": _s([256], U16),
    "SR0": _s([256], U16), "SR1": _s([256], U16), "SL0": _s([256], U16), "SL1": _s([256], U16),
    "i0": _s([256], I32), "i1": _s([256], I32), "i2": _s([256], I32), "i3": _s([256], I32), "i4": _s([256], I32),
    "i5": _s([256], I32), "X3": _s([2, 8, 16], F32), "X4": _s([2, 8, 16], F32),
    "f0": _s([256], F32), "f1": _s([256], F32), "f2": _s([256], F32), "f3": _s([256], F32),
    "ism": _s([32], I32), "col": _s([48], F32), "WT": _s([8], F32), "XM": _s([16], F32), "sm": _s([176], F32),
    "smb": _s([112], BF), "ONE": _s([256], BF), "ZR": _s([128], F32), "ZB": _s([256], BF),
    "K16": _s([128], F32), "RW": _s([1424], BF), "IO": _s([256], F32), "JW": _s([256], F32),
    "IB": _s([128], BF), "IF": _s([128], F32), "IN": _s([128], BF), "I8": _s([128], BF), "IA": _s([128], BF),
    "IAN": _s([128], BF), "IG": _s([384], BF), "IFN": _s([128], F32), "KK": _s([256], BF), "IS": _s([256], BF),
    "IR": _s([256], BF), "D6": _s([128], BF),
    "UT": _s([128], F32), "OF": _s([128], F32), "G8": _s([128], F32), "G8B": _s([256], BF),
    "BLK": _s([128], BF), "BLS": _s([128], BF), "TI": _s([128], BF), "TS": _s([128], BF), "TC": _s([128], BF),
    "TD": _s([128], BF), "BVW": _s([128], BF), "BST": _s([128], BF), "BL3": _s([128], BF), "NR": _s([128], BF),
    "sel": _s([64], BF), "PH": _s([8], F32), "SX": _s([144], BF), "SXD": _s([144], BF), "SXN": _s([144], BF),
    "SXF": _s([288], F32), "TB": _s([128], BF), "ST": _s([1024], BF), "SX3": _s([144], BF),
    "SXU": _s([144], BF), "SXT": _s([144], BF), "WM": _s([144], BF),
    "MK": _s([128], F32), "RST": _s([128], F32), "KP": _s([128], BF), "IOC": _s([256], BF), "THT": _s([256], F32),
    "TM": _s([128], F32), "TMB": _s([256], BF), "BASE": _s([144], F32),
    "NT": _s([256], F32), "NU": _s([256], F32), "LT_": _s([256], U16), "LU": _s([256], U16), "LI": _s([256], U16),
    "LK": _s([256], U16), "LS": _s([128], U16), "NQ": _s([2 * HW], BF), "NV": _s([256], BF), "NE": _s([2 * HW], BF),
    "C16": _s([2 * HW], BF), "THR": _s([256], F32), "Z": _s([256], F32), "Z2": _s([2 * HW], F32), "NW": _s([256], BF),
    "SS": _s([264], F32), "VI": _s([256], BF), "LTT": _s([520], BF), "LG": _s([256], BF), "VAL": _s([256], BF),
    "S5": _s([256], BF), "M2": _s([256], BF), "NC": _s([256], BF), "NRC": _s([256], BF),
    "WK": _s([520], F32), "YO": _s([512], F32), "ZO": _s([512], F32),
}
for _k in range(8):
    SCRATCH["P%d" % _k] = ("psum", [128, 512], F32)
SEMAPHORES = (["qv", "qa", "qt", "qp"] + ["d%d" % _k for _k in range(40)] + ["ar%d" % _k for _k in range(10)]
              + ["lo%d" % _k for _k in range(10)])
ALIAS = {"T2": ("WE", 4096, 4096), "PT": ("RL", 8192, 4112), "OH": ("T1", 0, 4096),
         "K1": ("NRC", 0, 256), "K2": ("VAL", 0, 256), "DF": ("UT", 0, 128)}
ALLP = (1 << 128) - 1
HELP = ((6,), (0, 1, 2, 3, 5, 6, 7), (0, 1, 2, 3, 5, 6, 7))
CUT = {"pp": "121121", "rl": "211211", "t": "11111111", "k": "112112", "pb": "4121", "c": "11111111", "rn": "112211",
       "fb": "11111111", "fp": "112112"}
CY, PE = 1.04e-3, 0.53e-3
BEGIN = (12.3, 52.0, 90.0)
TM = {"pw": 8.93, "v1": 20.5, "v2": 24.13, "v3": 28.69, "n0": 21.03, "n1": 27.77, "lsl": 15.5, "ltl": 21.49, "fb": 29.47,
      "nrc": 37.69, "t0": 8.75, "t1": 0.29, "dig": 25.33, "late": 30.77, "x4": 17.4, "st0": 1.7, "st1": 0.37, "pb0": 31.99,
      "pb1": 2.92, "pp0": 15.21, "pp1": 1.18, "pp2": -3.87, "k0": 17.59, "k1": 1.29, "bb": 46.15, "l2": 29.57, "ls": 24.55,
      "wk0": 30.48, "wk1": 32.93, "lk": 25.49, "bb0": 15.46, "ltt": 39.97, "ps0": 31.47, "ps1": 5.71, "oh0": 27.55, "ne": 16.35,
      "rn0": 46.06, "rn1": 0.04}
ENG, RLE = "avvv", "vaaavaaa"


def build(T):
    ops = []
    due = [None]

    def R(name, a=0, b=None, st=1, p=None):
        if name in ALIAS:
            name, off, size = ALIAS[name]
            a, b = a + off, (size if b is None else b) + off
        shp, dt = SCRATCH[name][1], SCRATCH[name][2]
        if b is None:
            b = shp[1]
        pm = ALLP
        ps = slice(0, 128)
        if p is not None:
            ps = slice(p[0], p[1], p[2])
            pm = sum(1 << q for q in range(p[0], p[1], p[2]))
        ap = T[name][ps, a:b:st] if st != 1 else T[name][ps, a:b]
        return {"ap": ap, "acc": [(name, a * SZ[dt], b * SZ[dt], pm)], "off": [], "n": len(range(a, b, st)), "w": SZ[dt],
                "ps": SCRATCH[name][0] == "psum", "rows": bin(pm).count("1")}

    def Q(name, B=None):
        acc = [(name, 0, 1024, ALLP)] if B is None else [(name, 512 * h + 64 * B, 512 * h + 64 * B + 64, ALLP) for h in (0, 1)]
        return {"ap": T[name][:] if B is None else T[name][:, :, B, :], "acc": acc, "off": [], "n": 256 if B is None else 32,
                "w": 4, "ps": False, "rows": 128}

    def X(name, h=None, cols=None):
        return {"ap": T[name][:, cols[0]:cols[1]] if cols else T[name][:] if h is None else T[name][h:8:2, :],
                "acc": [], "off": [], "n": 0, "w": 4, "ps": False, "rows": 0}

    def IND(win, off):
        return {"ap": win["ap"].indirect(off["ap"]), "acc": win["acc"], "off": off["acc"], "n": 16 * off["n"], "w": win["w"], "ps": False}

    def add(q, fn, outs, ins, grp=None, both=False):
        rd, wr = [], []
        views = [i for i in ins if isinstance(i, dict)]
        for o in outs:
            wr += o["acc"]
            rd += o["off"]
        for i in views:
            rd += i["acc"] + i["off"]
        o = outs[0]
        n = o["n"]
        if grp is not None:
            c = max(x["n"] * x["w"] * x["rows"] for x in [o] + views) / DMA
        elif q == "t":
            c = max(64, views[1]["n"]) * PE * (4 if views[0]["w"] == 4 else 1)
        elif q == "p":
            c = 0.17 + 2 * n * CY
        elif o["off"]:
            c = 0.06 + 3.8 * n * CY
        elif views and views[0]["off"]:
            c = 0.07 + 1.56 * n * CY
        elif q == "a":
            c = 0.1 + max(64, n) * CY
        else:
            f = 0.5 if all(x["w"] == 2 for x in [o] + views if x["n"] > 1) else 1.0
            if both and not (views[0]["ps"] or views[1]["ps"]):
                f *= 2
            c = 0.03 + max(64, n * f) * CY
        ops.append({"q": q, "fn": fn, "rd": rd, "wr": wr, "grp": grp, "c": c, "long": bool(views and views[0]["off"]),
                    "due": None if q == "p" else due[0]})

    def u(x):
        return x["ap"] if isinstance(x, dict) else x

    def ts(o, i, s1, op0, s2=None, op1=None):
        if op1 is None:
            add("v", lambda g: g.vector.tensor_scalar(u(o), u(i), u(s1), None, op0), [o], [i, s1])
        else:
            add("v", lambda g: g.vector.tensor_scalar(u(o), u(i), u(s1), u(s2), op0, op1), [o], [i, s1, s2])

    def tt(o, a, b, op):
        add("v", lambda g: g.vector.tensor_tensor(u(o), u(a), u(b), op), [o], [a, b], both=True)

    def cp(o, i):
        add("v", lambda g: g.vector.tensor_copy(u(o), u(i)), [o], [i])

    def ms(o, c):
        add("v", lambda g: g.vector.memset(u(o), c), [o], [])

    def turn(o, i):
        add("v", lambda g: g.vector.transpose(u(o), u(i)), [o], [i])

    def scan(o, d0, d1, init, op0, op1):
        add("v", lambda g: g.vector.tensor_tensor_scan(u(o), u(d0), u(d1), init, op0, op1), [o], [d0, d1])

    def act(o, i, scale=1.0, bias=0.0, fn=None):
        f = fn if fn is not None else (AF.Copy if (not isinstance(bias, dict) and bias == 0.0) else AF.Identity)
        add("a", lambda g: g.scalar.activation(u(o), u(i), f, u(bias), u(scale)), [o], [i, scale, bias])

    def either(n=2):
        same = [ops.pop() for _ in range(n - 1)] + [ops[-1]]
        v = ops[-1]
        v["alt"] = {a["q"]: a["fn"] for a in same}
        v["cq"] = {a["q"]: a["c"] for a in same}
        v["rd"] = [x for a in same for x in a["rd"]]

    def on(q):
        if q:
            ops[-1]["first"] = q

    def copy(o, i, bias=0.0):
        if bias == 0.0:
            cp(o, i)
        else:
            ts(o, i, bias, OP.add)
        act(o, i, 1.0, bias)
        either()

    def relu(o, i, bias):
        ts(o, i, bias, OP.add, 0.0, OP.max)
        act(o, i, 1.0, bias, AF.Relu)
        either()
        ops[-1]["lax"] = True

    def relu2(o, i):
        ts(o, i, -2.0, OP.mult, 0.0, OP.max)
        act(o, i, -2.0, 0.0, AF.Relu)
        either()

    def mm(o, l, r, st=True, sp=True):
        add("t", lambda g: g.tensor.matmul(u(o), u(l), u(r), st, sp), [o], [l, r])

    def mms(o, pairs):
        for k, (l, r) in enumerate(pairs):
            mm(o, l, r, k == 0, k == len(pairs) - 1)

    def iota(o, pat, base=0, cm=0, integer=False):
        if integer:
            add("p", lambda g: g.iota(u(o), pat, base, cm), [o], [])
        else:
            add("p", lambda g: g.iota(u(o), pat, base, cm, allow_small_or_imprecise_dtypes=True), [o], [])

    def asel(o, i, pat, op, fill, base, cm):
        add("p", lambda g: g.affine_select(u(o), u(i), pat, op, fill, base, cm), [o], [i])

    ng = [0]

    def dma(q, pairs):
        k = ng[0]
        ng[0] += 1
        for o, i in pairs:
            if q == "s":
                add("s", lambda g, o=o, i=i: g.sync.dma_start(u(o), u(i)), [o], [i], "d%d" % k)
            else:
                add("a", lambda g, o=o, i=i: g.scalar.dma_start(u(o), u(i)), [o], [i], "d%d" % k)
        return "d%d" % k

    def send(k, src, *to):
        ops.append({"q": "p", "send": (k, u(src), [u(x) for x, s in to]), "steps": [s for x, s in to], "rd": src["acc"], "wr": [],
                    "grp": "lo%d" % k, "c": src["n"] * src["w"] * 128 / LINK})

    def arrive(k, *to):
        ops.append({"q": "x", "steps": [s for x, s in to], "rd": [], "wr": [a for x, s in to for a in x["acc"]], "grp": "ar%d" % k,
                    "c": 0.0, "after": "lo%d" % k})

    def C(k):
        return R("col", k, k + 1)

    def XMc(k):
        return R("XM", k, k + 1)

    def rows(name, r, a):
        return R(name, a, a + 4096, 1, (r, 128, 16))

    def stage(dst, src, off, which):
        return [(R(dst, 256 * k, 256 * k + 256), rows(src, r, off)) for k, r in which]

    def unstage(dst, off, src, which):
        return [(rows(dst, r, off), R(src, 256 * k, 256 * k + 256)) for k, r in which]

    def unstage2(dst, off, src, which):
        return [(R(dst, off, off + 4096, 1, (16 * h + r, 128, 32)), R(src, 256 * k + 128 * h, 256 * k + 128 * h + 128))
                for k, r in which for h in (0, 1)]

    def gat(dst, k, n, win, lst, q=None):
        copy(R(dst[0], dst[1] + 512 * k, dst[1] + 512 * (k + n)), IND(win, R(lst, 32 * k, 32 * (k + n))))
        on(q)

    def cut(name, e=None):
        out, k = [], 0
        for n in CUT[name]:
            if e is None or k // 4 == e:
                out.append((k, int(n)))
            k += int(n)
        return out

    def fill(name, a, b, c):
        iota(R(name, a, b), [[0, b - a]], c, 0)

    def diag(name, w, a=0):
        asel(R(name, a, a + 128), R("ZR"), [[-1, 128]], OP.not_equal, w, 0, 1)
        if name not in ("IF", "IB"):
            ts(R(name, a, a + 128), R("IB"), w, OP.mult)
            act(R(name, a, a + 128), R("IB"), w)
            either(3)
            on("v")

    def one_row(name, pat, src, r, s, w):
        entries(R(name), pat, {(r, s): w})
        ts(R(name), R(src), XMc(r), OP.mult, w, OP.mult)
        either()
        on("v")

    def entries(o, pat, ws):
        src = R("ZB", 0, o["n"])
        for (r, s), w in ws.items():
            asel(o, src, pat, OP.not_equal, float(w), -r - 1000 * (s or 0), 1)
            src = o

    BY_G, BY_GS, BY_ROW, WIDE = [[-16, 8]], [[-16, 8], [1000, 16]], [[-16, 8], [0, 16]], [[-16, 9], [1000, 16]]

    def behind(k0, grp):
        for op in ops[k0:]:
            op["behind"] = grp

    P1, P8, P16 = (0, 1, 1), (0, 8, 1), (0, 16, 1)
    cX, cG, cINV, cPW, cN, cTH, cA, cNX, c4X, cN0, cB56, c256 = range(12)
    E1 = {0: 16, 1: 1, 3: 64, 4: -16, 5: -1, 7: -64}
    E2 = {0: -16, 1: -1, 2: -1, 3: -64, 4: 16, 5: 1, 6: 1, 7: 64}
    cM56, cSC, cB0, cB1, cB2, cPV = range(16, 22)
    sSC, sC, sN, sNE, sE1, sE2 = 0, 8, 16, 32, 40, 48
    rONE, r64, r7, rS8, rB16, rIO, rX0, rX4, rM45, rM2 = 0, 128, 256, 384, 512, 768, 1024, 1152, 1280, 1408

    def row(k, a=0, n=128):
        return R("RW", k + a, k + a + n, 1, P1)

    def H(name, e, a=0, n=128):
        w = HW if SCRATCH[name][1][1] == 2 * HW else 128
        return R(name, w * e + a, w * e + a + n)

    def PA(e, k, n=1):
        return R("P%d" % e, 128 * k, 128 * (k + n))

    def PB(e, k):
        return R("P%d" % (2 + e), 128 * k, 128 * k + 128)

    def PC(e, k):
        return R("P%d" % (4 + e), 128 * k, 128 * k + 128)

    def lin2bars(ps, src, base, sel, n=1, first=None):
        name, a = ps["acc"][0][0], ps["acc"][0][1] // 4
        if first:
            mm(ps, first[0], first[1], True, False)
        for s in range(16):
            mm(R(name, a + s, a + 128 * n, 16), R(src, base + s, base + 2048, 16), R("sel", sel, sel + 8 * n), not first, not first or s == 15)

    def to_offers(o, w, src, more=()):
        mms(o, [(R(w, 15 - x, 143 - x), R(src, x, 256, 16)) for x in range(16)] + list(more))

    def positions(e, t0):
        ps = R("P3", 256 * e, 256 * e + 128)
        mm(ps, row(rONE), row(rB16, 128 * e), True, False)
        mm(ps, R("SXN", 15, 143), H("NC", e), False, False)
        for k in range(1, 17):
            o = R("ST", 128 * (k % 8), 128 * (k % 8) + 128)
            due[0] = t0 + 0.15 * k
            relu(o, H("NC", e), -float(k))
            due[0] = None
            mm(ps, R("SXD", 16 - k, 144 - k) if k < 16 else R("SX", 0, 128), o, False, k == 16)

    def dig(dst, k, s, f, bank):
        if f is not s:
            cp(f, s)
        copy(R(dst, 512 * k, 512 * k + 256), f)
        on("a")
        mms(R(bank, 0, 256), [(R("IF"), f), (R("IN"), R(dst, 512 * k, 512 * k + 256))])
        copy(R(dst, 512 * k + 256, 512 * k + 512), R(bank, 0, 256))
        on("a")

    g0 = dma("s", [(R("i2", 128 * h, 128 * h + 128), X("bt", h)) for h in (0, 1)])
    dma("a", [(R("ism", 0, 1, 1, P8), X("pn")), (R("ism", 4, 5, 1, P8), X("th")), (R("i5", 0, 256, 1, P8), X("bl"))])
    for pairs in ([(R("i4"), X("bk"))], [(R("i0"), X("pt")), (R("i1"), X("pu"))], [(R("TN", 16, 4112), X("tones"))],
                  [(R("i3", 128 * h, 128 * h + 128), X("bu", h)) for h in (0, 1)]):
        k0 = len(ops)
        g1 = dma("s", pairs)
        behind(k0, g0)
        g0 = g1
    ms(R("PT", 0, 2064), 0.0)
    act(R("PT", 2064, 4112), R("PT", 0, 2048))
    ms(R("ONE"), 1.0)
    ms(R("ZR"), 0.0)
    ms(R("ZB"), 0.0)
    ms(R("OF"), 1.0)
    ms(R("TN", 0, 16), 0.0)
    iota(R("ism", 8, 9), [[0, 1]], 0, 1, True)
    iota(R("IO"), [[1, 256]])
    ts(R("ism", 9, 10), R("ism", 8, 9), 15, OP.bitwise_and)
    ts(R("ism", 10, 11), R("ism", 8, 9), 4, OP.arith_shift_right)
    cp(R("col", cX, cX + 2), R("ism", 9, 11))
    ts(R("XM"), R("IO", 0, 16), C(cX), OP.is_equal)
    ts(R("PH"), R("IO", 0, 8), C(cG), OP.is_equal)
    act(R("JW"), R("IO"), 16.0, C(cX))
    act(C(cINV), XMc(0), -1.0)
    act(C(cA), XMc(2), -1.0, C(cINV))
    act(R("PT", 0, 16), R("ONE", 0, 16), C(cA))
    act(C(c256), C(cX), 256.0)
    iota(R("ID", 0, 256), [[16, 16], [0, 16]])
    act(R("ID", 0, 256), R("ID", 0, 256), 1.0, C(c256))
    iota(R("ID", 256, 512), [[0, 16], [1, 16]])
    diag("IF", 1.0)
    diag("IB", 1.0)
    asel(R("DF"), R("IF"), [[-1, 128]], OP.not_equal, -1.0, 1, 1)
    asel(R("DF"), R("DF"), BY_GS, OP.not_equal, 0.0, 1, 1)
    asel(R("G8", 0, 128, 1, P8), R("OF", 0, 128, 1, P8), [[1, 8], [0, 16]], OP.is_equal, 0.0, 0, -1)
    asel(R("BLK"), R("ONE", 0, 128), BY_ROW, OP.is_ge, 0.0, 0, 1)
    asel(R("BLK"), R("BLK"), [[16, 8], [0, 16]], OP.is_ge, 0.0, 15, -1)
    act(R("BLS"), R("BLK"), -1.0 / 8192)
    asel(R("TI"), R("BLS"), [[1, 128]], OP.is_ge, 0.0, 0, -1)
    act(C(cPW), C(cG), 16.0, 15.0)
    ts(R("SXF", 0, 144), R("IO", 0, 144), C(cPW), OP.is_equal)
    tt(R("SXF", 145, 288), R("SXF", 1, 144), R("SXF", 0, 143), OP.subtract)
    act(R("SX"), R("SXF", 0, 144))
    act(R("SXD", 1, 144), R("SXF", 145, 288))
    act(R("TB"), R("TI"), 2.0 ** 26)
    asel(R("TB"), R("TB"), [[-1, 128]], OP.not_equal, 2.0 ** 20 - 8192, 0, 1)
    for k, c in ((rONE, 1.0), (r64, 64.0), (r7, 7.5), (rM45, -4.5 * BIG / 64)):
        ms(row(k), c)
    ms(row(rM2, 0, 16), -2.0)
    iota(row(rS8), [[0, 8], [8192, 16]])
    act(row(rB16, 0, 256), R("IO", 0, 256, 1, P1), 16.0)
    act(row(rIO, 0, 256), R("IO", 0, 256, 1, P1))
    asel(row(rX0), row(rONE), [[0, 8], [1, 16]], OP.is_equal, 0.0, 0, 0)
    asel(row(rX4), row(rONE), [[0, 8], [1, 16]], OP.is_equal, 0.0, -4, 0)
    asel(R("K16", 0, 128, 1, P16), R("OF", 0, 128, 1, P16), [[0, 8], [1, 16]], OP.is_equal, 0.0, 0, -1)
    ms(R("WT", 0, 3, 1, P16), 0.0)
    asel(R("WT", 1, 2, 1, P16), R("OF", 0, 1, 1, P16), [[0, 1]], OP.is_ge, 0.0, 4, -1)
    for k, ws in enumerate(({5: 1, 6: 1}, {5: 2.0 ** -19, 6: 2.0 ** -14}, {5: 128, 6: 4224, 7: 64})):
        for r, w in ws.items():
            asel(R("WT", k, k + 1, 1, P16), R("WT", k, k + 1, 1, P16), [[0, 1]], OP.not_equal, float(w), -r, 1)
    mm(R("P7", 0, 3), R("K16", 0, 128, 1, P16), R("WT", 0, 3, 1, P16))
    act(R("col", cM56, cM56 + 3), R("P7", 0, 3))
    act(R("sel", sSC, sSC + 8), R("PH"))
    entries(R("sel", sC, sC + 8), BY_G, {(4, None): 16})
    for n, w, a in (("IN", -1.0, 0), ("I8", -8192.0, 0), ("IAN", -float(AW), 0), ("IG", HUGE, 0), ("IS", 2.0 ** -19, 0),
                    ("IR", -2.0 ** -14, 0), ("IA", float(A1 - BB), 0), ("IS", -1.0 / 16, 128), ("IG", 2.0 ** 14 - 2.0 ** 19, 128),
                    ("IR", 2.0 ** -14, 128), ("IG", -16.0, 256), ("IFN", -1.0, 0)):
        diag(n, w, a)
    for n in ("NQ", "NE", "C16", "NV", "Z2", "LTT"):
        ms(R(n), 0.0)
    ts(R("B0"), R("i4"), 1.0, OP.add)
    send(6, R("B0"), (R("B1"), -1), (R("B2"), -2))
    ts(Q("X3"), R("i2"), 16.0, OP.add)
    for B in range(8):
        turn(R("f3", B, 256, 8), Q("X3", B))
    cp(R("SB"), R("f3"))
    send(0, R("SB"), (R("RB"), 1))
    due[0] = 2.0
    mm(R("P5", 0, 256), R("DF"), R("f3"))
    ts(R("NW"), R("P5", 0, 256), 0.0, OP.not_equal)
    mms(R("P5", 256, 512), [(R("IF"), R("f3")), (R("TB"), R("NW"))])
    copy(R("NU"), R("P5", 256, 512), -2.0 ** 20)
    for k in range(16):
        o = R(("YO", "ZO")[k % 4 // 2], 256 * (k % 2), 256 * (k % 2) + 256)
        due[0] = TM["st0"] + TM["st1"] * k
        relu(o, R("NU"), 8192.0 * (k + 1))
        due[0] = None
        mm(R("P4", 0, 256), R("SXF", 159 - k, 287 - k) if k < 15 else R("SXF", 0, 128), o, k == 0, k == 15)
    act(C(cB56), C(cX), -8192.0)
    ts(R("LK"), R("P4", 0, 256), C(cB56), OP.add, 4111.0, OP.min)
    act(R("G8B", 0, 128, 1, P8), R("G8", 0, 128, 1, P8))
    asel(R("G8B", 128, 256, 1, P8), R("G8B", 0, 128, 1, P8), [[0, 8], [1, 16]], OP.is_equal, 0.0, -2, 0)
    cp(R("M2", 0, 256, 1, P8), R("i5", 0, 256, 1, P8))
    mm(R("P6", 256, 512), R("G8B", 0, 128, 1, P8), R("M2", 0, 256, 1, P8))
    ts(R("VI"), R("P6", 256, 512), C(cX), OP.is_gt)
    tt(R("VI"), R("VI"), R("NW"), OP.mult)
    act(C(cN0), C(cX), 16.0)
    act(R("BASE", 128, 144), R("IO", 0, 16), 256.0, C(cN0))
    act(R("sm", 48, 64), R("BASE", 128, 144), 1.0, 15.0)
    to_offers(R("P6", 16, 32), "SX", "VI")
    tt(R("sm", 0, 16), R("P6", 16, 32), R("sm", 48, 64), OP.add)
    cp(R("LS", 64, 80), R("sm", 0, 16))
    mms(R("P7", 256, 512), [(R("G8B", 128, 256, 1, P8), R("M2", 0, 256, 1, P8)), (row(rX0), row(rIO, 0, 256))])
    act(C(cNX), XMc(1), 128.0)
    act(C(cNX), XMc(2), 127.0, C(cNX))
    act(R("LTT", 1, 257), R("P7", 256, 512), 1.0, C(cNX))
    act(C(cNX), C(cX), -1.0)
    fill("XA", BB - 16, BB + 1088, 99)
    for a in (A0, XT1 - 16, XT1 + 4096):
        iota(R("XA", a, a + 16), [[0, 16]], 99, 0)
    due[0] = 3.0
    cp(R("sm", 16, 24, 4, P8), R("ism", 0, 8, 4, P8))
    mm(R("P2", 0, 2), R("G8", 0, 128, 1, P8), R("sm", 16, 24, 4, P8))
    act(C(cN), R("P2", 0, 1), 8192.0, -4097.0)
    act(R("P2", 256, 512), R("JW"), -8192.0, C(cN))
    tt(R("f0"), R("i0"), R("P2", 256, 512), OP.min)
    ts(R("LT_"), R("f0"), -1.0, OP.max, 16.0, OP.add)
    tt(R("f1"), R("i1"), R("P2", 256, 512), OP.min)
    ts(R("LU"), R("f1"), -1.0, OP.max, 16.0, OP.add)
    due[0] = TM["x4"]
    ts(R("f1"), R("f1"), -1.0, OP.max)
    for B in range(8):
        turn(Q("X4", B), R("f1", B, 256, 8))
    due[0] = None
    act(R("col", cTH, cTH + 1, 1, P8), R("sm", 20, 21, 1, P8), 1.0, 8192.0)
    act(R("TM", 0, 128, 1, P8), R("G8", 0, 128, 1, P8), R("col", cTH, cTH + 1, 1, P8))
    asel(R("TM", 0, 128, 1, P8), R("TM", 0, 128, 1, P8), [[0, 8], [1, 16]], OP.not_equal, -4096.0, -15, 0)
    act(R("TMB", 0, 128, 1, P8), R("TM", 0, 128, 1, P8))
    tt(R("TMB", 128, 256, 1, P8), R("TM", 0, 128, 1, P8), R("TMB", 0, 128, 1, P8), OP.subtract)
    dma("s", unstage("PT", 16, "ID", [(0, 2), (1, 3)]) + unstage("PT", 16, "B0", [(0, 4)]))
    arrive(6, (R("B1"), -1), (R("B2"), -2))
    gp = dma("s", unstage("PT", 16, "B1", [(0, 5)]) + unstage("PT", 16, "B2", [(0, 6)]))
    fill("WE", 0, 1024, 0)
    k0 = len(ops)
    dma("s", [(R("XA", a, a + 1104), R("XA", BB - 16, BB + 1088)) for a in range(BB + 1088, A1, 1104)])
    dma("s", [(R("WE", a, a + 1024), R("WE", 0, 1024)) for a in range(1024, 12288, 1024) if a < 4096 or a >= 8192])
    behind(k0, gp)
    dma("s", [(R("RL", 4096, 8192), R("TN", 16, 4112))])

    def late_constants():
        act(R("sel", sNE, sNE + 8), R("PH"), BIG)
        iota(R("MK"), [[0, 8], [1, 16]])
        act(R("MK"), R("MK"), 1.0, C(cNX), AF.Abs)
        act(R("MK"), R("MK"), -1.0, 1.0, AF.Relu)
        iota(R("IOC"), [[-16, 256]], 4080)
        ts(R("IOC"), R("IO"), -16.0, OP.mult, 4080.0, OP.add)
        act(R("IOC"), R("IO"), -16.0, 4080.0)
        either(3)
        iota(R("ism", 16, 24), [[16, 8]], 15, 0, True)
        cp(R("LS", 80, 88), R("ism", 16, 24))
        act(C(cB56), C(cM56), -113.0, 128.0)
        act(C(c256), C(cM56), 16.0)
        act(R("sm", 24, 32), R("IO", 0, 8), C(c256), C(cB56))
        cp(R("LS", 88, 96), R("sm", 24, 32))
        keep, due[0] = due[0], TM["pw"]
        ms(R("K2"), 0.5)
        asel(R("K2"), R("K2"), [[0, 16], [1, 16]], OP.not_equal, 0.0, 0, 0)
        asel(R("K1"), R("ZB"), [[0, 16], [1, 16]], OP.not_equal, 65536.0, 0, 0)
        scan(R("K1"), R("K2"), R("K1"), 0.0, OP.mult, OP.add)
        tt(R("sm", 32, 48), R("K1", 0, 16), R("XM"), OP.mult)
        add("v", lambda g: g.vector.tensor_reduce(u(C(cPW)), u(R("sm", 32, 48)), AX, OP.add), [C(cPW)], [R("sm", 32, 48)])
        ts(R("WM"), R("SX"), C(cPW), OP.mult, 0.5, OP.mult)
        asel(R("K1", 0, 256, 1, P16), R("K1", 0, 256, 1, P16), [[-1, 16], [0, 16]], OP.is_ge, 1.0, 0, 1)
        asel(R("K1", 0, 256, 1, P16), R("K1", 0, 256, 1, P16), [[1, 16], [0, 16]], OP.is_ge, float(2 ** 20), 0, -1)
        act(R("K2", 0, 128, 1, P16), R("K16", 0, 128, 1, P16))
        mm(R("P7", 0, 256), R("K2", 0, 128, 1, P16), R("K1", 0, 256, 1, P16))
        act(R("THT"), R("P7", 0, 256))
        due[0] = keep
        iota(R("SS", 0, 1), [[0, 1]], 2 ** 21)
        iota(R("smb", 64, 65), [[0, 1]])
        iota(R("WK", 0, 1), [[0, 1]])
        asel(R("UT"), R("OF"), [[1, 128]], OP.is_gt, 0.0, 0, -1)
        asel(R("TS"), R("BLS"), [[1, 128]], OP.is_gt, 0.0, 0, -1)
        asel(R("TC"), R("BLS"), [[-1, 128]], OP.is_ge, 0.0, 0, 1)
        asel(R("TD"), R("BLS"), [[-1, 128]], OP.is_gt, 0.0, 0, 1)
        asel(R("KP"), R("ONE", 0, 128), [[0, 8], [1, 16]], OP.not_equal, 0.0, 0, 0)
        asel(R("RST"), R("ZR"), [[0, 8], [1, 16]], OP.not_equal, NONE, 0, 0)
        one_row("BVW", BY_ROW, "BLK", 5, None, -16.0)
        act(R("SXN"), R("SX"), -1.0)
        one_row("SX3", WIDE, "SX", 2, 15, 1.0)
        one_row("D6", BY_GS, "IB", 6, 6, -2.0 ** 19)
        asel(R("NR"), R("ONE", 0, 128), [[-1, 128]], OP.is_equal, 0.0, -4, 1)
        asel(R("NR"), R("NR"), [[0, 8], [-1, 16]], OP.is_ge, 0.0, 3, 0)
        act(C(cB1), XMc(7), 64.0, C(cB0))
        act(C(cB2), XMc(7), 128.0, C(cB0))
        act(C(cN0), C(cX), 16.0, 2049.0)
        act(R("col", cPV, cPV + 3), R("IO", 1, 4), 4096.0, C(cX))
        act(C(c4X), C(cX), 16.0, 1.0)
        iota(R("BASE", 0, 32), [[-8191, 2], [256, 16]], 16383)
        act(R("BASE", 0, 32), R("BASE", 0, 32), 1.0, C(c4X))
        iota(R("BASE", 96, 128), [[AW - 257, 2], [16, 16]], 257)
        act(R("BASE", 96, 128), R("BASE", 96, 128), 1.0, C(cX))
        iota(R("BASE", 32, 48), [[0, 16]], 256 + 8192)
        ms(R("BASE", 48, 64), 4103.5 + 8192)
        iota(R("BASE", 64, 96), [[0, 32]])
        for a, ws in ((sE1, E1), (sE2, E2), (sN, {0: 1, 1: 1}), (sN + 8, {2: 1, 3: 1})):
            entries(R("sel", a, a + 8), BY_G, {(r, None): w for r, w in ws.items()})

    def last_constants():
        entries(R("SXU"), WIDE, {(0, 15): 1, (1, 15): 1})
        entries(R("SXT"), WIDE, {(2, 15): 1, (3, 15): 1})
        entries(R("BST"), BY_ROW, {(0, None): 16, (1, None): 1, (3, None): 64})
        entries(R("BL3"), BY_ROW, {(2, None): 1})
        act(C(c4X), C(cX), 4.0, 512.0)
        act(C(cINV), C(cX), 1.0, -128.0)

    for v in range(3):
        last = v == 2
        xt, xo, an = (XT0, XT1, A1) if v % 2 == 0 else (XT1, XT0, A0)
        pv = 4096 * (v + 1)
        win = R("XA", A0, A1) if v % 2 == 0 else R("XA", BB, XT1)

        def at(t, t0=None):
            due[0] = None if t is None else (t0 if v == 0 and t0 is not None else BEGIN[v] + t)
        for e in (0, 1):
            if v == 0:
                at(None)
                mm(PA(e, 1), R("f0", 128 * e, 128 * e + 128), R("IF"))
                copy(H("NT", e), PA(e, 1))
                for k, n in cut("pp", e):
                    at(0, TM["pp0"] + TM["pp1"] * k + TM["pp2"] * e)
                    gat(("W", pv), k, n, R("PT"), "LT_")
            else:
                arrive(4 * v + e, (H("SR%d" % (v - 1), e), 1))
                for k, n in cut("rl", e):
                    at((0.0, 0.0, 0.9, 0.9, 1.8, 1.8, 2.7, 3.9)[k])
                    gat(("W", pv), k, n, R("RL", 0, pv + 16), "SR%d" % (v - 1), RLE[k])
                at(None)
                lin2bars(PA(e, 0), "W", pv + 2048 * e, sN, 2)
                at(2.6 + 3 * e)
                copy(H("NT", e), PA(e, 1))
                on(ENG[e])
                copy(H("NU", e), PA(e, 0))
                on(ENG[2 + e])
            at(2.9 + 3 * e, 8.0)
            tt(H("NQ", e, 1, 127), R("P%d" % e, 129, 256), H("NT", e, 0, 127), OP.not_equal)
            relu2(H("NV", e, 0, 127), R("P%d" % e, 129, 256))
            if v > 0:
                at(None)
                mm(PC(e, 2), H("NT", e), R("IF"))
                at(3.4 + 3 * e)
                ts(H("LT_", e), PC(e, 2), 16.0, OP.add)
                at(None)
                mm(PC(e, 3), H("NU", e), R("IF"))
                at(3.7 + 3 * e)
                ts(H("LU", e), PC(e, 3), 16.0, OP.add)
            at(None)
            lin2bars(PB(e, 0), "W", pv + 2048 * e, sC)
            copy(H("C16", e, 1), PB(e, 0))
            on("a")
            mms(PB(e, 1), [(R("ONE", 0, 128, 1, P8), R("TMB", 0, 128, 1, P8)), (R("ONE", 0, 128, 1, P8), R("TMB", 128, 256, 1, P8)),
                           (R("I8"), H("NQ", e, 1)), (R("I8"), H("NV", e))])
            copy(H("THR", e), PB(e, 1))
            on("a")
            mms(PB(e, 2), [(R("IB"), H("C16", e)), (R("IN"), H("C16", e, 1)), (R("IB"), H("NQ", e))])
        for e in (0, 1):
            for k, n in cut("t", e):
                a, b = 512 * k, 512 * (k + n)
                at(3.7 + 0.9 * k + 0.7 * e, TM["t0"] + TM["t1"] * k)
                gat(("XA", xt), k, n, R("TN"), "LT_", "a")
                at(4.8 + 1.1 * k, TM["t0"] + 1 + TM["t1"] * k)
                tt(R("T2", a, b), IND(R("TN"), R("LU", a // 16, b // 16)), R("XA", xt + a, xt + b), OP.mult)
            at(None)
            lin2bars(PC(e, 0), "T2", 2048 * e, sSC)
        if v == 0:
            for k, n in cut("k"):
                at(0, TM["k0"] + TM["k1"] * k)
                gat(("XA", A0 + 16), k, n, R("TN"), "LK")
            at(0, TM["dig"])
            x4 = Q("X4")
            dig("S1", 0, x4, x4, "P0")
            dig("S0", 0, R("i3"), R("f2"), "P1")
            send(1, R("S0", 0, 512), (R("R0"), 1))
            at(0, TM["late"])
            late_constants()
            at(None)
            dma("s", stage("S1", "W", pv, [(2, 2), (3, 3), (4, 5), (5, 6)]))
            send(2, R("S1"), (R("R1"), 1))
            dma("s", unstage2("W", pv, "S1", [(0, 0), (1, 1)]))
            arrive(2, (R("R1"), 1))
            dma("s", unstage2("RL", 4096, "R1", [(0, 0), (1, 1)]) + unstage("RL", 4096, "R1", [(k, k) for k in range(2, 6)]))
            arrive(0, (R("RB"), 1))
            for k, n in cut("pb"):
                at(0, TM["pb0"] + TM["pb1"] * k)
                gat(("RL", 0), k, n, R("PT"), "RB", "a")
            at(None)
            arrive(1, (R("R0"), 1))
            dma("s", unstage2("RL", 0, "R0", [(0, 0), (1, 1)]))
            for n, a in (("RL", 8192), ("RL", 12288), ("W", 16384)):
                act(R(n, a, a + 16), R("ONE", 0, 16), C(cA))
            at(0, TM["bb0"])
            copy(R("S5"), IND(R("XA", A0, BB), R("LS", 64, 80)))
            cp(IND(R("XA", BB, BB + AW), R("LS", 64, 80)), R("S5"))
        elif v == 1:
            dma("s", stage("S1", "W", pv, [(0, 0), (1, 1), (2, 2), (3, 3), (4, 5)]))
            send(3, R("S1", 0, 1280), (R("R2"), 1))
            arrive(3, (R("R2"), 1))
            dma("s", unstage("RL", 8192, "R2", [(k, k) for k in range(5)]))
        if v > 0:
            k0 = len(ops)
            dma("s", [(rows("WE", r, w), R("ZB")) for w in (0, 8192) for r in range(8)])
            if v == 1:
                dma("s", [(R("W", 0, 4096), R("TN", 16, 4112))])
            for op in ops[k0:]:
                op["rd"] = op["rd"] + R("SR%d" % (v - 1))["acc"]
            if v == 1:
                dma("s", unstage2("W", 0, "S0", [(k, k) for k in range(4)]))
        for e in (0, 1):
            at(10.0 + 4.3 * e, TM["ne"] + 2 * e)
            tt(H("NE", e, 1), PC(e, 0), H("THR", e), OP.is_lt)
            scan(H("Z", e), PB(e, 2), H("NE", e), 0.0, OP.add, OP.mult)
            at(None)
            mms(PC(e, 3), [(H("C16", e, 1), R("IB")), (H("NE", e, 1), R("IAN" if v % 2 == 0 else "IA")), (H("Z", e), R("IF"))])
            at(10.9 + 4.3 * e, TM["ne"] + 1 + 2 * e)
            ts(H("LI", e), PC(e, 3), float(AW) if v % 2 == 0 else 0.0, OP.add)
            scan(H("NW", e), R("ONE", 0, 128), H("NE", e), 0.0, OP.add, OP.mult)
            if not last:
                at(12.0 + 4.3 * e, 25.5 + 2 * e)
                scan(H("KK", e), H("NQ", e), H("NE", e), 0.0, OP.add, OP.mult)
            at(None)
            mms(PC(e, 2), [(row(r64), row(rS8)), (row(r64), row(r64)), (row(rONE), row(r7)), (R("IN"), H("C16", e, 1)),
                           (R("IG", 0, 128), H("NE", e, 1)), (R("IG", 128, 256), H("NW", e)), (R("IFN"), H("Z", e))])
        for e in (0, 1):
            for k, n in cut("c", e):
                a, b = 512 * k, 512 * (k + n)
                o, x, keys = R("T2", a, b), R("XA", xt + a, xt + b), IND(win, R("LI", a // 16, b // 16))
                if k in HELP[v]:
                    at(12.3 + 0.9 * HELP[v].index(k))
                    act(R("XA", xo + a, xo + b), keys)
                    keys = R("XA", xo + a, xo + b)
                at(13.7 + 0.9 * k + 0.5 * e + (k > 4))
                tt(o, keys, x, OP.not_equal)
            at(None)
            lin2bars(PC(e, 1), "T2", 2048 * e, sNE, 1, (row(r64), row(rM45)))
            at(17.9 + 4.5 * e)
            scan(H("Z", e), H("NE", e), PC(e, 1), 0.0, OP.mult, OP.max)
            tt(H("f1", e), PC(e, 2), H("Z", e), OP.add)
            scan(H("Z2", e), R("RST"), H("f1", e), 0.0, OP.max, OP.min)
            tt(H("f1", e), IND(H("Z2", e, 0, HW), R("LS", 80, 88)), R("MK"), OP.mult)
            km = R("P6", 8 * e, 8 * e + 8)
            at(None)
            mm(km, H("f1", e), R("PH"))
            t1, t0 = R("sm", 48 + 8 * e, 56 + 8 * e), R("sm", 160 + 8 * e, 168 + 8 * e)
            c16, t2, r16 = (R("smb", a + 8 * e, a + 8 * e + 8) for a in (0, 16, 32))
            at(19.3 + 4.7 * e)
            ts(t1, km, 1.5 * 2.0 ** 37, OP.add, 1.5 * 2.0 ** 37, OP.subtract)
            ts(t0, km, 1.5 * 2.0 ** 27, OP.add, 1.5 * 2.0 ** 27, OP.subtract)
            tt(c16, t0, t1, OP.subtract)
            ts(R("LS", 8 * e, 8 * e + 8), c16, -1.0 / 16, OP.mult, 256.0, OP.add)
            for y in range(8 * e, 8 * e + 8):
                o = R("OH", 256 * y, 256 * y + 256)
                at((TM["oh0"], 24.6)[e] + 0.01 * y)
                ts(o, R("IOC"), R("smb", y, y + 1), OP.is_equal)
                mm(R("P7", 0, 256), R("WM", 15 - y, 143 - y), o, y == 0, y == 15)
            at(22.2 + 3.6 * e)
            ts(t2, t1, 1.5 * 2.0 ** 42, OP.add, 1.5 * 2.0 ** 42, OP.subtract)
            tt(r16, t1, t2, OP.subtract)
            if not last:
                tt(R("smb", 88 + 8 * e, 96 + 8 * e), km, t0, OP.subtract)
            at((18.8, TM["v1"])[e])
            act(H("f2", e), IND(H("Z2", e, 0, HW), R("LS", 88, 96)))
            mm(R("P2", 256 + 128 * e, 384 + 128 * e), H("f2", e), R("IF"))
            act(H("S5", e), R("P2", 256 + 128 * e, 384 + 128 * e), 2.0 ** -19, 128.0)
            at((19.7, TM["v2"])[e])
            act(H("LG", e), IND(R("LTT", 0, 257), R("LS", 8 * e, 8 * e + 8)))
            mms(R("P2", 128 * e, 128 * e + 128), [(H("f2", e), R("IF")), (row(rX4), row(rIO, 128 * e)), (R("IB"), H("LG", e)), (R("D6"), H("S5", e))])
            at((20.5, TM["v3"])[e])
            act(H("VAL", e), R("P2", 128 * e, 128 * e + 128), C(cSC), C((cB0, cB1, cB2)[v]))
            if not last:
                ps = R("P3", 256 * e + 128, 256 * e + 256)
                at((TM["n0"], TM["n1"])[e])
                mms(ps, [(H("KK", e), R("IB")), (H("NW", e), R("IG", 256, 384)), (R("BVW"), H("S5", e))])
                relu(H("NC", e), ps, C(cN0))
                on("a")
                positions(e, BEGIN[v] + TM["ps0"] + TM["ps1"] * e)
                act(H("f3", e), R("P3", 256 * e, 256 * e + 128), 1.0, 16.0 if v % 2 == 0 else 16.0 + AW)
        if not last:
            at(14.0)
            act(R("WK", 1, 257), R("JW"), 1.0, 16.0 + (4096.0 if v % 2 == 0 else 0.0))
        c16, t2, r16, tk = R("smb", 0, 16), R("smb", 16, 32), R("smb", 32, 48), R("smb", 48, 64)
        at(26.0)
        act(R("SS", 1, 257), R("P7", 0, 256))
        at(None)
        to_offers(R("P6", 16, 32), "SX3", "LG", [(R("IR", 0, 128), r16), (row(r64), row(rM2, 0, 16))])
        mm(R("P4", 0, 96), R("IF"), R("BASE", 0, 96), True, False)
        for a, l, r in ((0, R("IS", 0, 128), t2), (16, R("IS", 0, 128), t2), (16, R("IR", 128, 256), r16), (32, R("IS", 128, 256), c16), (48, R("IN"), c16)):
            mm(R("P4", a, a + 16), l, r, False, False)
        if not last:
            mm(R("P4", 48, 64), R("IN"), R("smb", 88, 104), False, False)
            mms(R("P6", 32, 48), [(R("IF"), R("BASE", 128, 144)), (R("IS", 0, 128), t2), (R("IR", 128, 256), r16)])
            at(TM["l2"])
            cp(R("LS", 96, 112), R("P6", 32, 48))
            act(R("M2"), IND(R("XA", xt, xt + 4096), R("LS", 96, 112)))
        at(TM["nrc"])
        mm(R("P5", 256, 512), R("NR"), R("VAL"))
        act(R("NRC"), R("P5", 256, 512))
        at(26.6)
        tt(R("VI"), IND(R("SS", 0, 257), R("LS", 0, 16)), R("THT"), OP.is_ge)
        to_offers(R("P7", 256, 272), "SX", "VI")
        at(27.9)
        ts(tk, R("P7", 256, 272), 0.0, OP.is_equal, -8192.0, OP.mult)
        tt(R("smb", 65, 81), R("P6", 16, 32), tk, OP.mult)
        for a in (0, 0, 16, 32, 48):
            mm(R("P4", a, a + 16), R("IB"), tk, False, False)
        for a, l, b in ((64, "TS", 65), (64, "TC", 64), (80, "TI", 65), (80, "TD", 64)):
            mm(R("P4", a, a + 16), R(l), R("smb", b, b + 16), False, l == "TD")
        at(28.7)
        scan(R("sm", 64, 96), R("KP", 0, 32), R("P4", 64, 96), 0.0, OP.mult, OP.add)
        tt(R("sm", 96, 128), R("P4", 0, 32), R("sm", 64, 96), OP.add)
        cp(R("LS", 16, 48), R("sm", 96, 128))
        cp(IND(R("WE"), R("LS", 16, 32)), R("VAL"))
        at(30.0)
        cp(IND(R("WE", 8192, 24576), R("LS", 32, 48)), R("VAL"))
        at(TM["lsl"] if last else TM["ls"])
        tt(R("sm", 128, 160), R("P4", 32, 64), R("BASE", 96, 128), OP.min)
        cp(R("LS", 48, 80), R("sm", 128, 160))
        sl = "SL%d" % (v % 2)
        at(None)
        for w, sel in ((0, sE1), (8192, sE2)):
            for e in (0, 1):
                if w == 0:
                    mm(PA(e, 0), R("TS", 0, 128, 1, P1), R("TD", 0, 128, 1, P1), True, False)
                at(30.6 + 0.6 * e + w / 8192)
                for s in range(16):
                    mm(R("P%d" % e, s, 128, 16), R("WE", w + 2048 * e + s, w + 2048 * e + 2048, 16), R("sel", sel, sel + 8), False, w > 0 and s == 15)
        for e in (0, 1):
            at(32.4 + 0.6 * e)
            scan(H("Z2", e), R("KP"), PA(e, 0), 0.0, OP.mult, OP.add)
            copy(H("f1", e), IND(H("Z2", e, 0, HW), R("LS", 80, 88)))
            at(None)
            mms(PA(e, 1), [(row(rONE), row(rB16, 128 * e)), (H("Z2", e), R("IF"))] + [(H("f1", 0), R("OF"))] * e + [(H("f1", e), R("UT"))])
            at(33.6 + 0.8 * e)
            ts(H(sl, e), PA(e, 1), C(cPV + v), OP.add, pv + 4096.0, OP.min)
            if not last:
                send(4 * v + 4 + e, H(sl, e), (H("SR%d" % v, e), 1))
        if not last:
            for e in (0, 1):
                at(TM["wk%d" % e])
                cp(IND(R("WK"), R("LS", 48 + 8 * e, 56 + 8 * e)), H("f3", e))
            at(TM["bb"])
            cp(IND(R("XA", BB, A1), R("LS", 64, 80)), R("M2"))
            at(TM["lk"])
            cp(R("LK"), R("WK", 1, 257))
            for k, n in cut("rn"):
                at(TM["rn0"] + TM["rn1"] * k)
                gat(("XA", an + 16), k, n, R("XA", *((XT0, BB) if v == 0 else (A1, XT1 + 4112))), "LK")
            at(TM["ltt"])
            cp(IND(R("LTT"), R("LS", 48, 64)), R("NRC"))
            at(None)
            if v == 0:
                k0 = len(ops)
                dig("S0", 1, R("i2"), R("f0"), "P7")
                behind(k0, "lo5")
                last_constants()
        else:
            at(TM["ltl"])
            cp(IND(R("LTT"), R("LS", 48, 64)), R("NRC"))
            at(None)
            mm(R("P7", 256, 512), R("BL3"), R("LTT", 1, 257))
            act(R("M2"), R("P7", 256, 512), -4.0, C(c4X), AF.Relu)
            mms(R("P7", 0, 256), [(R("BST"), R("LTT", 1, 257)), (R("IA"), R("M2"))])
            ts(R("LK"), R("P7", 0, 256), C(cINV), OP.add, 16384.0, OP.min)
            for k, n in cut("fb"):
                at(TM["fb"] + 0.9 * k)
                gat(("T1", 0), k, n, R("W"), "LK", "a")
            at(None)
            for f, w in ((0, "SXU"), (1, "SXT")):
                mms(R("P%d" % (6 + f), 0, 256), [(R(w, 15 - x, 143 - x), R("T1", 256 * x, 256 * x + 256)) for x in range(16)])
                copy(R("ZO", 256 * f, 256 * f + 256), R("P%d" % (6 + f), 0, 256))
                dma("s", [(X(("zu", "zt")[f]), R("ZO", 256 * f, 256 * f + 256))])
            for q in range(4):
                for k, n in [x for x in cut("fp") if x[0] // 2 == q]:
                    at(35.0 + 0.7 * k)
                    gat(("XA", XT1), k, n, R("W"), sl, "v" if k < 5 else None)
                at(None)
                if q == 1:
                    lin2bars(R("P2", 0, 128), "XA", XT1, sN, 2)
                    copy(R("NT"), R("P2", 0, 256))
                    for f in (0, 1):
                        mm(R("P3", 128 * f, 128 * f + 128), H("NT", f), R("IF"))
                        copy(R("YO", 256 * f, 256 * f + 128), R("P3", 128 * f, 128 * f + 128))
                for f, w in ((0, "SXU"), (1, "SXT")) if q > 1 else ():
                    o = R("P%d" % (2 + q), 64 * f, 64 * f + 64)
                    mms(o, [(R(w, 15 - s, 143 - s), R("XA", XT1 + 1024 * q + s, XT1 + 1024 * q + 1024, 16)) for s in range(16)])
                    copy(R("YO", 256 * f + 64 * q, 256 * f + 64 * q + 64), o)
                if q:
                    a, b = 64 * q * (q > 1), 64 * q + 64
                    dma("s", [(X(("yu", "yt")[f], None, (a, b)), R("YO", 256 * f + a, 256 * f + b)) for f in (0, 1)])
    return ops


PLAN = {}


def order(ops, lanes):
    seen = {}
    for n, op in enumerate(ops):
        dep = set()
        for isw, accs in ((False, op["rd"]), (True, op["wr"])):
            for name, a, b, pm in accs:
                psum = SCRATCH[name][0] == "psum"
                for m, w2, a2, b2, pm2 in seen.get(name, []):
                    if psum:
                        dep.add(m)
                        continue
                    pad = 0 if op["grp"] is None and ops[m]["grp"] is None else 15
                    if (isw or w2) and pm & pm2 and (a & ~pad) < ((b2 + pad) & ~pad) and (a2 & ~pad) < ((b + pad) & ~pad):
                        if op["grp"] is None or ops[m]["grp"] != op["grp"]:
                            dep.add(m)
        for isw, accs in ((False, op["rd"]), (True, op["wr"])):
            for name, a, b, pm in accs:
                old = seen.get(name, [])
                if SCRATCH[name][0] == "psum":
                    old = []
                elif isw:
                    old = [x for x in old if not (a <= x[2] and x[3] <= b and (x[4] & ~pm) == 0 and x[0] in dep)]
                seen[name] = old + [(n, isw, a, b, pm)]
        dep.discard(n)
        op["dep"] = dep
    members = {}
    for n, op in enumerate(ops):
        if op["grp"] is not None:
            members.setdefault(op["grp"], []).append(n)
    for op in ops:
        for m in list(op["dep"]):
            if ops[m]["grp"] is not None:
                op["dep"].update(members[ops[m]["grp"]])
        op["soft"] = set(members[op["behind"]] if "behind" in op else []) - op["dep"]
        op["pre"] = set(op["dep"]) | set(members[op["after"]] if "after" in op else []) | op["soft"]
    if "seq" not in PLAN:
        plan(ops)
    seq = PLAN["seq"]
    for n, op in enumerate(ops):
        if "alt" in op:
            op["q"] = PLAN["on"][n]
            op["fn"] = op["alt"][op["q"]]
    place = {n: k for k, n in enumerate(seq)}
    need = set()
    done = {}
    for n in seq:
        op = ops[n]
        best = {}
        for m in op["dep"]:
            if ops[m]["grp"] is None and ops[m]["q"] == op["q"] and op["grp"] is None and op["q"] == "t":
                continue
            key = ops[m]["grp"] or ops[m]["q"]
            if key not in best or place[m] > place[best[key]]:
                best[key] = m
        keep = []
        for key, m in sorted(best.items()):
            if done.get((op["q"], key), -1) < place[m]:
                done[(op["q"], key)] = place[m] if ops[m]["grp"] is None else len(ops)
                keep.append((key, m))
                need.add(m)
        op["wait"] = keep
    total = {}
    for n in seq:
        op = ops[n]
        if op["grp"] is None:
            if n in need:
                total["q" + op["q"]] = total.get("q" + op["q"], 0) + 1
                op["val"] = total["q" + op["q"]]
        else:
            total[op["grp"]] = total.get(op["grp"], 0) + (16 if op["grp"][0] == "d" else lanes(op))
    return seq, need, total


HOP, LAT_D, LAT_R, ISSUE, DMA, LINK = 0.15, 2.0, 2.5, 0.3, 200e3, 60e3
SEED, ROUNDS, HEAT, EVEN, FREE, SLOW, QUICK = 1, 10000, 0.04, 0.001, 1, 0.8, 0.67
SEND, THETA, LEAN, END, AHEAD = 10.0, 0.2, 0.5, 135.0, 1.0


def plan(ops):
    N = len(ops)
    kind = [(op["grp"] or " ")[0] for op in ops]
    edge = [[(m, 0.0 if ops[m]["q"] == op["q"] == "t" else HOP) for m in sorted(op["pre"] - op["soft"])]
            + [(m, None) for m in sorted(op["soft"])] for op in ops]
    back = [[] for _ in ops]
    for n in range(N):
        for m, d in edge[n]:
            back[m].append((n, d))
    whole = []
    for n, op in enumerate(ops):
        if kind[n] == "d":
            whole.append({"d": (LAT_D, op["c"], 0.0)})
        elif kind[n] == "l":
            whole.append({"p": (0.0, ISSUE, LAT_R + op["c"])})
        else:
            whole.append({q: (0.0, c, 0.0) for q, c in sorted(op.get("cq", {op["q"]: op["c"]}).items())})
    marks = [n for n, op in enumerate(ops) if op["grp"] in ("ar5", "ar9")]

    def walk(shape):
        tail = [0.0] * N
        for n in range(N - 1, -1, -1):
            t = max([tail[k] for k, d in back[n]] + [0.0]) + sum(min(whole[n].values())) + HOP
            if ops[n].get("due") is not None:
                t = END - ops[n]["due"]
            tail[n] = t + (SEND if kind[n] == "l" else 0.0)
        left = [len(e) for e in edge]
        pool = {q: {} for q in "vatpd"}
        start, end, on, at = [0.0] * N, [0.0] * N, [""] * N, {q: 0.0 for q in "vatpd"}

        def enter(n):
            t = max([end[m] + d if d is not None else start[m] + 0.01 for m, d in edge[n]] + [0.0])
            if "x" in shape[n]:
                start[n], end[n], on[n] = t, t, "x"
                leave(n)
                return
            for q, sh in shape[n].items():
                pool[q][n] = t + sh[0]

        def leave(n):
            for k, d in back[n]:
                left[k] -= 1
                if not left[k]:
                    enter(k)
        for n in range(N):
            if not edge[n]:
                enter(n)
        while any(pool.values()):
            t, q = min([(max(at[q], min(p.values())), q) for q, p in pool.items() if p])
            p = pool[q]
            rank = {m: (tail[m] - (LEAN if q == "v" and len(shape[m]) > 1 else 0.0), -m) for m, r in p.items() if r <= t + AHEAD}
            n = max(rank, key=rank.get)
            f = max([m for m in rank if p[m] <= t], key=rank.get)
            if p[n] > t and t + shape[f][q][1] + tail[n] <= (max(p[n] + tail[n], p[n] + shape[n][q][1] + tail[f])
                                                           + (1.0 if "lax" in ops[n] else THETA)):
                n = f
            x, c, y = shape[n][q]
            t = max(t, p[n])
            start[n], end[n], on[n], at[q] = t - x, t + c + y, q, t + c
            for r in shape[n]:
                del pool[r][n]
            leave(n)
        return start, on

    rnd = [SEED]

    def draw(k):
        rnd[0] = (rnd[0] * 1103515245 + 12345) % 2147483648
        return (rnd[0] >> 8) % k

    start, on = walk([{op["first"]: w[op["first"]]} if "first" in op else w for op, w in zip(ops, whole)])
    seq = sorted(range(N), key=lambda n: (start[n], n))
    on = [ops[n]["q"] if kind[n] in "dl" else on[n] for n in range(N)]
    hard = [[(m, d) for m, d in e if d is not None] for e in edge]
    cost = [0.0 if kind[n] in "dl" else whole[n][on[n]][1] for n in range(N)]

    quick = [QUICK if op.get("long") else 1.0 for op in ops]
    reach = [N] * N

    def run(seq, k0, k1, end, slow):
        free = {}
        for n in seq[k0 - 1::-1] if k0 else ():
            if on[n] not in free:
                free[on[n]] = end[n + N]
            if kind[n] in "dl" and kind[n] not in free:
                free[kind[n]] = end[n]
            if len(free) == 8:
                break
        old, end = end, list(end)
        moved, k2 = set("vap"), k1
        for j in range(k0, N):
            n = seq[j]
            q = on[n]
            t = free.get(q, 0.0)
            for m, d in hard[n]:
                if end[m] + d > t:
                    t = end[m] + d
            k = kind[n]
            if k == " ":
                t += cost[n] * (1.3 if q == "p" else quick[n]) if slow else cost[n]
                end[n] = end[n + N] = free[q] = t
                if t != old[n] or j <= k2:
                    moved.add(q)
                    if t != old[n] and reach[n] > k1:
                        k1 = reach[n]
                elif moved:
                    moved.discard(q)
                elif j > k1:
                    break
                continue
            if k == "a":
                end[n] = end[n + N] = t
                free[q] = 0.0
            elif k == "d":
                end[n + N] = free[q] = t + 0.06
                end[n] = free[k] = max(t + LAT_D + 0.5 * slow, free.get(k, 0.0)) + ops[n]["c"] * (1 + 0.4 * slow)
            else:
                t += (0.7 + 4.0 * (k not in free)) if slow else ISSUE
                end[n + N] = free[q] = t
                end[n] = free[k] = max(t + LAT_R + slow, free.get(k, 0.0)) + ops[n]["c"] * (1 + slow)
            if end[n] != old[n] and reach[n] > k1:
                k1 = reach[n]
            if k != "a":
                if end[n] != old[n] or end[n + N] != old[n + N] or j <= k2:
                    moved.update((q, k))
                else:
                    moved.difference_update((q, k))
        return end

    def worth(a, b):
        return max(a[:N]) + 0.2 * sum(a[n] for n in marks) + SLOW * max(b[:N]) + EVEN * sum(a[:N])

    now = [run(seq, 0, N, [0.0] * (2 * N), s) for s in (0, 1)]
    best = level = worth(*now)
    top = (list(seq), list(on), now[0])
    pairs = None
    for k in range(ROUNDS):
        if pairs is None:
            place, prev, last = [0] * N, [None] * N, {}
            for j, n in enumerate(seq):
                place[n], prev[n], last[on[n]], reach[n] = j, last.get(on[n]), n, 0
                for m, d in hard[n]:
                    reach[m] = j
            pairs = []
            for end in (now[0], now[0], now[1]):
                n = (marks + [end.index(max(end[:N]))])[draw(len(marks) + 1)]
                while n is not None:
                    t, m = -1.0, None
                    for x, d in hard[n]:
                        if end[x] + d > t:
                            t, m = end[x] + d, x
                    if prev[n] is not None and on[n] != "x" and end[prev[n] + N] > t + 1e-9:
                        m = prev[n]
                        pairs.append((n, m))
                    n = m
        n, m = pairs[draw(len(pairs))]
        move = draw(8)
        if draw(10) < FREE:
            n = seq[draw(N)]
            m = prev[n]
            if m is None or on[n] == "x":
                continue
        for _ in range(draw(3) * draw(3)):
            m = prev[m] if prev[m] is not None else m
        x = None
        if move < 2 and len(whole[n]) + len(whole[m]) > 2:
            x = m if len(whole[m]) > 1 and (move or len(whole[n]) == 1) else n
            was = on[x]
            on[x] = [q for q in whole[x] if q != was][draw(len(whole[x]) - 1)]
            cost[x] = whole[x][on[x]][1]
            new, k0, k1 = seq, place[x], place[x]
        elif move % 2:
            k0 = place[m]
            k1 = min(N - 1, place[n] + draw(2) * draw(40))
            late = {m}
            for y in seq[k0 + 1:k1 + 1]:
                if any(z in late for z, d in edge[y]):
                    late.add(y)
            if n in late:
                continue
            part = seq[k0:k1 + 1]
            new = seq[:k0] + [y for y in part if y not in late] + [y for y in part if y in late] + seq[k1 + 1:]
        else:
            k0, k1 = place[m], place[n]
            soon = {n}
            for y in seq[k1 - 1:k0 - 1 if k0 else None:-1]:
                if any(z in soon for z, d in back[y]):
                    soon.add(y)
            if m in soon:
                continue
            part = seq[k0:k1 + 1]
            new = seq[:k0] + [y for y in part if y in soon] + [y for y in part if y not in soon] + seq[k1 + 1:]
        a = run(new, k0, k1, now[0], 0)
        bar = level + HEAT * (1.0 - k / ROUNDS) * draw(100) / 100
        b = run(new, k0, k1, now[1], 1) if worth(a, now[1]) <= bar + 0.5 else None
        if b is not None and worth(a, b) <= bar:
            seq, now, level, pairs = new, [a, b], worth(a, b), None
            if level < best:
                best, top = level, (list(seq), list(on), a)
        elif x is not None:
            on[x] = was
            cost[x] = whole[x][on[x]][1]
    seq, on, end = top
    PLAN["seq"], PLAN["on"], PLAN["span"], PLAN["marks"] = seq, on, max(end[:N]), [end[n] for n in marks]
    PLAN["dbg"] = (ops, [end[n] - whole[n].get(on[n], (0, ops[n]["c"]))[1] for n in range(N)], end[:N], edge, on)


def rank_program(g, core, T, topo):
    rank = T.rank_of(core)
    if rank is None:
        return

    def peer(r):
        return T.cores[r % len(T.cores)]

    def mask(r, steps):
        m = -1
        for s in steps:
            m &= topo.mask(peer(r), peer(r + s))
        return m

    def lanes(op):
        senders = [rank] if op["q"] == "p" else [rank - s for s in op["steps"]]
        return sum(bin(mask(r, op["steps"])).count("1") for r in senders)
    ops = build(T)
    seq, need, total = order(ops, lanes)
    queue = {"v": g.vector, "a": g.scalar, "t": g.tensor, "p": g, "s": g.sync}
    for n in seq:
        op = ops[n]
        if op["q"] == "x":
            continue
        for key, m in op["wait"]:
            if ops[m]["grp"] is None:
                queue[op["q"]].wait_ge(T.sem["q" + key], ops[m]["val"])
            else:
                queue[op["q"]].wait_ge(T.sem[key], total[key])
        if "send" in op:
            k, src, lands = op["send"]
            to = [topo.addr(peer(rank + s)) for s in op["steps"]]
            if len(to) == 1:
                g.remote_dma(lands[0], src, T.sem["ar%d" % k], T.sem["lo%d" % k], to[0][1], to[0][0], mask(rank, op["steps"]))
            else:
                g.remote_dma_fused([RemoteDMATransfer(dst_ids=[DstId(rid=a[0], pnc=a[1]) for a in to],
                                                      dma_engine_mask=mask(rank, op["steps"]), remote_sem=T.sem["ar%d" % k],
                                                      srcs=[src], dsts=lands)], local_sem=T.sem["lo%d" % k])
        elif op["grp"] is not None:
            op["fn"](g).then_inc(T.sem[op["grp"]], 16)
        elif n in need:
            op["fn"](g).then_inc(T.sem["q" + op["q"]], 1)
        else:
            op["fn"](g)
    for key in sorted(total):
        g.wait_ge(T.sem[key], total[key])
